import numpy as np, ml_dtypes
CORES = [13,21,141,149]
N = 4
BF = ml_dtypes.bfloat16
def gentries(a):
    return np.ascontiguousarray(a.reshape(8, 16, -1).transpose(0, 2, 1)).reshape(8, -1)
def gtable(e):
    e = np.asarray(e); return np.ascontiguousarray(e.reshape(8, -1, 16).transpose(0, 2, 1)).reshape(128, -1).astype(np.int32)
W, K, L, T = 2048, 768, 2, 2
TOP, NEG, EMPTY = 255, 9, 16
def parts(rng):
    j = rng.integers(0, W, (N, 8, 16, W), dtype=np.int32)
    x = rng.integers(0, 16, (N, 8, N, L, K)); x = np.where(rng.random(x.shape) < 0.125, EMPTY, x)
    return j, x, rng.integers(0, 16, (N, 8, K)), rng.integers(0, W, (N, 8, T, K))
def coef(rng, drift):
    c = drift + 50.0 * rng.standard_normal((N, 8, 1, W), dtype=np.float32) + 40.0 * rng.standard_normal((N, 8, 16, W), dtype=np.float32)
    return np.minimum(np.maximum(np.rint(c), -128), 127)
def pack(j, c, x, y, a):
    return {"jm": np.ascontiguousarray(j.reshape(N, 128, W)).astype(np.int32), "cf": (np.ascontiguousarray(c.reshape(N, 128, W)).astype(np.float32) + 0.0).astype(BF),
            "lt": np.ascontiguousarray(x.reshape(N, 8, N * L * K)).astype(np.float32).astype(BF), "y0": np.ascontiguousarray(y).astype(np.float32).astype(BF),
            "st": np.stack([gtable(q.reshape(8, T * K)) for q in a])}
def setup_inputs(rng):
    j, x, y, a = parts(rng)
    return pack(j, coef(rng, rng.choice(np.array([5.0, 15.0, 30.0, 45.0]), (N, 8, 1, 1))), x, y, a)
def setup_inputs_ties(rng):
    j, x, y, a = parts(rng); n = rng.choice(np.array([4, 6, 7, 8, 9]), (N, 8, 1, W))
    o = np.argsort(rng.random((N, 8, 16, W)), axis=2); c = np.where(o < n, -1, (rng.random(o.shape) < 0.8).astype(np.int64))
    p = rng.permutation(16)[:, None]
    c[:, 0] = np.where(p < 8, -1, 1); c[:, 1] = np.where(p < 9, -1, 1); c[:, 2] = np.where(p < 8, -1, 0)
    return pack(j, c, x, y, a)
def setup_inputs_clip(rng):
    j, x, y, a = parts(rng); s = np.where(rng.random((N, 8, 1, W)) < 0.75, 1, -1)
    c = s * rng.integers(100, 128, (N, 8, 16, W)); c = np.where(rng.random(c.shape) < 0.1, -c, c)
    c[:, 1::2, :5] = -np.abs(c[:, 1::2, :5]) - 1
    r = int(rng.integers(0, N)); x[:, 6, r] = rng.integers(0, 16, (N, L, K)); e = 127 // L
    for d in range(N):
        q = (r + d) % N; c[q, 6] = 1; c[q, 6, 1:8] = -1
        c[q, 6, 8] = -1 if d == 3 else 0
        c[q, 6, 0] = (-128, e, e, 255 - 2 * L * e)[d] if d < 4 else 0
    return pack(j, c, x, y, a)
def setup_inputs_gaps(rng):
    j, x, y, a = parts(rng); x = np.where(rng.random(x.shape) < 0.5, EMPTY, x)
    x[:, 0] = EMPTY; x[:, 1:4] = rng.integers(0, 16, (N, 3, N, L, K))
    for q in range(N):
        for s in range(N):
            if q != s: x[q, 2, s] = EMPTY
            if q != (s - 1) % N: x[q, 3, s] = EMPTY
    c = coef(rng, 20.0); r = int(rng.integers(0, N))
    c[r, 0] = -rng.integers(1, 129, (16, W)); c[r, 1] = -128; c[r, 1, 8:] += (rng.random(W) < 0.5).astype(np.float32)
    x[r, 1, r, 1:] = EMPTY
    return pack(j, c, x, y, a)
def setup_inputs_alike(rng):
    j, x, y, a = parts(rng)
    j[:, ::2] = rng.choice(np.array([0, W - 1, W // 2, 5], np.int32), (N, 4, 16, W)); j[:, 1] = np.arange(W)
    j[:, 6] = rng.integers(0, W, (N, 1, 1))
    x[:, 3] = rng.integers(0, 16, (N, 1, 1, 1)); y[:, 3] = rng.integers(0, 16, (N, 1))
    a[:, 2] = rng.integers(0, W, (N, 1, 1)); a[:, 5] = rng.choice(np.array([0, W - 1]), (N, T, K))
    c = coef(rng, 25.0); r = int(rng.integers(0, N)); c[r] = np.minimum(np.abs(c[r]), 127)
    return pack(j, c, x, y, a)
def setup_inputs_spread(rng):
    j, x, y, a = parts(rng)
    j = np.minimum((W * rng.random(j.shape) ** 3).astype(np.int64), W - 1); a = np.minimum((W * rng.random(a.shape) ** 3).astype(np.int64), W - 1)
    c = np.exp2(8.0 * rng.random((N, 8, 1, W))) * (0.5 * rng.standard_normal((N, 8, 16, W)) + 0.25)
    x = np.minimum((17 * rng.random(x.shape) ** 2).astype(np.int64), EMPTY); y = np.minimum((16 * rng.random(y.shape) ** 2).astype(np.int64), 15)
    return pack(j, np.minimum(np.maximum(np.rint(c), -128), 127), x, y, a)
def check_inputs(d):
    bad = []
    for k, lo, hi in (("jm", 0, W - 1), ("cf", -128, 127), ("lt", 0, 16), ("y0", 0, 15), ("st", 0, W - 1)):
        a = np.asarray(d[k]).astype(np.float32)
        if not (np.all(a == np.floor(a)) and np.min(a) >= lo and np.max(a) <= hi): bad.append("range of " + k)
        if np.any(np.signbit(a) & (a == 0)): bad.append("-0.0 in " + k)
    return bad
def reference(jm, cf, lt, y0, st):
    J = jm.astype(np.int64).reshape(N, 8, 16, W); C = cf.astype(np.float32).astype(np.int64).reshape(N, 8, 16, W)
    x = lt.astype(np.float32).astype(np.int64).reshape(N, 8, N, L, K); y = y0.astype(np.float32).astype(np.int64)
    start = np.stack([gentries(a) for a in st]).astype(np.int64).reshape(N, 8, T, K)
    new = np.full((N, 8, T, K), EMPTY, np.int64); v = np.zeros((N, 8, 16, K), np.int64); g = np.arange(8)[:, None]
    for t in range(T):
        for s in range(N):
            b = J[s][g, y[s], start[s, :, t]]; u = np.take_along_axis(C[s], b[:, None, :], 2)
            live = np.ones((8, K), bool)
            for d in range(N):
                q = (s + d) % N
                slots = [new[s, :, i] for i in range(t - 1, -1, -1)] if d == 0 else []
                for z in slots + [x[q, :, s, l] for l in range(L)]:
                    go = live & (z < EMPTY)
                    b = np.where(go, J[q][g, np.minimum(z, 15), b], b)
                    w = np.minimum(np.maximum(u + np.take_along_axis(C[q], b[:, None, :], 2), -TOP), TOP)
                    u = np.where(go[:, None, :], w, u)
                    hit = go & (np.add.reduce((u < 0).astype(np.int64), axis=1) >= NEG)
                    z[hit] = EMPTY; live = live & ~hit
            new[s, :, t] = np.where(live, y[s], EMPTY)
            y[s] = np.argmax(u, axis=1)
            v[s] = u
    return {"yl": x.reshape(N, 8, N * L * K).astype(np.float32).astype(BF), "yi": new.reshape(N, 8, T * K).astype(np.float32).astype(BF), "yv": v.reshape(N, 128, K).astype(np.float32).astype(BF)}

@@ -1,0 +1,631 @@
+from concourse.bass import DstId, RemoteDMATransfer
+from concourse.mybir import AluOpType as A, ActivationFunctionType as F
+
+OUTW = 4 * 3840 + 2304
+SCRATCH = {"LTD": ("dram", [8, 128, 48], "bfloat16")}
+for _ty, _s in (
+        ("bfloat16", "C0 2064 C1 2064 C2 2064 C3 2064 OHY 768 SG0 1536 SG1 1536 D0A 3840 D0B 3840 D1 3840 D0S 2304 D1S 2304 "
+         "VF 768 VN 768 LTA 384 LF 384 LT1 384 LZ 384 LI1 96 LI2 96 LI3 96 Y0W 64 YI0 64 YI1 64 KC 48 YT 128 ET 32 IDB 128 ID16 128 "
+         "SBB 144 SBX 144 EBA 768 EBB 768 EBC 768 IR 384 ONE 128 PAT 384 OUT %d " % OUTW + " ".join("OH%d 768" % k for k in range(9))),
+        ("int32", "J0 2056 J1 2056 J2 2056 J3 2056 STI 96 KI 48 KB 48 PI 8 PJ 8"),
+        ("float16", "MJ0 768 MJ1 768 STF 768 BE0 48 BE1 48 Z0 432 Z02 432 Z1 432 Z12 432 ZD 432 IDF 128 SBF 144"),
+        ("uint16", "STU 96 OFS 96 OFJ 48 OC0 48 OC1 48 LU 384 Y0U 48 SEL 48"),
+        ("float32", "KM 768 IOT 2048 TC0 48 TC1 48 Y1W 48 ZZ0 432 ZZ1 432 M0 48 M1 48 EE 48 EF 48 LD 432 DL 48 DM 48 T1 48 T2 48 PC 8 P15 8 "
+         "V8 8 V8A 8 V8B 8 XR 32 JR 48 JW 48 B5 48 DD 48 IV 128"),
+        ("psum", "XA 512 XB 512 KA 512 KBK 512 KEY 1024 YB 1024")):
+    _p = _s.split()
+    for _n, _w in zip(_p[::2], _p[1::2]):
+        SCRATCH[_n] = ("psum", [128, int(_w)], "float32") if _ty == "psum" else ("sbuf", [128, int(_w)], _ty)
+
+SEMAPHORES = "qv qs qp qg dJA dJB dC dSt dLo dLr dO lo rJ rC rL rF".split()
+SEMAPHORES += ["%s%d" % (a, d) for a in ("aJ", "aC", "aL", "aF") for d in (1, 2, 3)]
+
+WORLD = 256
+BIG = 40000.0
+QK = [BIG - (3840 * (k // 2) + 2 + 2 * (k % 2)) for k in range(8)] + [1.0]
+
+
+def routes(topo, cores, r):
+    c, n = cores[r], len(cores)
+    x1, x3 = cores[(r - 1) % n], cores[(r - 3) % n]
+    own = [e for e in topo.cores_of(c) if e != c and topo.may_write(e, x1)]
+    same = [e for e in own if topo.die(e) == topo.die(c)]
+    oth = [e for e in own if topo.die(e) != topo.die(c)]
+    relays = [same[0], oth[0], same[1], oth[1]]
+    far = [e for e in range(WORLD) if topo.mates(e, x3) and topo.may_write(e, x3)]
+    pick = []
+    for e in relays:
+        pick.append([y for y in far if topo.die(y) == topo.die(e) and y not in pick][0])
+    return relays, pick
+
+
+def hand_on(g, core, T, topo):
+    cores, n = T.cores, len(T.cores)
+    lo = [0]
+
+    def send(dst, out, in_, sem):
+        rid, pid = topo.addr(dst, core)
+        g.remote_dma(out, in_, T.sem[sem], T.sem.lo, pid, rid, topo.mask(core, dst))
+        lo[0] += len(topo.engines(core, dst))
+
+    for r in range(n):
+        relays, far = routes(topo, cores, r)
+        if core in relays:
+            i = relays.index(core)
+            x = [cores[(r - d) % n] for d in range(n)]
+            cs = slice(512 * i, 512 * i + 512)
+            g.wait_ge(T.sem.rJ, 8)
+            send(x[1], T.J1[:, cs], T.J0[:, cs], "aJ1")
+            if i in (0, 2):
+                d = 1 if i == 0 else 3
+                g.wait_ge(T.sem.rL, 4)
+                send(x[d], T.LTA[:, 96 * d:96 * d + 96], T.LI1[:], "aL%d" % d)
+            g.wait_ge(T.sem.rC, 4)
+            send(x[1], T.C1[:, cs], T.C0[:, cs], "aC1")
+            send(x[2], T.J2[:, cs], T.J0[:, cs], "aJ2")
+            send(far[i], T.J0[:, cs], T.J0[:, cs], "rJ")
+            send(x[2], T.C2[:, cs], T.C0[:, cs], "aC2")
+            send(far[i], T.C0[:, cs], T.C0[:, cs], "rC")
+            if i in (0, 2):
+                d = 3 if i == 0 else 1
+                g.wait_ge(T.sem.rF, 8)
+                send(cores[(r + d) % n], T["LI%d" % d][:], T.LI2[:], "aF%d" % d)
+        if core in far:
+            i = far.index(core)
+            x3 = cores[(r - 3) % n]
+            cs = slice(512 * i, 512 * i + 512)
+            k = len(topo.engines(relays[i], core))
+            g.wait_ge(T.sem.rJ, k)
+            send(x3, T.J3[:, cs], T.J0[:, cs], "aJ3")
+            g.wait_ge(T.sem.rC, k)
+            send(x3, T.C3[:, cs], T.C0[:, cs], "aC3")
+    if lo[0]:
+        g.wait_ge(T.sem.lo, lo[0])
+
+
+def rank_program(g, core, T, topo):
+    rank = T.rank_of(core)
+    if rank is None:
+        hand_on(g, core, T, topo)
+        return
+    cores, n = T.cores, len(T.cores)
+    relays, far = routes(topo, cores, rank)
+    Q = {"v": g.vector, "s": g.scalar, "p": g.tensor, "g": g, "y": g.sync}
+    SEM = {"v": "qv", "s": "qs", "p": "qp", "g": "qg"}
+    cnt = {q: 0 for q in SEM}
+    clock = {q: {} for q in Q}
+    lastw, readers = {}, {}
+
+    def need(q, toks):
+        best = {}
+        for t in toks:
+            if t and clock[q].get(t[0], 0) < t[1] and (t[0] not in best or best[t[0]][1] < t[1]):
+                best[t[0]] = t
+        for t in sorted(best.values(), key=lambda t: -len(t[2])):
+            if clock[q].get(t[0], 0) >= t[1]:
+                continue
+            Q[q].wait_ge(T.sem[t[0]], t[1])
+            for s, v in t[2].items():
+                if clock[q].get(s, 0) < v:
+                    clock[q][s] = v
+
+    def deps(q, reads, writes):
+        out = [lastw.get(r) for r in reads]
+        for w in writes:
+            t = lastw.get(w)
+            if t and not (q == "p" and t[0] == "qp"):
+                out.append(t)
+            out += readers.get(w, [])
+        return out
+
+    def done(tok, reads, writes):
+        for r in reads:
+            readers.setdefault(r, []).append(tok)
+        for w in writes:
+            lastw[w] = tok
+            readers[w] = []
+
+    def op(q, call, reads, writes):
+        need(q, deps(q, reads, writes))
+        cnt[q] += 1
+        call().then_inc(T.sem[SEM[q]], 1)
+        c = dict(clock[q])
+        c[SEM[q]] = cnt[q]
+        done((SEM[q], cnt[q], c), reads, writes)
+
+    def pe(items, writes):
+        allr = []
+        for i, (o, l, r, rd) in enumerate(items):
+            need("p", deps("p", rd, writes if i == 0 else []))
+            allr += rd
+            ins = g.tensor.matmul(o, l, r, i == 0, i == len(items) - 1)
+        cnt["p"] += 1
+        ins.then_inc(T.sem.qp, 1)
+        c = dict(clock["p"])
+        c["qp"] = cnt["p"]
+        done(("qp", cnt["p"], c), allr, writes)
+
+    def dma(q, out, in_, sem, total, reads, writes):
+        need(q, [t for t in deps(q, reads, writes) if t and t[0] != sem])
+        Q[q].dma_start(out, in_).then_inc(T.sem[sem], 16)
+        c = dict(clock[q])
+        c[sem] = total
+        done((sem, total, c), reads, writes)
+
+    def ts(out, in0, a, b, o0, o1, reads, writes):
+        if o1 is None:
+            op("v", lambda: g.vector.tensor_scalar(out, in0, a, None, o0), reads, writes)
+        else:
+            op("v", lambda: g.vector.tensor_scalar(out, in0, a, b, o0, o1), reads, writes)
+
+    def tt(out, a, b, o, reads, writes):
+        op("v", lambda: g.vector.tensor_tensor(out, a, b, o), reads, writes)
+
+    def cp(out, a, reads, writes):
+        op("v", lambda: g.vector.tensor_copy(out, a), reads, writes)
+
+    def fill(ap, val, writes):
+        op("v", lambda: g.vector.memset(ap, val), [], writes)
+
+    def act(out, in_, func, reads, writes, bias=0.0, scale=1.0):
+        op("s", lambda: g.scalar.activation(out, in_, func, bias=bias, scale=scale), reads, writes)
+
+    def iota(out, pattern, base, ch, writes):
+        op("g", lambda: g.iota(out, pattern, base, ch, allow_small_or_imprecise_dtypes=True), [], writes)
+
+    def blk(name, k, m=1):
+        return T[name][:, 48 * k:48 * (k + m)]
+
+    def ks(name, r):
+        return ["%s%d" % (name, k) for k in r]
+
+    dma("y", T.STI[:], T.st[:], "dSt", 16, [], ["STI"])
+    dma("s", T.J0[:, 0:1024], T.jm[:, 0:1024], "dJA", 16, [], ["J0a"])
+    dma("y", T.Y0W[:, 0:48], T.y0[:], "dLo", 48, [], ["Y0W"])
+    for d in range(1, n):
+        s = (rank - d) % n
+        for l in range(2):
+            a = (s * 2 + l) * 768
+            dma("s", T.LTD[2 * s + l], T.lt[:, a:a + 768], "dLr", 96, [], ["LTS"])
+    for l in range(2):
+        a = (rank * 2 + l) * 768
+        dma("y", T.LTA[:, 48 * l:48 * l + 48], T.lt[:, a:a + 768], "dLo", 48, [], ["LTA0"])
+    dma("y", T.J0[:, 1024:2048], T.jm[:, 1024:2048], "dJB", 16, [], ["J0b"])
+    dma("s", T.C0[:, 0:2048], T.cf[:], "dC", 16, [], ["C0"])
+    for d in range(1, n):
+        for a, w, k in (("aJ", "J", 32), ("aC", "C", 32), ("aL", "LTA", 8 if d != 2 else 2)):
+            nm = "%s%d" % (a, d)
+            lastw["%s%d" % (w, d)] = (nm, k, {nm: k})
+
+    iota(T.PI[:, 0:1], [[0, 1]], 0, 1, ["PI"])
+    iota(T.V8[:], [[-16, 8]], 0, 1, ["V8"])
+    iota(T.IOT[:, 0:512], [[1, 512]], 0, 0, ["IOT0"])
+    iota(T.XR[:], [[1, 32]], 0, 0, ["XR"])
+    iota(T.JR[:], [[16, 48]], 0, 0, ["JR"])
+    iota(T.IV[:], [[-1, 128]], 0, 1, ["IV"])
+
+    for d in range(4):
+        fill(T["J%d" % d][:, 2048:2056], 0, ["Jz%d" % d])
+        fill(T["C%d" % d][:, 2048:2064], 0.0, ["Cz%d" % d])
+    fill(T.SBB[:], 0.0, ["SBB"])
+    fill(T.ONE[:], 1.0, ["ONE"])
+    ts(T.PJ[:, 0:1], T.PI[:, 0:1], 15, None, A.bitwise_and, None, ["PI"], ["PJ"])
+    ts(T.V8A[:], T.V8[:], -0.5, None, A.is_gt, None, ["V8"], ["V8A"])
+    ts(T.V8B[:], T.V8[:], 15.5, None, A.is_lt, None, ["V8"], ["V8B"])
+    cp(T.PC[:, 0:1], T.PJ[:, 0:1], ["PJ"], ["PC"])
+    tt(T.SBB[:, 15:143:16], T.V8A[:], T.V8B[:], A.mult, ["V8A", "V8B"], ["SBB"])
+    for k in (1, 2, 3):
+        ts(T.IOT[:, 512 * k:512 * k + 512], T.IOT[:, 0:512], 512.0 * k, None, A.add, None, ["IOT0"], ["IOT%d" % k])
+    cp(T.SBF[:], T.SBB[:], ["SBB"], ["SBF"])
+    ts(T.ET[:], T.XR[:], T.PC[:, 0:1], None, A.is_equal, None, ["XR", "PC"], ["ET"])
+    ts(T.IDF[:], T.IV[:], 0.0, None, A.is_equal, None, ["IV"], ["IDF"])
+
+    def sels(o, buf, rd, sb="SBF", contiguous=False):
+        src = T[buf]
+        out = []
+        for h in range(16):
+            v = src[:, 48 * h:48 * h + 48] if contiguous else src[:, h:768:16]
+            out.append((o, T[sb][:, 15 - h:143 - h], v, [rd, sb]))
+        return out
+
+    def starts(t):
+        op("v", lambda: g.vector.tensor_copy(T.STF[:], T.IOT[:, 0:2048].indirect(blk("STU", t))), ks("IOT", range(4)) + ["STU"], ["STF"])
+        pe(sels(T.KEY[:, 512 * t:512 * t + 48], "STF", "STF", contiguous=True), ["KEY%d" % t])
+
+    def starts2(t):
+        ts(blk("OFS", t), T.KEY[:, 512 * t:512 * t + 48], 0.0625, None, A.mult, None, ["KEY%d" % t], ["OFS%d" % t])
+
+    def letters(d):
+        src, k = T.LTA[:, 96 * d:96 * d + 96], 2 * d + 1
+        L = "LTA%d" % d
+        cp(T.LU[:, 96 * d:96 * d + 96], src, [L], ["LU%d" % d])
+        ts(blk("Z0", k, 2), src, 15.5, 4096.0, A.is_gt, A.mult, [L], ks("Z0_", (k, k + 1)))
+        ts(blk("Z02", k, 2), src, 15.5, 8192.0, A.is_gt, A.mult, [L], ks("Z02_", (k, k + 1)))
+        if d == 0:
+            tt(blk("ZZ0", 1), blk("Z02", 1), blk("Z0", 2), A.subtract, ["Z02_1", "Z0_2"], ["ZZ0_1"])
+        else:
+            e = 2 * d
+            tt(blk("ZZ0", e, 2), blk("Z02", e, 2), blk("Z0", e + 1, 2), A.subtract,
+               ks("Z02_", (e, e + 1)) + ks("Z0_", (e + 1, e + 2)), ks("ZZ0_", (e, e + 1)))
+        if d == 3:
+            cp(blk("ZZ0", 8), blk("Z02", 8), ["Z02_8"], ["ZZ0_8"])
+
+    def onehot(k):
+        off = T.Y0U[:] if k == 0 else T.LU[:, 48 * (k - 1):48 * k]
+        act(T["OH%d" % k][:], T.ET[:].indirect(off), F.Copy, ["ET", "Y0U" if k == 0 else "LU%d" % ((k - 1) // 2)], ["OH%d" % k])
+
+    lo = [0]
+
+    def fused(items, reads):
+        need("g", deps("g", reads, []))
+        tr = []
+        for c, e, i, o, s in items:
+            rid, pid = topo.addr(c, core)
+            tr.append(RemoteDMATransfer(dst_ids=[DstId(rid=rid, pnc=pid)], dma_engine_mask=sum(1 << b for b in e),
+                                        remote_sem=T.sem[s], src=i, dst=o))
+            lo[0] += len(e)
+        g.remote_dma_fused(tr, local_sem=T.sem.lo)
+
+    on = topo.engines(core, relays[0])
+    direct = cores[(rank - 2) % n]
+    off = topo.engines(core, direct)
+    hi = [e for e in on if e not in off]
+
+    def tabs(nm, i):
+        return T[nm][:, 512 * i:512 * i + 512]
+
+    def piece(c, e, d, out, a, sem):
+        return [(c, e[l::2], T.LTD[2 * ((rank - d) % n) + l], T[out][:, a + 48 * l:a + 48 * l + 48], sem) for l in range(2)]
+
+    def half(a, key):
+        fused([(relays[a], on[0:8], tabs("J0", a), tabs("J0", a), "rJ"),
+               (relays[a + 1], on[8:16], tabs("J0", a + 1), tabs("J0", a + 1), "rJ")], [key])
+
+    half(0, "J0a")
+    fused(piece(direct, off[0:2], 2, "LTA", 192, "aL2") + piece(relays[0], hi[0:4], 1, "LI1", 0, "rL") +
+          piece(relays[2], hi[4:8], 3, "LI1", 0, "rL"), ["LTS"])
+    half(2, "J0b")
+    fused([(relays[i], on[4 * i:4 * i + 4], tabs("C0", i), tabs("C0", i), "rC") for i in range(4)], ["C0"])
+
+    iota(T.D0S[:], [[0, 2304]], 0, 0, ["D0S"])
+    iota(T.D0S[:, 0:2304:3], [[0, 768]], -1000, 0, ["D0S"])
+    iota(T.D1S[:], [[0, 2304]], -255, 0, ["D1S"])
+    iota(T.IR[0:1, :], [[0, 24], [-1, 16]], 15, 0, ["IR"])
+    iota(T.PAT[:], [[0, 384]], 0, 0, ["PAT"])
+    iota(T.PAT[:, 0:384:16], [[0, 24]], -16384, 0, ["PAT"])
+    iota(T.EBA[0:48, :], [[0, 768]], 1, 0, ["EBA"])
+    op("g", lambda: g.affine_select(T.EBB[0:48, :], T.EBA[0:48, :], [[1, 768]], A.is_ge, 0.0, 0, -16), ["EBA"], ["EBB"])
+    op("g", lambda: g.affine_select(T.EBC[0:48, :], T.EBB[0:48, :], [[-1, 768]], A.is_ge, 0.0, 15, 16), ["EBB"], ["EBC"])
+
+    def holes(nm, zeros):
+        fill(T[nm][:, 0:3840:5], -1000.0, [nm + "c0"])
+        for i in zeros:
+            fill(T[nm][:, i:3840:5], 0.0, [nm + "c%d" % i])
+
+    D1K = ["D1_0", "D1_1"]
+    fill(T.D1[:], -255.0, D1K)
+    cp(T.STU[:], T.STI[:], ["STI"], ["STU"])
+    starts(0)
+    holes("D0A", (1, 2, 4))
+    cp(T.Y0U[:], T.Y0W[:, 0:48], ["Y0W"], ["Y0U"])
+    onehot(0)
+    letters(0)
+    onehot(1)
+    onehot(2)
+    starts2(0)
+    ts(T.JW[:], T.JR[:], T.PC[:, 0:1], None, A.add, None, ["JR", "PC"], ["JW"])
+    ts(T.P15[:, 0:1], T.PC[:, 0:1], -1.0, 15.0, A.mult, A.add, ["PC"], ["P15"])
+    ts(T.B5[:], T.JW[:], 5.0, BIG, A.mult, A.add, ["JW"], ["B5"])
+    ts(T.DD[:], T.JW[:], 3.0, 15362.0, A.mult, A.add, ["JW"], ["DD"])
+    ts(T.IDB[:], T.IV[:], 0.0, None, A.is_equal, None, ["IV"], ["IDB"])
+    ts(T.ID16[:], T.IV[:], 0.0, 16.0, A.is_equal, A.mult, ["IV"], ["ID16"])
+    ts(T.SBX[:], T.SBB[:], T.PC[:, 0:1], None, A.mult, None, ["SBB", "PC"], ["SBX"])
+
+    XP = ["XA", "XB"]
+    KP = ["KA", "KBK"]
+
+    def jkeys(d):
+        return ["J0a", "J0b", "Jz0"] if d == 0 else ["J%d" % d, "Jz%d" % d]
+
+    def walk(t, gaps):
+        slots = list(range(1 - t, 9))
+        first = slots[0]
+        ZN, ZZN = "Z%d" % t, "ZZ%d" % t
+        MK = "M%d" % t
+        M = T[MK]
+
+        def zk(k):
+            return "%s_%d" % (ZN, k)
+
+        def step_j(k):
+            if k < first:
+                d, offs, oh, rd = 0, blk("OFS", t), (T.OH0 if t == 0 else T.OHY), ["OFS%d" % t, "OH0" if t == 0 else "OHY"]
+            else:
+                d, offs, oh, rd = (k - 1) // 2 if k else 0, T.OFJ[:], T["OH%d" % k], ["OFJ", "OH%d" % k]
+            m = "MJ%d" % (k % 2)
+            tt(T[m][:], T["J%d" % d][:, 0:2056].indirect(offs), oh[:], A.mult, rd + jkeys(d), [m])
+
+        def step_x(k):
+            X = XP[k % 2]
+            o = T[X][:, 0:48]
+            m = "MJ%d" % (k % 2)
+            items = [(o, T.IDF[:], blk(ZN, k + 1), ["IDF", zk(k + 1)])] if k < 8 else []
+            items += sels(o, m, m)
+            if k >= first:
+                b = "BE%d" % (k % 2)
+                items.append((o, T.IDF[:], T[b][:], ["IDF", b]))
+            pe(items, [X])
+
+        def step_off(k):
+            X = XP[k % 2]
+            if k < 8:
+                b = "BE%d" % ((k + 1) % 2)
+                ts(T.OFJ[:], T[X][:, 0:48], 2048.0, None, A.min, None, [X], ["OFJ"])
+                step_c1(k)
+                ts(T[b][:], T[X][:, 0:48], -4096.0, 0.0, A.add, A.max, [X], [b])
+            else:
+                step_c1(k)
+
+        def step_c1(k):
+            X, a = XP[k % 2], "TC%d" % (k % 2)
+            if k < first:
+                tt(T[a][:], T[X][:, 0:48], blk(ZN, first), A.subtract, [X, zk(first)], [a])
+            else:
+                tt(T[a][:], T[X][:, 0:48], blk(ZZN, k), A.add, [X, "%s_%d" % (ZZN, k)], [a])
+
+        def step_c(k):
+            a, o = "TC%d" % (k % 2), "OC%d" % (k % 2)
+            ts(T[o][:], T[a][:], 2048.0, None, A.min, None, [a], [o])
+            d = (k - 1) // 2 if k >= max(first, 1) else 0
+            win = T["C%d" % d][:, 0:2056].indirect(T[o][:])
+            rd = ["C%d" % d, "Cz%d" % d, o]
+            if k < first:
+                act(T.D1[:, 0:3840:5], win, F.Copy, rd, D1K, scale=-1.0)
+            elif k == 8:
+                act(T.D0S[:, 1:2304:3], win, F.Copy, rd, ["D0S"])
+            else:
+                b = "D0A" if (k // 2) % 2 == 0 else "D0B"
+                act(T[b][:, 1 + 2 * (k % 2):3840:5], win, F.Copy, rd, [b])
+
+        def scan(gr, hf):
+            if gr == 4:
+                a, w, x, y, dk = 1152 * hf, 1152, T.D0S, T.D1S, ["D0S", "D1S"]
+            else:
+                nm = ("D0A", "D0B")[gr % 2]
+                a, w, x, y = 1920 * hf, 1920, T[nm], T.D1
+                dk = [nm + e for e in ("", "c0", "c2", "c4") + (() if gr % 2 else ("c1",))] + ["D1_%d" % hf]
+            b = 3840 * gr + a
+            op("v", lambda: g.vector.tensor_tensor_scan(T.OUT[:, b:b + w], x[:, a:a + w], y[:, a:a + w], 0.0, A.subtract, A.max),
+               dk, ["OUT%d_%d" % (gr, hf)])
+
+        def carry(gr, hf, q):
+            a = 3840 * (gr - 1) + 1920 * hf
+            src = T.OUT[:, a + 4:a + 1920:5]
+            if gr == 4:
+                out, w = T.D1S[:, 1152 * hf:1152 * hf + 1152:3], ["D1S"]
+            else:
+                out, w = T.D1[:, 1920 * hf:1920 * hf + 1920:5], ["D1_%d" % hf]
+            rd = ["OUT%d_%d" % (gr - 1, hf)]
+            if q == "v":
+                cp(out, src, rd, w)
+            else:
+                act(out, src, F.Copy, rd, w)
+
+        how = {}
+
+        def sign(k, q, hf):
+            if k < first:
+                return
+            gr, a = k // 2, 768 * (k % 2) + 384 * hf
+            if k == 8:
+                src = T.OUT[:, 15362 + 1152 * hf:15360 + 1152 * hf + 1152:3]
+            else:
+                b = 3840 * gr + 1920 * hf
+                src = T.OUT[:, b + 2 + 2 * (k % 2):b + 1920:5]
+            rd, o = ["OUT%d_%d" % (gr, hf)], T["SG%d" % (gr % 2)][:, a:a + 384]
+            w = ["SG%d_%d%d" % (gr % 2, k % 2, hf)]
+            how[k] = q
+            if q == "v":
+                ts(o, src, 0.0, -1.0, A.is_gt, A.mult, rd, w)
+            else:
+                act(o, src, F.Sign, rd, w, bias=0.5, scale=-1.0)
+
+        def count(gr):
+            k0, k1 = max(2 * gr, first), min(2 * gr + 1, 8)
+            m, p, a = k1 - k0 + 1, gr % 2, 768 * (k0 % 2)
+            o = T[KP[p]][:, 0:48 * m]
+            rd = ["SG%d_%d%d" % (p, k % 2, hf) for k in range(k0, k1 + 1) for hf in (0, 1)] + ["SBB"]
+            pe([(o, T.IDF[:], blk(ZN, k0, m), ["IDF"] + [zk(k) for k in range(k0, k1 + 1)])] +
+               [(o, T.SBB[:, 15 - h:143 - h], T["SG%d" % p][:, a + h:a + 768 * m:16], rd) for h in range(16)], [KP[p]])
+
+        def judge1(gr):
+            p = KP[gr % 2]
+            k0, k1 = max(2 * gr, first), min(2 * gr + 1, 8)
+            for k in range(k0, k1 + 1):
+                out, w = (M, MK) if k == first else (T.EE, "EE") if k % 2 == 0 else (T.EF, "EF")
+                thr = -8.5 if how[k] == "v" else -1.0
+                ts(out[:], T[p][:, 48 * (k - k0):48 * (k - k0) + 48], thr, QK[k], A.is_lt, A.mult, [p], [w])
+
+        def judge2(gr):
+            for k in range(max(2 * gr, first + 1), min(2 * gr + 1, 8) + 1):
+                w = "EE" if k % 2 == 0 else "EF"
+                tt(M[:], M[:], T[w][:], A.max, [MK, w], [MK])
+
+        def leave(kk):
+            if t == 0:
+                return
+            for k in kk:
+                ts(blk("LD", k), M[:], QK[k], 16.0, A.is_equal, A.mult, [MK], ["LD%d" % k])
+            if kk[0]:
+                a, m = kk[0] - 1, len(kk)
+                tt(blk("LF", a, m), blk("LT1", a, m), blk("LD", a + 1, m), A.max, ["LT1"] + ks("LD", kk), ks("LF", kk))
+                return
+            ts(T.DM[:], T.M0[:], 0.5, 16.0, A.is_gt, A.mult, ["M0"], ["DM"])
+            tt(T.DL[:], blk("LD", 0), T.DM[:], A.max, ["LD0", "DM"], ["DL"])
+            tt(T.YI0[:, 0:48], T.Y0W[:, 0:48], T.DL[:], A.max, ["Y0W", "DL"], ["YI0"])
+
+        def goes(d):
+            rd, src = ks("LF", (2 * d + 1, 2 * d + 2)), T.LF[:, 96 * d:96 * d + 96]
+            if d == 2:
+                fused([(cores[(rank + 2) % n], off[0:2], src, T.LI2[:], "aF2")], rd)
+            else:
+                fused([(relays[0 if d == 3 else 2], hi[0:8], src, T.LI2[:], "rF")], rd)
+
+        step_j(first - 1)
+        step_x(first - 1)
+        for f in gaps.get(first - 1, []):
+            f()
+        step_off(first - 1)
+        step_c(first - 1)
+        late = []
+        for k in slots:
+            step_j(k)
+            for f in late:
+                f()
+            late = []
+            step_x(k)
+            gr, hf = (k - 2) // 2, k % 2
+            due = {5: 0, 7: 1}.get(k)
+            if due is not None:
+                judge1(due)
+            if k >= 2:
+                scan(gr, hf)
+                if gr == 3 or t == 0:
+                    carry(gr + 1, hf, "v")
+                if gr < 3 and t == 0:
+                    sign(2 * gr, "v", hf)
+                    sign(2 * gr + 1, "s", hf)
+            if due is not None:
+                judge2(due)
+            if k in (4, 6, 8):
+                count((k - 4) // 2)
+            for f in gaps.get(k, []):
+                f()
+            step_off(k)
+            step_c(k)
+            if t == 0 and k < 7:
+                late.append(lambda k=k: onehot(k + 2))
+            if k >= 2 and t == 1 and k < 8:
+                late.append(lambda gr=gr, hf=hf: (carry(gr + 1, hf, "s"), sign(2 * gr, "s", hf), sign(2 * gr + 1, "s", hf)))
+        scan(3, 1)
+        carry(4, 1, "v")
+        for hf in range(2):
+            sign(6, "v", hf)
+            sign(7, "s", hf)
+        scan(4, 0)
+        count(3)
+        judge1(2)
+        scan(4, 1)
+        judge2(2)
+        if t:
+            sign(8, "v", 0)
+            sign(8, "v", 1)
+            count(4)
+            leave((1, 2, 3, 4))
+            goes(1)
+        judge1(3)
+        judge2(3)
+        if t:
+            judge1(4)
+            judge2(4)
+            leave((5, 6, 7, 8))
+            goes(3)
+        tt(T.T1[:], T.B5[:], M[:], A.subtract, ["B5", MK], ["T1"])
+        tt(T.T2[:], T.T1[:], T.DD[:], A.min, ["T1", "DD"], ["T2"])
+        cp(T.SEL[:], T.T2[:], ["T2"], ["SEL"])
+        outs = ["OUT%d_%d" % (gr, hf) for gr in range(5) for hf in range(2)]
+        for hf in range(2):
+            ts(T.VF[:, 384 * hf:384 * hf + 384], T.OUT[:, 0:OUTW].indirect(T.SEL[:, 24 * hf:24 * hf + 24]), -1.0, None, A.mult, None,
+               ["SEL"] + outs, ["VF%d" % hf])
+            if hf == 0:
+                if t == 0:
+                    sign(8, "s", 0)
+                    sign(8, "s", 1)
+                    count(4)
+                else:
+                    goes(2)
+                    leave((0,))
+        return lambda: (judge1(4), judge2(4))
+
+    fin = walk(0, {0: [lambda: holes("D0B", (2, 4))], 1: [lambda: letters(1), lambda: starts(1)], 2: [lambda: starts2(1)],
+                   3: [lambda: letters(2)], 5: [lambda: letters(3)]})
+
+    for hf in range(2):
+        base = 512 * hf
+        pe([(T.KEY[:, base:base + 384], T.ONE[0:1, :], T.IR[0:1, :], ["ONE", "IR"])] +
+           [(T.KEY[:, base + 128 * b:base + 128 * b + 128], T.VF[:, 384 * hf + 128 * b:384 * hf + 128 * b + 128], T.ID16[:], ["VF%d" % hf, "ID16"])
+            for b in range(3)], ["KEY%d" % hf])
+    S8 = range(1, 9)
+    for hf in range(2):
+        op("v", lambda hf=hf: g.vector.tensor_tensor_scan(T.KM[:, 384 * hf:384 * hf + 384], T.PAT[:], T.KEY[:, 512 * hf:512 * hf + 384],
+                                                         0.0, A.add, A.max), ["PAT", "KEY%d" % hf], ["KM%d" % hf])
+    cp(T.KI[:], T.KM[:, 15:768:16], ["KM0", "KM1"], ["KI"])
+    ts(T.KB[:], T.KI[:], 15, None, A.bitwise_and, None, ["KI"], ["KB"])
+    cp(T.KC[:], T.KB[:], ["KB"], ["KC"])
+    pe([(T.XA[0:48, 0:128], T.KC[:], T.IDB[:], ["KC", "IDB"])], ["XA"])
+    cp(T.YT[0:48, :], T.XA[0:48, 0:128], ["XA"], ["YT"])
+    for hf in range(2):
+        for b in range(3):
+            q = 3 * hf + b
+            pe([(T.YB[:, 512 * hf + 128 * b:512 * hf + 128 * b + 128], T.EBC[0:48, 128 * q:128 * q + 128], T.YT[0:48, :], ["EBC", "YT"])],
+               ["YB%d" % hf])
+    fin()
+    for k in S8:
+        ts(blk("ZD", k), T.M0[:], QK[k], 4096.0, A.is_equal, A.mult, ["M0"], ["ZD%d" % k])
+    ts(blk("Z1", 0), T.M0[:], 0.5, 4096.0, A.is_gt, A.mult, ["M0"], ["Z1_0"])
+    Z1K = ks("Z1_", range(9))
+    for hf in range(2):
+        ts(T.OHY[:, 384 * hf:384 * hf + 384], T.YB[:, 512 * hf:512 * hf + 384], T.P15[:, 0:1], None, A.is_equal, None,
+           ["YB%d" % hf, "P15"], ["OHY"])
+
+    def marks():
+        tt(blk("Z1", 1, 8), blk("Z0", 1, 8), blk("ZD", 1, 8), A.add, ks("ZD", S8) + ks("Z0_", S8), Z1K[1:])
+        ts(T.Z12[:], T.Z1[:], 2.0, None, A.mult, None, Z1K, ["Z12"])
+
+    def marks2():
+        tt(blk("ZZ1", 0, 8), blk("Z12", 0, 8), blk("Z1", 1, 8), A.subtract, ["Z12"] + Z1K, ks("ZZ1_", range(8)))
+        cp(blk("ZZ1", 8), blk("Z12", 8), ["Z12"], ["ZZ1_8"])
+
+    def kept():
+        ts(T.LZ[:], blk("Z1", 1, 8), 1.0 / 256.0, None, A.mult, None, Z1K, ["LZ"])
+        tt(T.LT1[:], T.LTA[:], T.LZ[:], A.max, ["LZ"] + ks("LTA", range(4)), ["LT1"])
+
+    def newword():
+        pe(sels(T.YB[:, 0:48], "OHY", "OHY", "SBX"), ["YB0"])
+
+    def newword2():
+        cp(T.Y1W[:], T.YB[:, 0:48], ["YB0"], ["Y1W"])
+
+    walk(1, {-1: [marks], 0: [marks2], 1: [kept, newword], 2: [newword2]})
+
+    ts(T.DM[:], T.M1[:], 0.5, 16.0, A.is_gt, A.mult, ["M1"], ["DM"])
+    tt(T.YI1[:, 0:48], T.Y1W[:], T.DM[:], A.max, ["Y1W", "DM"], ["YI1"])
+    for h in range(16):
+        out, src = T.VN[:, 48 * h:48 * h + 48], T.VF[:, h:768:16]
+        if h % 2:
+            act(out, src, F.Copy, ["VF0", "VF1"], ["VN%d" % h])
+        else:
+            cp(out, src, ["VF0", "VF1"], ["VN%d" % h])
+    total = 16 * 11
+    dma("y", T.yi[:, 0:768], T.YI0[:, 0:48], "dO", total, ["YI0"], ["o1"])
+    for l in range(2):
+        a = (rank * 2 + l) * 768
+        dma("y", T.yl[:, a:a + 768], T.LF[:, 48 * l:48 * l + 48], "dO", total, ["LF%d" % (l + 1)], ["o2%d" % l])
+
+    def home(d):
+        s = (rank - d) % n
+        nm = "aF%d" % d
+        k = 2 if d == 2 else 8
+        lastw["LI%d" % d] = (nm, k, {nm: k})
+        for l in range(2):
+            a = (s * 2 + l) * 768
+            dma("y", T.yl[:, a:a + 768], T["LI%d" % d][:, 48 * l:48 * l + 48], "dO", total, ["LI%d" % d], ["o3%d%d" % (d, l)])
+
+    home(1)
+    dma("y", T.yi[:, 768:1536], T.YI1[:, 0:48], "dO", total, ["YI1"], ["o4"])
+    dma("y", T.yv[:], T.VN[:], "dO", total, ks("VN", range(16)), ["o5"])
+    home(2)
+    home(3)
+    g.sync.wait_ge(T.sem.dO, total)
+    for s, v in (("lo", lo[0]), ("qv", cnt["v"]), ("qs", cnt["s"]), ("qp", cnt["p"]), ("qg", cnt["g"]), ("dLr", 96)):
+        g.wait_ge(T.sem[s], v)

@@ -1,28 +1,26 @@
 from concourse.bass import DstId, RemoteDMATransfer
 from concourse.mybir import AluOpType as A, ActivationFunctionType as F
 
-OUTW = 4 * 3840 + 2304
-SCRATCH = {"LTD": ("dram", [8, 128, 48], "bfloat16")}
+SCRATCH = {"LTD": ("dram", [6, 128, 48], "bfloat16"), "RET": ("dram", [6, 128, 48], "bfloat16")}
 for _ty, _s in (
-        ("bfloat16", "C0 2064 C1 2064 C2 2064 C3 2064 OHY 768 SG0 1536 SG1 1536 D0A 3840 D0B 3840 D1 3840 D0S 2304 D1S 2304 "
-         "VF 768 VN 768 LTA 384 LF 384 LT1 384 LZ 384 LI1 96 LI2 96 LI3 96 Y0W 64 YI0 64 YI1 64 KC 48 YT 128 ET 32 IDB 128 ID16 128 "
-         "SBB 144 SBX 144 EBA 768 EBB 768 EBC 768 IR 384 ONE 128 PAT 384 OUT %d " % OUTW + " ".join("OH%d 768" % k for k in range(9))),
-        ("int32", "J0 2056 J1 2056 J2 2056 J3 2056 STI 96 KI 48 KB 48 PI 8 PJ 8"),
-        ("float16", "MJ0 768 MJ1 768 STF 768 BE0 48 BE1 48 Z0 432 Z02 432 Z1 432 Z12 432 ZD 432 IDF 128 SBF 144"),
-        ("uint16", "STU 96 OFS 96 OFJ 48 OC0 48 OC1 48 LU 384 Y0U 48 SEL 48"),
-        ("float32", "KM 768 IOT 2048 TC0 48 TC1 48 Y1W 48 ZZ0 432 ZZ1 432 M0 48 M1 48 EE 48 EF 48 LD 432 DL 48 DM 48 T1 48 T2 48 PC 8 P15 8 "
-         "V8 8 V8A 8 V8B 8 XR 32 JR 48 JW 48 B5 48 DD 48 IV 128"),
-        ("psum", "XA 512 XB 512 KA 512 KBK 512 KEY 1024 YB 1024")):
+        ("bfloat16", "C0 2064 C1 2064 C2 2064 C3 2064 OHN 768 CG0 768 CG1 768 VS 768 OUT 6912 SG0 768 SG1 768 VF 768 VN 768 "
+         "LTA 384 LF 384 Y0W 64 Y0R 768 YI0 64 YI1 64 ET 32 IDB 128 I32 128 SBB 144 GE 128 "
+         "IR 512 ONE 128 PAT 512 " + " ".join("OH%d 768" % k for k in range(9))),
+        ("int32", "JA 6144 JB 6144 STI 96 KI 128 KB 128 KY 128 PI 8 PJ 8"),
+        ("float16", "MJ0 768 MJ1 768 JZ 1552 F0 432 F1 432 ZZ0 432 ZZ1 432 H0 480 H1 480 IDF 128 NID 128 ID3 128 SBF 144 "
+         "LB 144 LY 144 JC 48 T16 48 Y1W 48"),
+        ("uint16", "STU 96 OFJ 48 OC0 48 OC1 48 LU 384 Y0U 48 SEL 48 KO 8"),
+        ("float32", "KM 1040 TC0 48 TC1 48 PC 8 PK 8 V8 8 V8A 8 V8B 8 XR 32 XS 32 JR 48 IV 128"),
+        ("psum", "X 512 AD 1024 KA 512 KBK 512 KEY 1024 MS 512")):
     _p = _s.split()
     for _n, _w in zip(_p[::2], _p[1::2]):
         SCRATCH[_n] = ("psum", [128, int(_w)], "float32") if _ty == "psum" else ("sbuf", [128, int(_w)], _ty)
 
-SEMAPHORES = "qv qs qp qg dJA dJB dC dSt dLo dLr dO lo rJ rC rL rF".split()
+SEMAPHORES = "qv qs qp qg dJA dJB dC dSt dY dW dLo dLr dO lo rJ rC rL rF".split()
 SEMAPHORES += ["%s%d" % (a, d) for a in ("aJ", "aC", "aL", "aF") for d in (1, 2, 3)]
 
 WORLD = 256
-BIG = 40000.0
-QK = [BIG - (3840 * (k // 2) + 2 + 2 * (k % 2)) for k in range(8)] + [1.0]
+JAT = {0: ("JA", 0), 1: ("JA", 4096), 2: ("JB", 0), 3: ("JB", 4096)}
 
 
 def routes(topo, cores, r):
@@ -39,6 +37,17 @@ def routes(topo, cores, r):
     return relays, pick
 
 
+def carriers(topo, cores, r):
+    relays = routes(topo, cores, r)[0]
+    rest = [e for e in topo.cores_of(cores[r]) if e != cores[r] and e not in relays]
+    return relays[0:2] + rest[0:2] + relays[2:4]
+
+
+def jpiece(T, d, i):
+    nm, a = JAT[d]
+    return T[nm][:, a + 512 * i:a + 512 * i + 512]
+
+
 def hand_on(g, core, T, topo):
     cores, n = T.cores, len(T.cores)
     lo = [0]
@@ -50,33 +59,38 @@ def hand_on(g, core, T, topo):
 
     for r in range(n):
         relays, far = routes(topo, cores, r)
+        x = [cores[(r - d) % n] for d in range(n)]
+        if core in carriers(topo, cores, r):
+            i = carriers(topo, cores, r).index(core)
+            g.wait_ge(T.sem.rL, 2)
+            send(x[i // 2 + 1], T.LTA[:, 96 + 48 * i:144 + 48 * i], T.LTD[0], "aL%d" % (i // 2 + 1))
         if core in relays:
             i = relays.index(core)
-            x = [cores[(r - d) % n] for d in range(n)]
             cs = slice(512 * i, 512 * i + 512)
             g.wait_ge(T.sem.rJ, 8)
-            send(x[1], T.J1[:, cs], T.J0[:, cs], "aJ1")
-            if i in (0, 2):
-                d = 1 if i == 0 else 3
-                g.wait_ge(T.sem.rL, 4)
-                send(x[d], T.LTA[:, 96 * d:96 * d + 96], T.LI1[:], "aL%d" % d)
+            send(x[1], jpiece(T, 1, i), jpiece(T, 0, i), "aJ1")
             g.wait_ge(T.sem.rC, 4)
             send(x[1], T.C1[:, cs], T.C0[:, cs], "aC1")
-            send(x[2], T.J2[:, cs], T.J0[:, cs], "aJ2")
-            send(far[i], T.J0[:, cs], T.J0[:, cs], "rJ")
+            send(x[2], jpiece(T, 2, i), jpiece(T, 0, i), "aJ2")
+            send(far[i], jpiece(T, 0, i), jpiece(T, 0, i), "rJ")
             send(x[2], T.C2[:, cs], T.C0[:, cs], "aC2")
             send(far[i], T.C0[:, cs], T.C0[:, cs], "rC")
             if i in (0, 2):
                 d = 3 if i == 0 else 1
-                g.wait_ge(T.sem.rF, 8)
-                send(cores[(r + d) % n], T["LI%d" % d][:], T.LI2[:], "aF%d" % d)
+                g.wait_ge(T.sem.rF, 16)
+                rid, pid = topo.addr(cores[(r + d) % n], core)
+                e = topo.engines(core, cores[(r + d) % n])
+                g.remote_dma_fused([RemoteDMATransfer(dst_ids=[DstId(rid=rid, pnc=pid)], dma_engine_mask=sum(1 << b for b in e[4 * l:4 * l + 4]),
+                                                      remote_sem=T.sem["aF%d" % d], src=T.RET[2 * d - 2 + l], dst=T.RET[2 * d - 2 + l])
+                                    for l in range(2)], local_sem=T.sem.lo)
+                lo[0] += 8
         if core in far:
             i = far.index(core)
             x3 = cores[(r - 3) % n]
             cs = slice(512 * i, 512 * i + 512)
             k = len(topo.engines(relays[i], core))
             g.wait_ge(T.sem.rJ, k)
-            send(x3, T.J3[:, cs], T.J0[:, cs], "aJ3")
+            send(x3, jpiece(T, 3, i), jpiece(T, 0, i), "aJ3")
             g.wait_ge(T.sem.rC, k)
             send(x3, T.C3[:, cs], T.C0[:, cs], "aC3")
     if lo[0]:
@@ -133,12 +147,12 @@ def rank_program(g, core, T, topo):
         c[SEM[q]] = cnt[q]
         done((SEM[q], cnt[q], c), reads, writes)
 
-    def pe(items, writes):
+    def pe(items, writes, start=True, stop=True):
         allr = []
         for i, (o, l, r, rd) in enumerate(items):
             need("p", deps("p", rd, writes if i == 0 else []))
             allr += rd
-            ins = g.tensor.matmul(o, l, r, i == 0, i == len(items) - 1)
+            ins = g.tensor.matmul(o, l, r, start and i == 0, stop and i == len(items) - 1)
         cnt["p"] += 1
         ins.then_inc(T.sem.qp, 1)
         c = dict(clock["p"])
@@ -180,78 +194,71 @@ def rank_program(g, core, T, topo):
         return ["%s%d" % (name, k) for k in r]
 
     dma("y", T.STI[:], T.st[:], "dSt", 16, [], ["STI"])
-    dma("s", T.J0[:, 0:1024], T.jm[:, 0:1024], "dJA", 16, [], ["J0a"])
-    dma("y", T.Y0W[:, 0:48], T.y0[:], "dLo", 48, [], ["Y0W"])
+    dma("s", T.Y0R[0:8, :], T.y0[:], "dY", 16, [], ["Y0R"])
     for d in range(1, n):
         s = (rank - d) % n
         for l in range(2):
             a = (s * 2 + l) * 768
-            dma("s", T.LTD[2 * s + l], T.lt[:, a:a + 768], "dLr", 96, [], ["LTS"])
+            dma("sy"[l], T.LTD[2 * d - 2 + l], T.lt[:, a:a + 768], "dLr", 96, [], ["LTS"])
     for l in range(2):
         a = (rank * 2 + l) * 768
-        dma("y", T.LTA[:, 48 * l:48 * l + 48], T.lt[:, a:a + 768], "dLo", 48, [], ["LTA0"])
-    dma("y", T.J0[:, 1024:2048], T.jm[:, 1024:2048], "dJB", 16, [], ["J0b"])
+        dma("sy"[l], blk("LTA", l), T.lt[:, a:a + 768], "dLo", 32, [], ["LTA0"])
+    dma("s", T.JA[:, 0:1024], T.jm[:, 0:1024], "dJA", 16, [], ["J0a"])
+    dma("y", T.JA[:, 1024:2048], T.jm[:, 1024:2048], "dJB", 16, [], ["J0b"])
     dma("s", T.C0[:, 0:2048], T.cf[:], "dC", 16, [], ["C0"])
+    dma("y", T.Y0W[:, 0:48], T.y0[:], "dW", 16, [], ["Y0W"])
     for d in range(1, n):
-        for a, w, k in (("aJ", "J", 32), ("aC", "C", 32), ("aL", "LTA", 8 if d != 2 else 2)):
+        for a, w, k in (("aJ", "J", 32), ("aC", "C", 32), ("aL", "LTA", 16)):
             nm = "%s%d" % (a, d)
             lastw["%s%d" % (w, d)] = (nm, k, {nm: k})
 
     iota(T.PI[:, 0:1], [[0, 1]], 0, 1, ["PI"])
     iota(T.V8[:], [[-16, 8]], 0, 1, ["V8"])
-    iota(T.IOT[:, 0:512], [[1, 512]], 0, 0, ["IOT0"])
-    iota(T.XR[:], [[1, 32]], 0, 0, ["XR"])
-    iota(T.JR[:], [[16, 48]], 0, 0, ["JR"])
     iota(T.IV[:], [[-1, 128]], 0, 1, ["IV"])
+    iota(T.XR[:], [[0, 2], [1, 16]], 0, 0, ["XR"])
+    iota(T.JA[:, 2048:2560], [[1, 512]], 0, 0, ["IDA0"])
 
-    for d in range(4):
-        fill(T["J%d" % d][:, 2048:2056], 0, ["Jz%d" % d])
-        fill(T["C%d" % d][:, 2048:2064], 0.0, ["Cz%d" % d])
     fill(T.SBB[:], 0.0, ["SBB"])
+    for d in range(4):
+        fill(T["C%d" % d][:, 2048:2064], 0.0, ["Cz%d" % d])
     fill(T.ONE[:], 1.0, ["ONE"])
     ts(T.PJ[:, 0:1], T.PI[:, 0:1], 15, None, A.bitwise_and, None, ["PI"], ["PJ"])
     ts(T.V8A[:], T.V8[:], -0.5, None, A.is_gt, None, ["V8"], ["V8A"])
     ts(T.V8B[:], T.V8[:], 15.5, None, A.is_lt, None, ["V8"], ["V8B"])
     cp(T.PC[:, 0:1], T.PJ[:, 0:1], ["PJ"], ["PC"])
     tt(T.SBB[:, 15:143:16], T.V8A[:], T.V8B[:], A.mult, ["V8A", "V8B"], ["SBB"])
-    for k in (1, 2, 3):
-        ts(T.IOT[:, 512 * k:512 * k + 512], T.IOT[:, 0:512], 512.0 * k, None, A.add, None, ["IOT0"], ["IOT%d" % k])
+    ts(T.IDB[:], T.IV[:], 0.0, None, A.is_equal, None, ["IV"], ["IDB"])
+    pe([(T.X[0:8, 0:128], T.SBB[:, 15:143:16], T.IDB[:], ["SBB", "IDB"])], ["X"])
     cp(T.SBF[:], T.SBB[:], ["SBB"], ["SBF"])
     ts(T.ET[:], T.XR[:], T.PC[:, 0:1], None, A.is_equal, None, ["XR", "PC"], ["ET"])
-    ts(T.IDF[:], T.IV[:], 0.0, None, A.is_equal, None, ["IV"], ["IDF"])
+    cp(T.IDF[:], T.IDB[:], ["IDB"], ["IDF"])
+    cp(T.GE[0:8, :], T.X[0:8, 0:128], ["X"], ["GE"])
+    ts(T.NID[:], T.IDB[:], -1.0, None, A.mult, None, ["IDB"], ["NID"])
 
     def sels(o, buf, rd, sb="SBF", contiguous=False):
         src = T[buf]
         out = []
         for h in range(16):
             v = src[:, 48 * h:48 * h + 48] if contiguous else src[:, h:768:16]
-            out.append((o, T[sb][:, 15 - h:143 - h], v, [rd, sb]))
+            out.append((o, T[sb][:, 15 - h:143 - h], v, rd + [sb]))
         return out
 
-    def starts(t):
-        op("v", lambda: g.vector.tensor_copy(T.STF[:], T.IOT[:, 0:2048].indirect(blk("STU", t))), ks("IOT", range(4)) + ["STU"], ["STF"])
-        pe(sels(T.KEY[:, 512 * t:512 * t + 48], "STF", "STF", contiguous=True), ["KEY%d" % t])
-
-    def starts2(t):
-        ts(blk("OFS", t), T.KEY[:, 512 * t:512 * t + 48], 0.0625, None, A.mult, None, ["KEY%d" % t], ["OFS%d" % t])
+    def tab(k):
+        return (k - 1) // 2 if k > 0 else 0
 
     def letters(d):
         src, k = T.LTA[:, 96 * d:96 * d + 96], 2 * d + 1
         L = "LTA%d" % d
         cp(T.LU[:, 96 * d:96 * d + 96], src, [L], ["LU%d" % d])
-        ts(blk("Z0", k, 2), src, 15.5, 4096.0, A.is_gt, A.mult, [L], ks("Z0_", (k, k + 1)))
-        ts(blk("Z02", k, 2), src, 15.5, 8192.0, A.is_gt, A.mult, [L], ks("Z02_", (k, k + 1)))
-        if d == 0:
-            tt(blk("ZZ0", 1), blk("Z02", 1), blk("Z0", 2), A.subtract, ["Z02_1", "Z0_2"], ["ZZ0_1"])
-        else:
-            e = 2 * d
-            tt(blk("ZZ0", e, 2), blk("Z02", e, 2), blk("Z0", e + 1, 2), A.subtract,
-               ks("Z02_", (e, e + 1)) + ks("Z0_", (e + 1, e + 2)), ks("ZZ0_", (e, e + 1)))
-        if d == 3:
-            cp(blk("ZZ0", 8), blk("Z02", 8), ["Z02_8"], ["ZZ0_8"])
+        ts(blk("F0", k, 2), src, 15.5, 2048.0, A.is_gt, A.mult, [L], ks("F0_", (k, k + 1)))
+
+    def diffs(d):
+        k, m = (1, 1) if d == 0 else (2 * d, 2)
+        tt(blk("ZZ0", k, m), blk("F0", k, m), blk("F0", k + 1, m), A.add if d % 2 else A.subtract,
+           ks("F0_", range(k, k + m + 1)), ks("ZZ0_", range(k, k + m)))
 
     def onehot(k):
-        off = T.Y0U[:] if k == 0 else T.LU[:, 48 * (k - 1):48 * k]
+        off = T.Y0U[:] if k == 0 else blk("LU", k - 1)
         act(T["OH%d" % k][:], T.ET[:].indirect(off), F.Copy, ["ET", "Y0U" if k == 0 else "LU%d" % ((k - 1) // 2)], ["OH%d" % k])
 
     lo = [0]
@@ -271,335 +278,329 @@ def rank_program(g, core, T, topo):
     off = topo.engines(core, direct)
     hi = [e for e in on if e not in off]
 
-    def tabs(nm, i):
-        return T[nm][:, 512 * i:512 * i + 512]
-
-    def piece(c, e, d, out, a, sem):
-        return [(c, e[l::2], T.LTD[2 * ((rank - d) % n) + l], T[out][:, a + 48 * l:a + 48 * l + 48], sem) for l in range(2)]
-
     def half(a, key):
-        fused([(relays[a], on[0:8], tabs("J0", a), tabs("J0", a), "rJ"),
-               (relays[a + 1], on[8:16], tabs("J0", a + 1), tabs("J0", a + 1), "rJ")], [key])
+        fused([(relays[a], on[0:8], jpiece(T, 0, a), jpiece(T, 0, a), "rJ"),
+               (relays[a + 1], on[8:16], jpiece(T, 0, a + 1), jpiece(T, 0, a + 1), "rJ")], [key])
 
+    fused([(e, on[2 * i:2 * i + 2], T.LTD[i], T.LTD[0], "rL") for i, e in enumerate(carriers(topo, cores, rank))], ["LTS"])
     half(0, "J0a")
-    fused(piece(direct, off[0:2], 2, "LTA", 192, "aL2") + piece(relays[0], hi[0:4], 1, "LI1", 0, "rL") +
-          piece(relays[2], hi[4:8], 3, "LI1", 0, "rL"), ["LTS"])
     half(2, "J0b")
-    fused([(relays[i], on[4 * i:4 * i + 4], tabs("C0", i), tabs("C0", i), "rC") for i in range(4)], ["C0"])
+    fused([(relays[i], on[4 * i:4 * i + 4], T.C0[:, 512 * i:512 * i + 512], T.C0[:, 512 * i:512 * i + 512], "rC") for i in range(4)], ["C0"])
 
-    iota(T.D0S[:], [[0, 2304]], 0, 0, ["D0S"])
-    iota(T.D0S[:, 0:2304:3], [[0, 768]], -1000, 0, ["D0S"])
-    iota(T.D1S[:], [[0, 2304]], -255, 0, ["D1S"])
-    iota(T.IR[0:1, :], [[0, 24], [-1, 16]], 15, 0, ["IR"])
-    iota(T.PAT[:], [[0, 384]], 0, 0, ["PAT"])
-    iota(T.PAT[:, 0:384:16], [[0, 24]], -16384, 0, ["PAT"])
-    iota(T.EBA[0:48, :], [[0, 768]], 1, 0, ["EBA"])
-    op("g", lambda: g.affine_select(T.EBB[0:48, :], T.EBA[0:48, :], [[1, 768]], A.is_ge, 0.0, 0, -16), ["EBA"], ["EBB"])
-    op("g", lambda: g.affine_select(T.EBC[0:48, :], T.EBB[0:48, :], [[-1, 768]], A.is_ge, 0.0, 15, 16), ["EBB"], ["EBC"])
+    iota(T.JR[:], [[16, 48]], 0, 0, ["JR"])
+    iota(T.IR[0:1, :], [[0, 32], [-2048, 16]], 30720, 0, ["IR"])
+    iota(T.JB[:, 2048:4096], [[1, 2048]], 0, 0, ["IDB2"])
+    iota(T.PAT[:], [[0, 512]], 0, 0, ["PAT"])
+    iota(T.PAT[:, 0:512:16], [[0, 32]], -16777215, 0, ["PAT"])
+    iota(T.KM[:, 0:1024], [[0, 1024]], 0, 0, ["KM0", "KM1"])
+    iota(T.KM[:, 1024:1040], [[0, 16]], 30720, 0, ["KMz"])
 
-    def holes(nm, zeros):
-        fill(T[nm][:, 0:3840:5], -1000.0, [nm + "c0"])
-        for i in zeros:
-            fill(T[nm][:, i:3840:5], 0.0, [nm + "c%d" % i])
-
-    D1K = ["D1_0", "D1_1"]
-    fill(T.D1[:], -255.0, D1K)
     cp(T.STU[:], T.STI[:], ["STI"], ["STU"])
-    starts(0)
-    holes("D0A", (1, 2, 4))
-    cp(T.Y0U[:], T.Y0W[:, 0:48], ["Y0W"], ["Y0U"])
-    onehot(0)
+    for hf in range(2):
+        pe([(T.AD[:, 512 * hf:512 * hf + 384], T.GE[0:8, :], T.Y0R[0:8, 384 * hf:384 * hf + 384], ["GE", "Y0R"])], ["AD%d" % hf])
+    for hf in range(2):
+        ts(T.OHN[:, 384 * hf:384 * hf + 384], T.AD[:, 512 * hf:512 * hf + 384], T.PC[:, 0:1], None, A.is_equal, None,
+           ["AD%d" % hf, "PC"], ["OHN%d" % hf])
     letters(0)
     onehot(1)
     onehot(2)
-    starts2(0)
-    ts(T.JW[:], T.JR[:], T.PC[:, 0:1], None, A.add, None, ["JR", "PC"], ["JW"])
-    ts(T.P15[:, 0:1], T.PC[:, 0:1], -1.0, 15.0, A.mult, A.add, ["PC"], ["P15"])
-    ts(T.B5[:], T.JW[:], 5.0, BIG, A.mult, A.add, ["JW"], ["B5"])
-    ts(T.DD[:], T.JW[:], 3.0, 15362.0, A.mult, A.add, ["JW"], ["DD"])
-    ts(T.IDB[:], T.IV[:], 0.0, None, A.is_equal, None, ["IV"], ["IDB"])
-    ts(T.ID16[:], T.IV[:], 0.0, 16.0, A.is_equal, A.mult, ["IV"], ["ID16"])
-    ts(T.SBX[:], T.SBB[:], T.PC[:, 0:1], None, A.mult, None, ["SBB", "PC"], ["SBX"])
+    diffs(0)
 
-    XP = ["XA", "XB"]
+    def same(k):
+        ts(T.JA[:, 2048 + 512 * k:2560 + 512 * k], T.JA[:, 2048:2560], 512.0 * k, None, A.add, None, ["IDA0"], ["IDA%d" % k])
+
+    same(1)
+    same(2)
+
+    def late_constants():
+        for t in range(2):
+            ts(T["H%d" % t][:, 0:96], T.IDB[:, 0:96], 0.0, None, A.mult, None, ["IDB"], ks("H%d_" % t, (-1, 0)))
+        ts(T.ID3[:], T.IDB[:], -0.1875, None, A.mult, None, ["IDB"], ["ID3"])
+        ts(T.I32[:], T.IDB[:], 32768.0, None, A.mult, None, ["IDB"], ["I32"])
+        cp(T.JC[:], T.JR[:], ["JR"], ["JC"])
+        ts(T.T16[:], T.JR[:], 0.0, -16.0, A.mult, A.add, ["JR"], ["T16"])
+        ts(T.PK[:, 0:1], T.PC[:, 0:1], 128.0, 15.0, A.mult, A.add, ["PC"], ["PK"])
+        ts(T.LB[:, 0:16], T.IDB[:, 0:16], 0.0, None, A.mult, None, ["IDB"], ["LB"])
+        ts(T.LY[:, 0:16], T.IDB[:, 0:16], 0.0, None, A.mult, None, ["IDB"], ["LY"])
+        ts(T.KO[:], T.JR[:, 0:8], T.PK[:, 0:1], 1024.0, A.add, A.min, ["JR", "PK"], ["KO"])
+
+    def start_images():
+        cp(T.Y0U[:], T.Y0W[:, 0:48], ["Y0W"], ["Y0U"])
+        ts(T.JZ[:, 0:1538:2], T.C0[:, 0:769], 0.0, None, A.mult, None, ["C0"], ["JZ0"])
+        cp(T.JZ[:, 1:1537:2], T.JA[:, 0:2048].indirect(blk("STU", 1)), ["STU", "J0a", "J0b"], ["JZ1"])
+
+    def start_keys():
+        for b in range(2):
+            items = [(T.KEY[0:96, 512 * b:512 * b + 512], T.ONE[0:1, 0:96], T.IR[0:1, :], ["ONE", "IR"])]
+            for hp in range(4 * b, 4 * b + 4):
+                for e in range(2):
+                    a = 96 * (hp + 8 * e) + 1 - e
+                    items.append((T.KEY[0:96, 128 * hp:128 * hp + 128], T.JZ[:, a:a + 96], T.IDF[:], ["JZ0", "JZ1", "IDF"]))
+            pe(items, ["KEY%d" % b], stop=False)
+
     KP = ["KA", "KBK"]
+    X = T.X[:, 0:48]
 
-    def jkeys(d):
-        return ["J0a", "J0b", "Jz0"] if d == 0 else ["J%d" % d, "Jz%d" % d]
+    def jwin(d):
+        nm, a = JAT[d]
+        a = a // 2
+        rd = ["J0a", "J0b"] if d == 0 else ["J%d" % d]
+        return T[nm][:, a:a + 4096], rd + (ks("IDA", range(4)) if d < 2 else ["IDB2"])
 
-    def walk(t, gaps):
-        slots = list(range(1 - t, 9))
-        first = slots[0]
-        ZN, ZZN = "Z%d" % t, "ZZ%d" % t
-        MK = "M%d" % t
-        M = T[MK]
+    def walk(t, gaps, sgaps, vsign):
+        first = 1 - t
+        FN, ZN, HN = "F%d" % t, "ZZ%d" % t, "H%d" % t
 
-        def zk(k):
-            return "%s_%d" % (ZN, k)
+        def fk(k):
+            return "%s_%d" % (FN, k)
+
+        def hk(k):
+            return "%s_%d" % (HN, k)
+
+        def vblk(k, hf):
+            if k < first:
+                return T.VS[:, 384 * hf:384 * hf + 384], "VS_%d" % hf
+            return T.OUT[:, 768 * k + 384 * hf:768 * k + 384 * hf + 384], "OUT%d_%d" % (k, hf)
 
         def step_j(k):
-            if k < first:
-                d, offs, oh, rd = 0, blk("OFS", t), (T.OH0 if t == 0 else T.OHY), ["OFS%d" % t, "OH0" if t == 0 else "OHY"]
-            else:
-                d, offs, oh, rd = (k - 1) // 2 if k else 0, T.OFJ[:], T["OH%d" % k], ["OFJ", "OH%d" % k]
             m = "MJ%d" % (k % 2)
-            tt(T[m][:], T["J%d" % d][:, 0:2056].indirect(offs), oh[:], A.mult, rd + jkeys(d), [m])
+            if k < first:
+                tt(T[m][:], T.JA[:, 0:2048].indirect(blk("STU", 0)), T.OHN[:], A.mult, ["STU", "OHN0", "OHN1", "J0a", "J0b"], [m])
+            else:
+                win, rd = jwin(tab(k))
+                tt(T[m][:], win.indirect(T.OFJ[:]), T["OH%d" % k][:], A.mult, rd + ["OFJ", "OH%d" % k], [m])
 
         def step_x(k):
-            X = XP[k % 2]
-            o = T[X][:, 0:48]
             m = "MJ%d" % (k % 2)
-            items = [(o, T.IDF[:], blk(ZN, k + 1), ["IDF", zk(k + 1)])] if k < 8 else []
-            items += sels(o, m, m)
-            if k >= first:
-                b = "BE%d" % (k % 2)
-                items.append((o, T.IDF[:], T[b][:], ["IDF", b]))
-            pe(items, [X])
-
-        def step_off(k):
-            X = XP[k % 2]
+            if k < first and t:
+                items = [(X, T.LB[0:96, 8 - 8 * e:136 - 8 * e], T.IDF[0:96, e:96:2], ["LB", "IDF"]) for e in range(2)]
+            else:
+                items = sels(X, m, [m], contiguous=k < first)
             if k < 8:
-                b = "BE%d" % ((k + 1) % 2)
-                ts(T.OFJ[:], T[X][:, 0:48], 2048.0, None, A.min, None, [X], ["OFJ"])
-                step_c1(k)
-                ts(T[b][:], T[X][:, 0:48], -4096.0, 0.0, A.add, A.max, [X], [b])
-            else:
-                step_c1(k)
+                w = "NID" if tab(k + 1) % 2 else "IDF"
+                items.append((X, T[w][:], blk(FN, k + 1), [w, fk(k + 1)]))
+            pe(items, ["X"])
 
-        def step_c1(k):
-            X, a = XP[k % 2], "TC%d" % (k % 2)
-            if k < first:
-                tt(T[a][:], T[X][:, 0:48], blk(ZN, first), A.subtract, [X, zk(first)], [a])
-            else:
-                tt(T[a][:], T[X][:, 0:48], blk(ZZN, k), A.add, [X, "%s_%d" % (ZZN, k)], [a])
-
-        def step_c(k):
+        def step_off(k, between=None):
             a, o = "TC%d" % (k % 2), "OC%d" % (k % 2)
-            ts(T[o][:], T[a][:], 2048.0, None, A.min, None, [a], [o])
-            d = (k - 1) // 2 if k >= max(first, 1) else 0
-            win = T["C%d" % d][:, 0:2056].indirect(T[o][:])
-            rd = ["C%d" % d, "Cz%d" % d, o]
+            if k < 8:
+                ts(T.OFJ[:], X, 2048.0 * (tab(k + 1) % 2), None, A.add, None, ["X"], ["OFJ"])
             if k < first:
-                act(T.D1[:, 0:3840:5], win, F.Copy, rd, D1K, scale=-1.0)
+                tt(T[a][:], X, blk(FN, first), A.subtract, ["X", fk(first)], [a])
             elif k == 8:
-                act(T.D0S[:, 1:2304:3], win, F.Copy, rd, ["D0S"])
+                tt(T[a][:], X, blk(FN, 8), A.add, ["X", fk(8)], [a])
             else:
-                b = "D0A" if (k // 2) % 2 == 0 else "D0B"
-                act(T[b][:, 1 + 2 * (k % 2):3840:5], win, F.Copy, rd, [b])
+                tt(T[a][:], X, blk(ZN, k), A.add, ["X", "%s_%d" % (ZN, k)], [a])
+            if between:
+                between()
+            ts(T[o][:], T[a][:], 2048.0, None, A.min, None, [a], [o])
 
-        def scan(gr, hf):
-            if gr == 4:
-                a, w, x, y, dk = 1152 * hf, 1152, T.D0S, T.D1S, ["D0S", "D1S"]
-            else:
-                nm = ("D0A", "D0B")[gr % 2]
-                a, w, x, y = 1920 * hf, 1920, T[nm], T.D1
-                dk = [nm + e for e in ("", "c0", "c2", "c4") + (() if gr % 2 else ("c1",))] + ["D1_%d" % hf]
-            b = 3840 * gr + a
-            op("v", lambda: g.vector.tensor_tensor_scan(T.OUT[:, b:b + w], x[:, a:a + w], y[:, a:a + w], 0.0, A.subtract, A.max),
-               dk, ["OUT%d_%d" % (gr, hf)])
+        def step_c(k, hf):
+            d, o, c = tab(k), "OC%d" % (k % 2), "VS" if k < first else "CG%d" % (k % 2)
+            act(T[c][:, 384 * hf:384 * hf + 384], T["C%d" % d][:, 0:2056].indirect(T[o][:, 24 * hf:24 * hf + 24]), F.Copy,
+                ["C%d" % d, "Cz%d" % d, o], ["%s_%d" % (c, hf)])
 
-        def carry(gr, hf, q):
-            a = 3840 * (gr - 1) + 1920 * hf
-            src = T.OUT[:, a + 4:a + 1920:5]
-            if gr == 4:
-                out, w = T.D1S[:, 1152 * hf:1152 * hf + 1152:3], ["D1S"]
-            else:
-                out, w = T.D1[:, 1920 * hf:1920 * hf + 1920:5], ["D1_%d" % hf]
-            rd = ["OUT%d_%d" % (gr - 1, hf)]
-            if q == "v":
-                cp(out, src, rd, w)
-            else:
-                act(out, src, F.Copy, rd, w)
+        def add(k, hf):
+            if k < first:
+                return
+            v, vk = vblk(k - 1, hf)
+            c = "CG%d" % (k % 2)
+            o = T.AD[:, 512 * hf:512 * hf + 384]
+            pe([(o, T.IDB[:], v, ["IDB", vk]), (o, T.IDB[:], T[c][:, 384 * hf:384 * hf + 384], ["IDB", "%s_%d" % (c, hf)])], ["AD%d" % hf])
+
+        def cut(k, hf):
+            if k < first:
+                return
+            v, vk = vblk(k, hf)
+            ts(v, T.AD[:, 512 * hf:512 * hf + 384], 255.0, -255.0, A.min, A.max, ["AD%d" % hf], [vk])
 
         how = {}
 
-        def sign(k, q, hf):
+        def sign(k, hf, q, src=None):
             if k < first:
                 return
-            gr, a = k // 2, 768 * (k % 2) + 384 * hf
-            if k == 8:
-                src = T.OUT[:, 15362 + 1152 * hf:15360 + 1152 * hf + 1152:3]
-            else:
-                b = 3840 * gr + 1920 * hf
-                src = T.OUT[:, b + 2 + 2 * (k % 2):b + 1920:5]
-            rd, o = ["OUT%d_%d" % (gr, hf)], T["SG%d" % (gr % 2)][:, a:a + 384]
-            w = ["SG%d_%d%d" % (gr % 2, k % 2, hf)]
-            how[k] = q
+            v, vk = src or vblk(k, hf)
+            s = "SG%d" % (k % 2)
+            o, w = T[s][:, 384 * hf:384 * hf + 384], ["%s_%d" % (s, hf)]
+            how[k, hf] = q
             if q == "v":
-                ts(o, src, 0.0, -1.0, A.is_gt, A.mult, rd, w)
+                ts(o, v, 0.0, 2.0, A.is_ge, A.mult, [vk], w)
             else:
-                act(o, src, F.Sign, rd, w, bias=0.5, scale=-1.0)
+                act(o, v, F.Sign, [vk], w, bias=0.5)
 
-        def count(gr):
-            k0, k1 = max(2 * gr, first), min(2 * gr + 1, 8)
-            m, p, a = k1 - k0 + 1, gr % 2, 768 * (k0 % 2)
-            o = T[KP[p]][:, 0:48 * m]
-            rd = ["SG%d_%d%d" % (p, k % 2, hf) for k in range(k0, k1 + 1) for hf in (0, 1)] + ["SBB"]
-            pe([(o, T.IDF[:], blk(ZN, k0, m), ["IDF"] + [zk(k) for k in range(k0, k1 + 1)])] +
-               [(o, T.SBB[:, 15 - h:143 - h], T["SG%d" % p][:, a + h:a + 768 * m:16], rd) for h in range(16)], [KP[p]])
-
-        def judge1(gr):
-            p = KP[gr % 2]
-            k0, k1 = max(2 * gr, first), min(2 * gr + 1, 8)
-            for k in range(k0, k1 + 1):
-                out, w = (M, MK) if k == first else (T.EE, "EE") if k % 2 == 0 else (T.EF, "EF")
-                thr = -8.5 if how[k] == "v" else -1.0
-                ts(out[:], T[p][:, 48 * (k - k0):48 * (k - k0) + 48], thr, QK[k], A.is_lt, A.mult, [p], [w])
-
-        def judge2(gr):
-            for k in range(max(2 * gr, first + 1), min(2 * gr + 1, 8) + 1):
-                w = "EE" if k % 2 == 0 else "EF"
-                tt(M[:], M[:], T[w][:], A.max, [MK, w], [MK])
-
-        def leave(kk):
-            if t == 0:
+        def count(k, dead="NID"):
+            if k < first:
                 return
-            for k in kk:
-                ts(blk("LD", k), M[:], QK[k], 16.0, A.is_equal, A.mult, [MK], ["LD%d" % k])
-            if kk[0]:
-                a, m = kk[0] - 1, len(kk)
-                tt(blk("LF", a, m), blk("LT1", a, m), blk("LD", a + 1, m), A.max, ["LT1"] + ks("LD", kk), ks("LF", kk))
+            p, s = KP[k % 2], "SG%d" % (k % 2)
+            o = T[p][:, 0:48]
+            items = sels(o, s, [s + "_0", s + "_1"], "SBB")
+            if how[k, 0] != how[k, 1]:
+                a = 24 * (how[k, 1] == "v")
+                items.append((T[p][:, a:a + 24], T.IDF[:], T.T16[:, 0:24], ["IDF", "T16"]))
+            items.append((o, T.IDF[:], blk(FN, k), ["IDF", fk(k)]))
+            if k > first:
+                items.append((o, T[dead][:], blk(HN, k), [dead, hk(k - 1)]))
+            pe(items, [p])
+
+        def judge(k):
+            if k < first:
                 return
-            ts(T.DM[:], T.M0[:], 0.5, 16.0, A.is_gt, A.mult, ["M0"], ["DM"])
-            tt(T.DL[:], blk("LD", 0), T.DM[:], A.max, ["LD0", "DM"], ["DL"])
-            tt(T.YI0[:, 0:48], T.Y0W[:, 0:48], T.DL[:], A.max, ["Y0W", "DL"], ["YI0"])
+            p = KP[k % 2]
+            thr = 15.0 if how[k, 0] == how[k, 1] == "v" else -1.0
+            ts(blk(HN, k + 1), T[p][:, 0:48], thr, 4096.0, A.is_lt, A.mult, [p], [hk(k)])
+
+        def left(d):
+            k, o = 2 * d + 1, T.KEY[:, 512 * (d % 2):512 * (d % 2) + 96]
+            pe([(o, T.IDB[:], T.LTA[:, 96 * d:96 * d + 96], ["IDB", "LTA%d" % d]),
+                (o, T.IDF[:], blk(FN, k, 2), ["IDF", fk(k), fk(k + 1)]),
+                (o, T.NID[:], blk(HN, k, 2), ["NID", hk(k - 1), hk(k)]),
+                (o, T.IDF[:], blk(HN, k + 1, 2), ["IDF", hk(k), hk(k + 1)])], ["KEY%d" % (d % 2)])
+
+        def left2(d):
+            ts(T.LF[:, 96 * d:96 * d + 96], T.KEY[:, 512 * (d % 2):512 * (d % 2) + 96], 16.0, None, A.min, None,
+               ["KEY%d" % (d % 2)], ["LF%d" % d])
 
         def goes(d):
-            rd, src = ks("LF", (2 * d + 1, 2 * d + 2)), T.LF[:, 96 * d:96 * d + 96]
             if d == 2:
-                fused([(cores[(rank + 2) % n], off[0:2], src, T.LI2[:], "aF2")], rd)
+                c, e, sem = cores[(rank + 2) % n], off, "aF2"
             else:
-                fused([(relays[0 if d == 3 else 2], hi[0:8], src, T.LI2[:], "rF")], rd)
+                c, e, sem = relays[0 if d == 3 else 2], on, "rF"
+            m = len(e) // 2
+            fused([(c, e[m * l:m * l + m], blk("LF", 2 * d + l), T.RET[2 * d - 2 + l], sem) for l in range(2)], ["LF%d" % d])
 
-        step_j(first - 1)
-        step_x(first - 1)
-        for f in gaps.get(first - 1, []):
-            f()
-        step_off(first - 1)
-        step_c(first - 1)
-        late = []
-        for k in slots:
-            step_j(k)
-            for f in late:
+        def run(fs):
+            for f in fs:
                 f()
-            late = []
+
+        for k in range(first - 1, 9):
+            if k >= first or t == 0:
+                step_j(k)
+            add(k - 1, 0)
             step_x(k)
-            gr, hf = (k - 2) // 2, k % 2
-            due = {5: 0, 7: 1}.get(k)
-            if due is not None:
-                judge1(due)
-            if k >= 2:
-                scan(gr, hf)
-                if gr == 3 or t == 0:
-                    carry(gr + 1, hf, "v")
-                if gr < 3 and t == 0:
-                    sign(2 * gr, "v", hf)
-                    sign(2 * gr + 1, "s", hf)
-            if due is not None:
-                judge2(due)
-            if k in (4, 6, 8):
-                count((k - 4) // 2)
-            for f in gaps.get(k, []):
-                f()
-            step_off(k)
-            step_c(k)
-            if t == 0 and k < 7:
-                late.append(lambda k=k: onehot(k + 2))
-            if k >= 2 and t == 1 and k < 8:
-                late.append(lambda gr=gr, hf=hf: (carry(gr + 1, hf, "s"), sign(2 * gr, "s", hf), sign(2 * gr + 1, "s", hf)))
-        scan(3, 1)
-        carry(4, 1, "v")
-        for hf in range(2):
-            sign(6, "v", hf)
-            sign(7, "s", hf)
-        scan(4, 0)
-        count(3)
-        judge1(2)
-        scan(4, 1)
-        judge2(2)
+            run(gaps.get((k, 0), []))
+            cut(k - 2, 1)
+            add(k - 1, 1)
+            cut(k - 1, 0)
+            for hf in range(2):
+                sign(k - 2, hf, "v" if (k - 2, hf) in vsign else "s")
+            run(gaps.get(k, []))
+            if t and k in (6, 8):
+                left2(k // 2 - 3)
+            step_off(k, lambda: judge(k - 3))
+            if t and k == 8:
+                goes(1)
+            run(sgaps.get(k, []))
+            step_c(k, 0)
+            if k < 8:
+                step_c(k, 1)
+            count(k - 2)
+            if t and k in (5, 7):
+                left(k // 2 - 2)
+        cut(7, 1)
+        add(8, 0)
+        sign(7, 0, "s")
+        sign(7, 1, "s")
+        judge(6)
+        S = T.MS[:, 0:48]
+        pe([(S, T.IDF[:], T.JC[:], ["IDF", "JC"])] + [(S, T.ID3[:], blk(HN, k + 1), ["ID3", hk(k)]) for k in range(first, 7)], ["MS"],
+           stop=False)
         if t:
-            sign(8, "v", 0)
-            sign(8, "v", 1)
-            count(4)
-            leave((1, 2, 3, 4))
-            goes(1)
-        judge1(3)
-        judge2(3)
+            left(2)
+        tt(T.CG0[:, 384:768], T.C3[:, 0:2056].indirect(T.OC0[:, 24:48]), vblk(7, 1)[0], A.add, ["C3", "Cz3", "OC0", "OUT7_1"], ["CG0_1"])
+        count(7)
+        cut(8, 0)
+        sign(8, 1, "s", (T.CG0[:, 384:768], "CG0_1"))
         if t:
-            judge1(4)
-            judge2(4)
-            leave((5, 6, 7, 8))
+            sign(8, 0, "v")
+            left2(2)
+            goes(2)
+        ts(vblk(8, 1)[0], T.CG0[:, 384:768], 255.0, -255.0, A.min, A.max, ["CG0_1"], ["OUT8_1"])
+        judge(7)
+        if t:
+            count(8, "IDF")
+        pe([(S, T.ID3[:], blk(HN, 8), ["ID3", hk(7)])], ["MS"], start=False)
+        if t:
+            o = T.KEY[:, 512:608]
+            pe([(o, T.IDB[:], T.LTA[:, 288:384], ["IDB", "LTA3"]), (o, T.IDF[:], blk(FN, 7, 2), ["IDF", fk(7), fk(8)]),
+                (T.KEY[:, 512:560], T.NID[:], blk(HN, 7), ["NID", hk(6)]), (T.KEY[:, 512:560], T.IDF[:], blk(HN, 8), ["IDF", hk(7)])], ["KEY1"])
+            left2(3)
+            ts(blk(HN, 9), T.KA[:, 0:48], -1.0, 16.0, A.is_lt, A.mult, ["KA"], [hk(8)])
+            tt(blk("LF", 7), blk("LF", 7), blk(HN, 9), A.max, ["LF3", hk(8)], ["LF3"])
             goes(3)
-        tt(T.T1[:], T.B5[:], M[:], A.subtract, ["B5", MK], ["T1"])
-        tt(T.T2[:], T.T1[:], T.DD[:], A.min, ["T1", "DD"], ["T2"])
-        cp(T.SEL[:], T.T2[:], ["T2"], ["SEL"])
-        outs = ["OUT%d_%d" % (gr, hf) for gr in range(5) for hf in range(2)]
-        for hf in range(2):
-            ts(T.VF[:, 384 * hf:384 * hf + 384], T.OUT[:, 0:OUTW].indirect(T.SEL[:, 24 * hf:24 * hf + 24]), -1.0, None, A.mult, None,
-               ["SEL"] + outs, ["VF%d" % hf])
-            if hf == 0:
-                if t == 0:
-                    sign(8, "s", 0)
-                    sign(8, "s", 1)
-                    count(4)
-                else:
-                    goes(2)
-                    leave((0,))
-        return lambda: (judge1(4), judge2(4))
+        ts(T.SEL[:], S, T.PC[:, 0:1], 768.0 * (8 - first), A.add, A.add, ["MS", "PC"], ["SEL"])
+        outs = ["OUT%d_%d" % (k, hf) for k in range(first, 9) for hf in range(2)]
+        win = T.OUT[:, 768 * first:6912]
+        act(T.VF[:, 384:768], win.indirect(T.SEL[:, 24:48]), F.Copy, ["SEL"] + outs, ["VF1"])
+        cp(T.VF[:, 0:384], win.indirect(T.SEL[:, 0:24]), ["SEL"] + outs, ["VF0"])
+        if t == 0:
+            sign(8, 0, "s")
+            return lambda: count(8), lambda: judge(8)
 
-    fin = walk(0, {0: [lambda: holes("D0B", (2, 4))], 1: [lambda: letters(1), lambda: starts(1)], 2: [lambda: starts2(1)],
-                   3: [lambda: letters(2)], 5: [lambda: letters(3)]})
+    def oh(k):
+        return lambda: onehot(k)
 
-    for hf in range(2):
-        base = 512 * hf
-        pe([(T.KEY[:, base:base + 384], T.ONE[0:1, :], T.IR[0:1, :], ["ONE", "IR"])] +
-           [(T.KEY[:, base + 128 * b:base + 128 * b + 128], T.VF[:, 384 * hf + 128 * b:384 * hf + 128 * b + 128], T.ID16[:], ["VF%d" % hf, "ID16"])
-            for b in range(3)], ["KEY%d" % hf])
+    def lt(d):
+        return [lambda: letters(d), lambda: diffs(d)]
+
+    cnt8, jdg8 = walk(0, {(0, 0): [lambda: same(3)], (1, 0): [late_constants], 1: lt(1), (2, 0): [start_images], 3: [start_keys] + lt(2), 5: lt(3)},
+                      {1: [oh(3)], 2: [oh(4)], 3: [oh(5)], 4: [oh(6)], 5: [oh(7)], 6: [oh(8)]},
+                      [(k, hf) for k in range(1, 5) for hf in range(2)])
+    onehot(0)
+
+    for b in range(2):
+        pe([(T.KEY[0:96, 128 * hp:128 * hp + 128], T.VF[:, hp:768:8], T.I32[:], ["VF0", "VF1", "I32"]) for hp in range(4 * b, 4 * b + 4)],
+           ["KEY%d" % b], start=False)
+    cnt8()
+    for b in range(2):
+        op("v", lambda b=b: g.vector.tensor_tensor_scan(T.KM[0:96, 512 * b:512 * b + 512], T.PAT[0:96, :], T.KEY[0:96, 512 * b:512 * b + 512],
+                                                       0.0, A.add, A.max), ["PAT", "KEY%d" % b], ["KM%d" % b])
+        if b == 0:
+            jdg8()
     S8 = range(1, 9)
-    for hf in range(2):
-        op("v", lambda hf=hf: g.vector.tensor_tensor_scan(T.KM[:, 384 * hf:384 * hf + 384], T.PAT[:], T.KEY[:, 512 * hf:512 * hf + 384],
-                                                         0.0, A.add, A.max), ["PAT", "KEY%d" % hf], ["KM%d" % hf])
-    cp(T.KI[:], T.KM[:, 15:768:16], ["KM0", "KM1"], ["KI"])
-    ts(T.KB[:], T.KI[:], 15, None, A.bitwise_and, None, ["KI"], ["KB"])
-    cp(T.KC[:], T.KB[:], ["KB"], ["KC"])
-    pe([(T.XA[0:48, 0:128], T.KC[:], T.IDB[:], ["KC", "IDB"])], ["XA"])
-    cp(T.YT[0:48, :], T.XA[0:48, 0:128], ["XA"], ["YT"])
-    for hf in range(2):
-        for b in range(3):
-            q = 3 * hf + b
-            pe([(T.YB[:, 512 * hf + 128 * b:512 * hf + 128 * b + 128], T.EBC[0:48, 128 * q:128 * q + 128], T.YT[0:48, :], ["EBC", "YT"])],
-               ["YB%d" % hf])
-    fin()
-    for k in S8:
-        ts(blk("ZD", k), T.M0[:], QK[k], 4096.0, A.is_equal, A.mult, ["M0"], ["ZD%d" % k])
-    ts(blk("Z1", 0), T.M0[:], 0.5, 4096.0, A.is_gt, A.mult, ["M0"], ["Z1_0"])
-    Z1K = ks("Z1_", range(9))
-    for hf in range(2):
-        ts(T.OHY[:, 384 * hf:384 * hf + 384], T.YB[:, 512 * hf:512 * hf + 384], T.P15[:, 0:1], None, A.is_equal, None,
-           ["YB%d" % hf, "P15"], ["OHY"])
+    o = T.MS[:, 0:384]
+    pe([(o, T.IDF[:], blk("F0", 1, 8), ["IDF"] + ks("F0_", S8)), (o, T.NID[:], blk("H0", 1, 8), ["NID"] + ks("H0_", range(8))),
+        (o, T.IDF[:], blk("H0", 2, 8), ["IDF"] + ks("H0_", S8))], ["MS"])
+    cp(T.KI[:], T.KM[:].indirect(T.KO[:]), ["KM0", "KM1", "KMz", "KO"], ["KI"])
+    ts(blk("F1", 0), blk("H0", 9), 0.5, None, A.mult, None, ["H0_8"], ["F1_0"])
+    ts(T.KB[:], T.KI[:], 2047, None, A.bitwise_and, None, ["KI"], ["KB"])
+    cp(T.LB[:, 8:136], T.KB[:], ["KB"], ["LB"])
 
     def marks():
-        tt(blk("Z1", 1, 8), blk("Z0", 1, 8), blk("ZD", 1, 8), A.add, ks("ZD", S8) + ks("Z0_", S8), Z1K[1:])
-        ts(T.Z12[:], T.Z1[:], 2.0, None, A.mult, None, Z1K, ["Z12"])
+        ts(blk("F1", 1, 8), T.MS[:, 0:384], 1000.0, 2048.0, A.is_gt, A.mult, ["MS"], ks("F1_", S8))
 
     def marks2():
-        tt(blk("ZZ1", 0, 8), blk("Z12", 0, 8), blk("Z1", 1, 8), A.subtract, ["Z12"] + Z1K, ks("ZZ1_", range(8)))
-        cp(blk("ZZ1", 8), blk("Z12", 8), ["Z12"], ["ZZ1_8"])
+        pe([(T.MS[:, 0:384], T.IDF[:], blk("F1", 0, 8), ["IDF"] + ks("F1_", range(8)))] +
+           [(T.MS[:, 96 * d:96 * d + 96], T["IDF" if d % 2 else "NID"][:], blk("F1", 2 * d + 1, 2), ["IDF", "NID"] + ks("F1_", S8))
+            for d in range(4)], ["MS"])
 
-    def kept():
-        ts(T.LZ[:], blk("Z1", 1, 8), 1.0 / 256.0, None, A.mult, None, Z1K, ["LZ"])
-        tt(T.LT1[:], T.LTA[:], T.LZ[:], A.max, ["LZ"] + ks("LTA", range(4)), ["LT1"])
+    def marks3():
+        cp(blk("ZZ1", 0, 8), T.MS[:, 0:384], ["MS"], ks("ZZ1_", range(8)))
 
     def newword():
-        pe(sels(T.YB[:, 0:48], "OHY", "OHY", "SBX"), ["YB0"])
+        ts(T.KY[:], T.KI[:], 11, 15, A.arith_shift_right, A.bitwise_and, ["KI"], ["KY"])
+        ts(T.LY[:, 8:136], T.KY[:], -1.0, 15.0, A.mult, A.add, ["KY"], ["LY"])
 
     def newword2():
-        cp(T.Y1W[:], T.YB[:, 0:48], ["YB0"], ["Y1W"])
+        o = T.MS[:, 0:48]
+        pe([(o, T.LY[0:96, 8 - 8 * e:136 - 8 * e], T.IDF[0:96, e:96:2], ["LY", "IDF"]) for e in range(2)], ["MS"])
 
-    walk(1, {-1: [marks], 0: [marks2], 1: [kept, newword], 2: [newword2]})
+    def newword3():
+        cp(T.Y1W[:], T.MS[:, 0:48], ["MS"], ["Y1W"])
 
-    ts(T.DM[:], T.M1[:], 0.5, 16.0, A.is_gt, A.mult, ["M1"], ["DM"])
-    tt(T.YI1[:, 0:48], T.Y1W[:], T.DM[:], A.max, ["Y1W", "DM"], ["YI1"])
+    def first_word():
+        o = T.MS[:, 0:48]
+        pe([(o, T.IDB[:], T.Y0W[:, 0:48], ["IDB", "Y0W"]), (o, T.IDF[:], blk("F1", 0), ["IDF", "F1_0"]),
+            (o, T.IDF[:], blk("H1", 1), ["IDF", "H1_0"])], ["MS"])
+
+    def first_word2():
+        ts(T.YI0[:, 0:48], T.MS[:, 0:48], 16.0, None, A.min, None, ["MS"], ["YI0"])
+
+    walk(1, {(-1, 0): [marks, marks2], (0, 0): [marks3], (1, 0): [newword, newword2], 2: [newword3], 5: [first_word], 6: [first_word2]},
+         {}, ())
+
+    o = T.X[:, 0:48]
+    pe([(o, T.IDF[:], T.Y1W[:], ["IDF", "Y1W"]), (o, T.IDF[:], blk("H1", 8), ["IDF", "H1_7"]), (o, T.IDF[:], blk("H1", 9), ["IDF", "H1_8"])], ["X"])
+    ts(T.YI1[:, 0:48], o, 16.0, None, A.min, None, ["X"], ["YI1"])
     for h in range(16):
         out, src = T.VN[:, 48 * h:48 * h + 48], T.VF[:, h:768:16]
         if h % 2:
@@ -610,22 +611,21 @@ def rank_program(g, core, T, topo):
     dma("y", T.yi[:, 0:768], T.YI0[:, 0:48], "dO", total, ["YI0"], ["o1"])
     for l in range(2):
         a = (rank * 2 + l) * 768
-        dma("y", T.yl[:, a:a + 768], T.LF[:, 48 * l:48 * l + 48], "dO", total, ["LF%d" % (l + 1)], ["o2%d" % l])
+        dma("y", T.yl[:, a:a + 768], blk("LF", l), "dO", total, ["LF0"], ["o2%d" % l])
 
     def home(d):
         s = (rank - d) % n
         nm = "aF%d" % d
-        k = 2 if d == 2 else 8
-        lastw["LI%d" % d] = (nm, k, {nm: k})
+        lastw["LI%d" % d] = (nm, 8, {nm: 8})
         for l in range(2):
             a = (s * 2 + l) * 768
-            dma("y", T.yl[:, a:a + 768], T["LI%d" % d][:, 48 * l:48 * l + 48], "dO", total, ["LI%d" % d], ["o3%d%d" % (d, l)])
+            dma("ys"[l] if d == 3 else "y", T.yl[:, a:a + 768], T.RET[2 * d - 2 + l], "dO", total, ["LI%d" % d], ["o3%d%d" % (d, l)])
 
     home(1)
     dma("y", T.yi[:, 768:1536], T.YI1[:, 0:48], "dO", total, ["YI1"], ["o4"])
-    dma("y", T.yv[:], T.VN[:], "dO", total, ks("VN", range(16)), ["o5"])
     home(2)
+    dma("s", T.yv[:], T.VN[:], "dO", total, ks("VN", range(16)), ["o5"])
     home(3)
     g.sync.wait_ge(T.sem.dO, total)
-    for s, v in (("lo", lo[0]), ("qv", cnt["v"]), ("qs", cnt["s"]), ("qp", cnt["p"]), ("qg", cnt["g"]), ("dLr", 96)):
+    for s, v in (("lo", lo[0]), ("qv", cnt["v"]), ("qs", cnt["s"]), ("qp", cnt["p"]), ("qg", cnt["g"])):
         g.wait_ge(T.sem[s], v)

@@ -4,95 +4,95 @@ from concourse.mybir import AluOpType as A, ActivationFunctionType as F
 SCRATCH = {"LTD": ("dram", [6, 128, 48], "bfloat16"), "RET": ("dram", [6, 128, 48], "bfloat16")}
 for _ty, _s in (
         ("bfloat16", "C0 2064 C1 2064 C2 2064 C3 2064 OHN 768 CG0 768 CG1 768 VS 768 OUT 6912 SG0 768 SG1 768 VF 768 VN 768 "
-         "LTA 384 LF 384 Y0W 64 Y0R 768 YI0 64 YI1 64 ET 32 IDB 128 I32 128 SBB 144 GE 128 "
-         "IR 512 ONE 128 PAT 512 " + " ".join("OH%d 768" % k for k in range(9))),
+         "LTA 384 LF 384 Y0W 64 Y0R 768 YI0 64 YI1 64 ET 32 IDB 128 SBB 144 GE 128 IR 512 ONE 128 PAT 512 "
+         "F0 432 F1 432 ZZ0 432 ZZ1 432 H0 480 H1 480 DL 96 JC 48 T16 48 Y1W 48 "
+         "NIB 128 P1K 128 N1K 128 P2K 128 N2K 128 M384 128 P256 128 M48 128 I32 128 " + " ".join("OH%d 768" % k for k in range(9))),
         ("int32", "JA 6144 JB 6144 STI 96 KI 128 KB 128 KY 128 PI 8 PJ 8"),
-        ("float16", "MJ0 768 MJ1 768 JZ 1552 F0 432 F1 432 ZZ0 432 ZZ1 432 H0 480 H1 480 IDF 128 NID 128 ID3 128 SBF 144 "
-         "LB 144 LY 144 JC 48 T16 48 Y1W 48"),
+        ("float16", "MJ0 768 MJ1 768 JZ 1536 IDF 128 SBF 144 LB 144 LY 144"),
         ("uint16", "STU 96 OFJ 48 OC0 48 OC1 48 LU 384 Y0U 48 SEL 48 KO 8"),
-        ("float32", "KM 1040 TC0 48 TC1 48 PC 8 PK 8 V8 8 V8A 8 V8B 8 XR 32 XS 32 JR 48 IV 128"),
+        ("float32", "KM 1040 TC0 48 TC1 48 PC 8 PK 8 V8 8 V8A 8 V8B 8 XR 32 JR 48 IV 128"),
         ("psum", "X 512 AD 1024 KA 512 KBK 512 KEY 1024 MS 512")):
     _p = _s.split()
     for _n, _w in zip(_p[::2], _p[1::2]):
         SCRATCH[_n] = ("psum", [128, int(_w)], "float32") if _ty == "psum" else ("sbuf", [128, int(_w)], _ty)
 
-SEMAPHORES = "qv qs qp qg dJA dJB dC dSt dY dW dLo dLr dO lo rJ rC rL rF".split()
+SEMAPHORES = "qv qs qp qg dJA dJB dC dSt dY dW dLo dLr dO lo rJ rC rL rF fC2 fJ3 fC3".split()
 SEMAPHORES += ["%s%d" % (a, d) for a in ("aJ", "aC", "aL", "aF") for d in (1, 2, 3)]
 
 WORLD = 256
 JAT = {0: ("JA", 0), 1: ("JA", 4096), 2: ("JB", 0), 3: ("JB", 4096)}
+SCALED = (("NIB", -1), ("N2K", -2048), ("P1K", 1024), ("N1K", -1024), ("M384", -384), ("I32", 32768), ("P2K", 2048), ("P256", 256), ("M48", -48))
 
 
 def routes(topo, cores, r):
     c, n = cores[r], len(cores)
-    x1, x3 = cores[(r - 1) % n], cores[(r - 3) % n]
-    own = [e for e in topo.cores_of(c) if e != c and topo.may_write(e, x1)]
+    own = [e for e in topo.cores_of(c) if e != c and topo.may_write(e, cores[(r - 1) % n])]
     same = [e for e in own if topo.die(e) == topo.die(c)]
     oth = [e for e in own if topo.die(e) != topo.die(c)]
     relays = [same[0], oth[0], same[1], oth[1]]
-    far = [e for e in range(WORLD) if topo.mates(e, x3) and topo.may_write(e, x3)]
-    pick = []
-    for e in relays:
-        pick.append([y for y in far if topo.die(y) == topo.die(e) and y not in pick][0])
-    return relays, pick
+    far = [e for e in range(WORLD) if topo.mates(e, c) and topo.may_write(e, c)]
+    return relays, [[y for y in far if topo.die(y) == topo.die(e)][i // 2] for i, e in enumerate(relays)]
 
 
-def carriers(topo, cores, r):
-    relays = routes(topo, cores, r)[0]
-    rest = [e for e in topo.cores_of(cores[r]) if e != cores[r] and e not in relays]
-    return relays[0:2] + rest[0:2] + relays[2:4]
+def piece(T, w, d, i, half=None):
+    nm, a = JAT[d] if w == "J" else ("C%d" % d, 0)
+    a += 512 * i + 256 * (half or 0)
+    return T[nm][:, a:a + (512 if half is None else 256)]
 
 
-def jpiece(T, d, i):
-    nm, a = JAT[d]
-    return T[nm][:, a + 512 * i:a + 512 * i + 512]
+def transfers(topo, T, core, items):
+    tr = []
+    for c, e, i, o, s in items:
+        rid, pid = topo.addr(c, core)
+        tr.append(RemoteDMATransfer(dst_ids=[DstId(rid=rid, pnc=pid)], dma_engine_mask=sum(1 << b for b in e), remote_sem=T.sem[s], src=i, dst=o))
+    return tr
 
 
 def hand_on(g, core, T, topo):
     cores, n = T.cores, len(T.cores)
     lo = [0]
 
+    def fused(items):
+        g.remote_dma_fused(transfers(topo, T, core, items), local_sem=T.sem.lo)
+        lo[0] += sum(len(it[1]) for it in items)
+
     def send(dst, out, in_, sem):
-        rid, pid = topo.addr(dst, core)
-        g.remote_dma(out, in_, T.sem[sem], T.sem.lo, pid, rid, topo.mask(core, dst))
-        lo[0] += len(topo.engines(core, dst))
+        fused([(dst, topo.engines(core, dst), in_, out, sem)])
 
     for r in range(n):
-        relays, far = routes(topo, cores, r)
+        relays, gates = routes(topo, cores, r)
         x = [cores[(r - d) % n] for d in range(n)]
-        if core in carriers(topo, cores, r):
-            i = carriers(topo, cores, r).index(core)
+        into = [routes(topo, cores, (r - d) % n)[1] for d in range(n)]
+        carriers = relays + into[3][0:2]
+        if core in carriers:
+            i = carriers.index(core)
             g.wait_ge(T.sem.rL, 2)
             send(x[i // 2 + 1], T.LTA[:, 96 + 48 * i:144 + 48 * i], T.LTD[0], "aL%d" % (i // 2 + 1))
+    for r in range(n):
+        relays, gates = routes(topo, cores, r)
+        x = [cores[(r - d) % n] for d in range(n)]
+        into = [routes(topo, cores, (r - d) % n)[1] for d in range(n)]
         if core in relays:
             i = relays.index(core)
-            cs = slice(512 * i, 512 * i + 512)
+            off = topo.engines(core, x[1])
+            a, b = off[0:4], off[4:8]
+            J, C = piece(T, "J", 0, i), piece(T, "C", 0, i)
             g.wait_ge(T.sem.rJ, 8)
-            send(x[1], jpiece(T, 1, i), jpiece(T, 0, i), "aJ1")
+            send(x[1], piece(T, "J", 1, i), J, "aJ1")
+            fused([(into[3][i], b, piece(T, "J", 0, i, 0), piece(T, "J", 3, i, 0), "fJ3")])
             g.wait_ge(T.sem.rC, 4)
-            send(x[1], T.C1[:, cs], T.C0[:, cs], "aC1")
-            send(x[2], jpiece(T, 2, i), jpiece(T, 0, i), "aJ2")
-            send(far[i], jpiece(T, 0, i), jpiece(T, 0, i), "rJ")
-            send(x[2], T.C2[:, cs], T.C0[:, cs], "aC2")
-            send(far[i], T.C0[:, cs], T.C0[:, cs], "rC")
+            fused([(x[1], a, C, piece(T, "C", 1, i), "aC1"), (into[2][i], b, C, piece(T, "C", 2, i), "fC2")])
+            fused([(x[2], a, J, piece(T, "J", 2, i), "aJ2")])
+            fused([(x[3], a, piece(T, "J", 0, i, 1), piece(T, "J", 3, i, 1), "aJ3"), (into[3][i], b, C, piece(T, "C", 3, i), "fC3")])
             if i in (0, 2):
                 d = 3 if i == 0 else 1
                 g.wait_ge(T.sem.rF, 16)
-                rid, pid = topo.addr(cores[(r + d) % n], core)
-                e = topo.engines(core, cores[(r + d) % n])
-                g.remote_dma_fused([RemoteDMATransfer(dst_ids=[DstId(rid=rid, pnc=pid)], dma_engine_mask=sum(1 << b for b in e[4 * l:4 * l + 4]),
-                                                      remote_sem=T.sem["aF%d" % d], src=T.RET[2 * d - 2 + l], dst=T.RET[2 * d - 2 + l])
-                                    for l in range(2)], local_sem=T.sem.lo)
-                lo[0] += 8
-        if core in far:
-            i = far.index(core)
-            x3 = cores[(r - 3) % n]
-            cs = slice(512 * i, 512 * i + 512)
-            k = len(topo.engines(relays[i], core))
-            g.wait_ge(T.sem.rJ, k)
-            send(x3, jpiece(T, 3, i), jpiece(T, 0, i), "aJ3")
-            g.wait_ge(T.sem.rC, k)
-            send(x3, T.C3[:, cs], T.C0[:, cs], "aC3")
+                fused([(cores[(r + d) % n], off[4 * l:4 * l + 4], T.RET[2 * d - 2 + l], T.RET[2 * d - 2 + l], "aF%d" % d) for l in range(2)])
+        if core in gates:
+            i = gates.index(core)
+            for w, d, h in (("J", 3, 0), ("C", 2, None), ("C", 3, None)):
+                g.wait_ge(T.sem["f%s%d" % (w, d)], 4)
+                send(x[0], piece(T, w, d, i, h), piece(T, w, d, i, h), "a%s%d" % (w, d))
     if lo[0]:
         g.wait_ge(T.sem.lo, lo[0])
 
@@ -103,7 +103,8 @@ def rank_program(g, core, T, topo):
         hand_on(g, core, T, topo)
         return
     cores, n = T.cores, len(T.cores)
-    relays, far = routes(topo, cores, rank)
+    relays = routes(topo, cores, rank)[0]
+    carriers = relays + routes(topo, cores, (rank - 3) % n)[1][0:2]
     Q = {"v": g.vector, "s": g.scalar, "p": g.tensor, "g": g, "y": g.sync}
     SEM = {"v": "qv", "s": "qs", "p": "qp", "g": "qg"}
     cnt = {q: 0 for q in SEM}
@@ -159,6 +160,9 @@ def rank_program(g, core, T, topo):
         c["qp"] = cnt["p"]
         done(("qp", cnt["p"], c), allr, writes)
 
+    def lin(o, terms):
+        return [(o, T[m][:], x, [m] + rd) for m, x, rd in terms]
+
     def dma(q, out, in_, sem, total, reads, writes):
         need(q, [t for t in deps(q, reads, writes) if t and t[0] != sem])
         Q[q].dma_start(out, in_).then_inc(T.sem[sem], 16)
@@ -208,7 +212,7 @@ def rank_program(g, core, T, topo):
     dma("s", T.C0[:, 0:2048], T.cf[:], "dC", 16, [], ["C0"])
     dma("y", T.Y0W[:, 0:48], T.y0[:], "dW", 16, [], ["Y0W"])
     for d in range(1, n):
-        for a, w, k in (("aJ", "J", 32), ("aC", "C", 32), ("aL", "LTA", 16)):
+        for a, w, k in (("aJ", "J", (32, 16, 48)[d - 1]), ("aC", "C", (16, 32, 32)[d - 1]), ("aL", "LTA", 16)):
             nm = "%s%d" % (a, d)
             lastw["%s%d" % (w, d)] = (nm, k, {nm: k})
 
@@ -232,8 +236,15 @@ def rank_program(g, core, T, topo):
     cp(T.SBF[:], T.SBB[:], ["SBB"], ["SBF"])
     ts(T.ET[:], T.XR[:], T.PC[:, 0:1], None, A.is_equal, None, ["XR", "PC"], ["ET"])
     cp(T.IDF[:], T.IDB[:], ["IDB"], ["IDF"])
-    cp(T.GE[0:8, :], T.X[0:8, 0:128], ["X"], ["GE"])
-    ts(T.NID[:], T.IDB[:], -1.0, None, A.mult, None, ["IDB"], ["NID"])
+    act(T.GE[0:8, :], T.X[0:8, 0:128], F.Copy, ["X"], ["GE"])
+    for m, w in SCALED:
+        act(T[m][:], T.IDB[:], F.Copy, ["IDB"], [m], scale=float(w))
+    for t in range(2):
+        fill(T["H%d" % t][:, 0:96], -1.0, ks("H%d_" % t, (-1, 0)))
+    fill(T.T16[:], -16.0, ["T16"])
+    ts(T.PK[:, 0:1], T.PC[:, 0:1], 128.0, 15.0, A.mult, A.add, ["PC"], ["PK"])
+    for m in ("LB", "LY"):
+        ts(T[m][:, 0:16], T.IDB[:, 0:16], 0.0, None, A.mult, None, ["IDB"], [m])
 
     def sels(o, buf, rd, sb="SBF", contiguous=False):
         src = T[buf]
@@ -246,16 +257,16 @@ def rank_program(g, core, T, topo):
     def tab(k):
         return (k - 1) // 2 if k > 0 else 0
 
-    def letters(d):
-        src, k = T.LTA[:, 96 * d:96 * d + 96], 2 * d + 1
-        L = "LTA%d" % d
-        cp(T.LU[:, 96 * d:96 * d + 96], src, [L], ["LU%d" % d])
-        ts(blk("F0", k, 2), src, 15.5, 2048.0, A.is_gt, A.mult, [L], ks("F0_", (k, k + 1)))
+    def letters(a, b):
+        src, rd = T.LTA[:, 96 * a:96 * b], ks("LTA", range(a, b))
+        ts(blk("F0", 2 * a + 1, 2 * (b - a)), src, 15.5, 2048.0, A.is_gt, A.mult, rd, ks("F0_", range(2 * a + 1, 2 * b + 1)))
+        cp(T.LU[:, 96 * a:96 * b], src, rd, ks("LU", range(a, b)))
 
-    def diffs(d):
-        k, m = (1, 1) if d == 0 else (2 * d, 2)
-        tt(blk("ZZ0", k, m), blk("F0", k, m), blk("F0", k + 1, m), A.add if d % 2 else A.subtract,
-           ks("F0_", range(k, k + m + 1)), ks("ZZ0_", range(k, k + m)))
+    def diffs(t, a):
+        FN = "F%d" % t
+        rd = ks(FN + "_", range(2 * a, 9))
+        pe(lin(T.MS[:, 96 * a:384], [("IDB", blk(FN, 2 * a, 8 - 2 * a), rd)]) +
+           [lin(T.MS[:, 96 * d:96 * d + 96], [("IDB" if d % 2 else "NIB", blk(FN, 2 * d + 1, 2), rd)])[0] for d in range(a, 4)], ["MS"])
 
     def onehot(k):
         off = T.Y0U[:] if k == 0 else blk("LU", k - 1)
@@ -265,27 +276,17 @@ def rank_program(g, core, T, topo):
 
     def fused(items, reads):
         need("g", deps("g", reads, []))
-        tr = []
-        for c, e, i, o, s in items:
-            rid, pid = topo.addr(c, core)
-            tr.append(RemoteDMATransfer(dst_ids=[DstId(rid=rid, pnc=pid)], dma_engine_mask=sum(1 << b for b in e),
-                                        remote_sem=T.sem[s], src=i, dst=o))
-            lo[0] += len(e)
-        g.remote_dma_fused(tr, local_sem=T.sem.lo)
+        g.remote_dma_fused(transfers(topo, T, core, items), local_sem=T.sem.lo)
+        lo[0] += sum(len(it[1]) for it in items)
 
     on = topo.engines(core, relays[0])
-    direct = cores[(rank - 2) % n]
-    off = topo.engines(core, direct)
-    hi = [e for e in on if e not in off]
+    off = topo.engines(core, cores[(rank + 2) % n])
 
-    def half(a, key):
-        fused([(relays[a], on[0:8], jpiece(T, 0, a), jpiece(T, 0, a), "rJ"),
-               (relays[a + 1], on[8:16], jpiece(T, 0, a + 1), jpiece(T, 0, a + 1), "rJ")], [key])
-
-    fused([(e, on[2 * i:2 * i + 2], T.LTD[i], T.LTD[0], "rL") for i, e in enumerate(carriers(topo, cores, rank))], ["LTS"])
-    half(0, "J0a")
-    half(2, "J0b")
-    fused([(relays[i], on[4 * i:4 * i + 4], T.C0[:, 512 * i:512 * i + 512], T.C0[:, 512 * i:512 * i + 512], "rC") for i in range(4)], ["C0"])
+    order = [e for e in on if e not in off] + off
+    fused([(e, order[2 * i:2 * i + 2], T.LTD[i], T.LTD[0], "rL") for i, e in enumerate(carriers)], ["LTS"])
+    for a, key in ((0, "J0a"), (2, "J0b")):
+        fused([(relays[a + i], on[8 * i:8 * i + 8], piece(T, "J", 0, a + i), piece(T, "J", 0, a + i), "rJ") for i in range(2)], [key])
+    fused([(relays[i], on[4 * i:4 * i + 4], piece(T, "C", 0, i), piece(T, "C", 0, i), "rC") for i in range(4)], ["C0"])
 
     iota(T.JR[:], [[16, 48]], 0, 0, ["JR"])
     iota(T.IR[0:1, :], [[0, 32], [-2048, 16]], 30720, 0, ["IR"])
@@ -301,10 +302,10 @@ def rank_program(g, core, T, topo):
     for hf in range(2):
         ts(T.OHN[:, 384 * hf:384 * hf + 384], T.AD[:, 512 * hf:512 * hf + 384], T.PC[:, 0:1], None, A.is_equal, None,
            ["AD%d" % hf, "PC"], ["OHN%d" % hf])
-    letters(0)
+    letters(0, 1)
     onehot(1)
     onehot(2)
-    diffs(0)
+    tt(blk("ZZ0", 1), blk("F0", 1), blk("F0", 2), A.subtract, ["F0_1", "F0_2"], ["ZZ0_1"])
 
     def same(k):
         ts(T.JA[:, 2048 + 512 * k:2560 + 512 * k], T.JA[:, 2048:2560], 512.0 * k, None, A.add, None, ["IDA0"], ["IDA%d" % k])
@@ -313,21 +314,13 @@ def rank_program(g, core, T, topo):
     same(2)
 
     def late_constants():
-        for t in range(2):
-            ts(T["H%d" % t][:, 0:96], T.IDB[:, 0:96], 0.0, None, A.mult, None, ["IDB"], ks("H%d_" % t, (-1, 0)))
-        ts(T.ID3[:], T.IDB[:], -0.1875, None, A.mult, None, ["IDB"], ["ID3"])
-        ts(T.I32[:], T.IDB[:], 32768.0, None, A.mult, None, ["IDB"], ["I32"])
-        cp(T.JC[:], T.JR[:], ["JR"], ["JC"])
-        ts(T.T16[:], T.JR[:], 0.0, -16.0, A.mult, A.add, ["JR"], ["T16"])
-        ts(T.PK[:, 0:1], T.PC[:, 0:1], 128.0, 15.0, A.mult, A.add, ["PC"], ["PK"])
-        ts(T.LB[:, 0:16], T.IDB[:, 0:16], 0.0, None, A.mult, None, ["IDB"], ["LB"])
-        ts(T.LY[:, 0:16], T.IDB[:, 0:16], 0.0, None, A.mult, None, ["IDB"], ["LY"])
+        act(T.JC[:], T.JR[:], F.Copy, ["JR"], ["JC"])
         ts(T.KO[:], T.JR[:, 0:8], T.PK[:, 0:1], 1024.0, A.add, A.min, ["JR", "PK"], ["KO"])
+        cp(T.Y0U[:], T.Y0W[:, 0:48], ["Y0W"], ["Y0U"])
+        ts(T.JZ[:, 0:1536:2], T.OHN[:], 0.0, None, A.mult, None, ["OHN0", "OHN1"], ["JZ0"])
 
     def start_images():
-        cp(T.Y0U[:], T.Y0W[:, 0:48], ["Y0W"], ["Y0U"])
-        ts(T.JZ[:, 0:1538:2], T.C0[:, 0:769], 0.0, None, A.mult, None, ["C0"], ["JZ0"])
-        cp(T.JZ[:, 1:1537:2], T.JA[:, 0:2048].indirect(blk("STU", 1)), ["STU", "J0a", "J0b"], ["JZ1"])
+        cp(T.JZ[:, 1:1536:2], T.JA[:, 0:2048].indirect(blk("STU", 1)), ["STU", "J0a", "J0b"], ["JZ1"])
 
     def start_keys():
         for b in range(2):
@@ -347,7 +340,10 @@ def rank_program(g, core, T, topo):
         rd = ["J0a", "J0b"] if d == 0 else ["J%d" % d]
         return T[nm][:, a:a + 4096], rd + (ks("IDA", range(4)) if d < 2 else ["IDB2"])
 
-    def walk(t, gaps, sgaps, vsign):
+    def unfold(o, m):
+        return [(o, T[m][0:96, 8 - 8 * e:136 - 8 * e], T.IDF[0:96, e:96:2], [m, "IDF"]) for e in range(2)]
+
+    def walk(t, gaps, vsign):
         first = 1 - t
         FN, ZN, HN = "F%d" % t, "ZZ%d" % t, "H%d" % t
 
@@ -372,27 +368,21 @@ def rank_program(g, core, T, topo):
 
         def step_x(k):
             m = "MJ%d" % (k % 2)
-            if k < first and t:
-                items = [(X, T.LB[0:96, 8 - 8 * e:136 - 8 * e], T.IDF[0:96, e:96:2], ["LB", "IDF"]) for e in range(2)]
-            else:
-                items = sels(X, m, [m], contiguous=k < first)
+            items = unfold(X, "LB") if k < first and t else sels(X, m, [m], contiguous=k < first)
             if k < 8:
-                w = "NID" if tab(k + 1) % 2 else "IDF"
-                items.append((X, T[w][:], blk(FN, k + 1), [w, fk(k + 1)]))
+                items += lin(X, [("NIB" if tab(k + 1) % 2 else "IDB", blk(FN, k + 1), [fk(k + 1)])])
             pe(items, ["X"])
 
-        def step_off(k, between=None):
+        def step_off(k):
             a, o = "TC%d" % (k % 2), "OC%d" % (k % 2)
-            if k < 8:
-                ts(T.OFJ[:], X, 2048.0 * (tab(k + 1) % 2), None, A.add, None, ["X"], ["OFJ"])
             if k < first:
                 tt(T[a][:], X, blk(FN, first), A.subtract, ["X", fk(first)], [a])
             elif k == 8:
                 tt(T[a][:], X, blk(FN, 8), A.add, ["X", fk(8)], [a])
             else:
                 tt(T[a][:], X, blk(ZN, k), A.add, ["X", "%s_%d" % (ZN, k)], [a])
-            if between:
-                between()
+            if k < 8:
+                ts(T.OFJ[:], X, 2048.0 * (tab(k + 1) % 2), None, A.add, None, ["X"], ["OFJ"])
             ts(T[o][:], T[a][:], 2048.0, None, A.min, None, [a], [o])
 
         def step_c(k, hf):
@@ -405,8 +395,8 @@ def rank_program(g, core, T, topo):
                 return
             v, vk = vblk(k - 1, hf)
             c = "CG%d" % (k % 2)
-            o = T.AD[:, 512 * hf:512 * hf + 384]
-            pe([(o, T.IDB[:], v, ["IDB", vk]), (o, T.IDB[:], T[c][:, 384 * hf:384 * hf + 384], ["IDB", "%s_%d" % (c, hf)])], ["AD%d" % hf])
+            pe(lin(T.AD[:, 512 * hf:512 * hf + 384], [("IDB", v, [vk]), ("IDB", T[c][:, 384 * hf:384 * hf + 384], ["%s_%d" % (c, hf)])]),
+               ["AD%d" % hf])
 
         def cut(k, hf):
             if k < first:
@@ -424,11 +414,11 @@ def rank_program(g, core, T, topo):
             o, w = T[s][:, 384 * hf:384 * hf + 384], ["%s_%d" % (s, hf)]
             how[k, hf] = q
             if q == "v":
-                ts(o, v, 0.0, 2.0, A.is_ge, A.mult, [vk], w)
+                ts(o, v, 0.0, 2.0, A.is_ge, A.mult, [vk], w if src is None or vk[0] != "A" else w + [vk])
             else:
-                act(o, v, F.Sign, [vk], w, bias=0.5)
+                act(o, v, F.Sign, [vk], w if src is None or vk[0] != "A" else w + [vk], bias=0.5)
 
-        def count(k, dead="NID"):
+        def count(k, dead=None):
             if k < first:
                 return
             p, s = KP[k % 2], "SG%d" % (k % 2)
@@ -436,29 +426,31 @@ def rank_program(g, core, T, topo):
             items = sels(o, s, [s + "_0", s + "_1"], "SBB")
             if how[k, 0] != how[k, 1]:
                 a = 24 * (how[k, 1] == "v")
-                items.append((T[p][:, a:a + 24], T.IDF[:], T.T16[:, 0:24], ["IDF", "T16"]))
-            items.append((o, T.IDF[:], blk(FN, k), ["IDF", fk(k)]))
-            if k > first:
-                items.append((o, T[dead][:], blk(HN, k), [dead, hk(k - 1)]))
+                items += lin(T[p][:, a:a + 24], [("IDB", T.T16[:, 0:24], ["T16"])])
+            items += lin(o, [("IDB", blk(FN, k), [fk(k)])] + (dead or [("N2K", blk(HN, k), [hk(k - 1)])]))
             pe(items, [p])
 
         def judge(k):
             if k < first:
                 return
             p = KP[k % 2]
-            thr = 15.0 if how[k, 0] == how[k, 1] == "v" else -1.0
-            ts(blk(HN, k + 1), T[p][:, 0:48], thr, 4096.0, A.is_lt, A.mult, [p], [hk(k)])
+            thr = 2063.0 if how[k, 0] == how[k, 1] == "v" else 2047.0
+            act(blk(HN, k + 1), T[p][:, 0:48], F.Sign, [p], [hk(k)], bias=thr, scale=-1.0)
 
         def left(d):
-            k, o = 2 * d + 1, T.KEY[:, 512 * (d % 2):512 * (d % 2) + 96]
-            pe([(o, T.IDB[:], T.LTA[:, 96 * d:96 * d + 96], ["IDB", "LTA%d" % d]),
-                (o, T.IDF[:], blk(FN, k, 2), ["IDF", fk(k), fk(k + 1)]),
-                (o, T.NID[:], blk(HN, k, 2), ["NID", hk(k - 1), hk(k)]),
-                (o, T.IDF[:], blk(HN, k + 1, 2), ["IDF", hk(k), hk(k + 1)])], ["KEY%d" % (d % 2)])
+            k = 2 * d + 1
+            terms = [("IDB", T.LTA[:, 96 * d:96 * d + 96], ["LTA%d" % d]), ("IDB", blk(FN, k, 2), [fk(k), fk(k + 1)])]
+            if d < 3:
+                terms += [("N1K", blk(HN, k, 2), [hk(k - 1), hk(k)]), ("P1K", blk(HN, k + 1, 2), [hk(k), hk(k + 1)])]
+            pe(lin(T.KEY[:, 512 * (d % 2):512 * (d % 2) + 96], terms), ["KEY%d" % (d % 2)])
 
         def left2(d):
             ts(T.LF[:, 96 * d:96 * d + 96], T.KEY[:, 512 * (d % 2):512 * (d % 2) + 96], 16.0, None, A.min, None,
                ["KEY%d" % (d % 2)], ["LF%d" % d])
+
+        def last(k):
+            ts(blk("DL", k - 7), T[KP[k % 2]][:, 0:48], -2049.0, 16.0, A.is_lt, A.mult, [KP[k % 2]], ["DL%d" % k])
+            tt(blk("LF", k - 1), blk("LF", k - 1), blk("DL", k - 7), A.max, ["LF3", "DL%d" % k], ["LF3"])
 
         def goes(d):
             if d == 2:
@@ -468,139 +460,115 @@ def rank_program(g, core, T, topo):
             m = len(e) // 2
             fused([(c, e[m * l:m * l + m], blk("LF", 2 * d + l), T.RET[2 * d - 2 + l], sem) for l in range(2)], ["LF%d" % d])
 
-        def run(fs):
-            for f in fs:
+        def run(key):
+            for f in gaps.get(key, []):
                 f()
 
         for k in range(first - 1, 9):
             if k >= first or t == 0:
                 step_j(k)
+            run((k, "j"))
             add(k - 1, 0)
             step_x(k)
-            run(gaps.get((k, 0), []))
+            run((k, "x"))
             cut(k - 2, 1)
             add(k - 1, 1)
             cut(k - 1, 0)
+            judge(k - 3)
             for hf in range(2):
                 sign(k - 2, hf, "v" if (k - 2, hf) in vsign else "s")
-            run(gaps.get(k, []))
-            if t and k in (6, 8):
-                left2(k // 2 - 3)
-            step_off(k, lambda: judge(k - 3))
+            if t and k in (2, 6, 8):
+                left2({2: 3, 6: 0, 8: 1}[k])
+            run((k, "c"))
+            step_off(k)
             if t and k == 8:
                 goes(1)
-            run(sgaps.get(k, []))
+            run((k, "o"))
             step_c(k, 0)
             if k < 8:
                 step_c(k, 1)
             count(k - 2)
-            if t and k in (5, 7):
-                left(k // 2 - 2)
+            if t and k in (1, 5, 7):
+                left({1: 3, 5: 0, 7: 1}[k])
         cut(7, 1)
         add(8, 0)
         sign(7, 0, "s")
-        sign(7, 1, "s")
         judge(6)
+        sign(7, 1, "v")
+        raw = T.CG0[:, 384:768]
+        tt(raw, T.C3[:, 0:2056].indirect(T.OC0[:, 24:48]), vblk(7, 1)[0], A.add, ["C3", "Cz3", "OC0", "OUT7_1"], ["CG0_1"])
         S = T.MS[:, 0:48]
-        pe([(S, T.IDF[:], T.JC[:], ["IDF", "JC"])] + [(S, T.ID3[:], blk(HN, k + 1), ["ID3", hk(k)]) for k in range(first, 7)], ["MS"],
-           stop=False)
-        if t:
+        gone = [("IDB", T.JC[:], ["JC"])] + [("M384", blk(HN, k + 1), [hk(k)]) for k in range(first, 7)]
+        if t == 0:
+            count(7)
+            pe(lin(S, gone), ["MS"], stop=False)
+            cut(8, 0)
+            sign(8, 1, "s", (raw, "CG0_1"))
+            judge(7)
+            ts(vblk(8, 1)[0], raw, 255.0, -255.0, A.min, A.max, ["CG0_1"], ["OUT8_1"])
+            pe(lin(S, [("M384", blk(HN, 8), [hk(7)])]), ["MS"], start=False)
+            sign(8, 0, "s")
+            count(8)
+        else:
+            dead = [("P2K", blk(HN, 7), [hk(6)])]
+            count(7, dead)
+            sign(8, 0, "s", (T.AD[:, 0:384], "AD0"))
+            sign(8, 1, "v", (raw, "CG0_1"))
+            ts(vblk(8, 1)[0], raw, 255.0, -255.0, A.min, A.max, ["CG0_1"], ["OUT8_1"])
+            last(7)
+            count(8, dead + [("P256", blk("DL", 0), ["DL7"])])
+            cut(8, 0)
+            pe(lin(S, gone + [("M384", blk(HN, 7), [hk(6)]), ("M48", blk("DL", 0), ["DL7"])]), ["MS"])
             left(2)
-        tt(T.CG0[:, 384:768], T.C3[:, 0:2056].indirect(T.OC0[:, 24:48]), vblk(7, 1)[0], A.add, ["C3", "Cz3", "OC0", "OUT7_1"], ["CG0_1"])
-        count(7)
-        cut(8, 0)
-        sign(8, 1, "s", (T.CG0[:, 384:768], "CG0_1"))
+            last(8)
+            goes(3)
+        ts(T.SEL[:], S, T.PC[:, 0:1], 384.0 * (8 - first), A.add, A.add, ["MS", "PC"], ["SEL"])
         if t:
-            sign(8, 0, "v")
             left2(2)
             goes(2)
-        ts(vblk(8, 1)[0], T.CG0[:, 384:768], 255.0, -255.0, A.min, A.max, ["CG0_1"], ["OUT8_1"])
-        judge(7)
-        if t:
-            count(8, "IDF")
-        pe([(S, T.ID3[:], blk(HN, 8), ["ID3", hk(7)])], ["MS"], start=False)
-        if t:
-            o = T.KEY[:, 512:608]
-            pe([(o, T.IDB[:], T.LTA[:, 288:384], ["IDB", "LTA3"]), (o, T.IDF[:], blk(FN, 7, 2), ["IDF", fk(7), fk(8)]),
-                (T.KEY[:, 512:560], T.NID[:], blk(HN, 7), ["NID", hk(6)]), (T.KEY[:, 512:560], T.IDF[:], blk(HN, 8), ["IDF", hk(7)])], ["KEY1"])
-            left2(3)
-            ts(blk(HN, 9), T.KA[:, 0:48], -1.0, 16.0, A.is_lt, A.mult, ["KA"], [hk(8)])
-            tt(blk("LF", 7), blk("LF", 7), blk(HN, 9), A.max, ["LF3", hk(8)], ["LF3"])
-            goes(3)
-        ts(T.SEL[:], S, T.PC[:, 0:1], 768.0 * (8 - first), A.add, A.add, ["MS", "PC"], ["SEL"])
         outs = ["OUT%d_%d" % (k, hf) for k in range(first, 9) for hf in range(2)]
         win = T.OUT[:, 768 * first:6912]
         act(T.VF[:, 384:768], win.indirect(T.SEL[:, 24:48]), F.Copy, ["SEL"] + outs, ["VF1"])
         cp(T.VF[:, 0:384], win.indirect(T.SEL[:, 0:24]), ["SEL"] + outs, ["VF0"])
         if t == 0:
-            sign(8, 0, "s")
-            return lambda: count(8), lambda: judge(8)
+            judge(8)
 
-    def oh(k):
-        return lambda: onehot(k)
+    def oh(*kk):
+        return [lambda k=k: onehot(k) for k in kk]
 
-    def lt(d):
-        return [lambda: letters(d), lambda: diffs(d)]
+    walk(0, {(0, "x"): [lambda: same(3)], (1, "x"): [late_constants], (2, "j"): [lambda: letters(1, 4)],
+             (2, "x"): [lambda: diffs(0, 1), start_images], (2, "c"): [lambda: cp(blk("ZZ0", 2, 6), T.MS[:, 96:384], ["MS"], ks("ZZ0_", range(2, 8)))],
+             (2, "o"): oh(3, 4), (3, "o"): oh(5) + [start_keys], (4, "o"): oh(6), (5, "o"): oh(7), (6, "o"): oh(8)},
+         [(k, hf) for k in range(1, 5) for hf in range(2)])
 
-    cnt8, jdg8 = walk(0, {(0, 0): [lambda: same(3)], (1, 0): [late_constants], 1: lt(1), (2, 0): [start_images], 3: [start_keys] + lt(2), 5: lt(3)},
-                      {1: [oh(3)], 2: [oh(4)], 3: [oh(5)], 4: [oh(6)], 5: [oh(7)], 6: [oh(8)]},
-                      [(k, hf) for k in range(1, 5) for hf in range(2)])
+    act(blk("F1", 0), blk("H0", 9), F.Identity, ["H0_8"], ["F1_0"], bias=1024.0, scale=1024.0)
     onehot(0)
-
     for b in range(2):
         pe([(T.KEY[0:96, 128 * hp:128 * hp + 128], T.VF[:, hp:768:8], T.I32[:], ["VF0", "VF1", "I32"]) for hp in range(4 * b, 4 * b + 4)],
            ["KEY%d" % b], start=False)
-    cnt8()
     for b in range(2):
         op("v", lambda b=b: g.vector.tensor_tensor_scan(T.KM[0:96, 512 * b:512 * b + 512], T.PAT[0:96, :], T.KEY[0:96, 512 * b:512 * b + 512],
                                                        0.0, A.add, A.max), ["PAT", "KEY%d" % b], ["KM%d" % b])
-        if b == 0:
-            jdg8()
     S8 = range(1, 9)
-    o = T.MS[:, 0:384]
-    pe([(o, T.IDF[:], blk("F0", 1, 8), ["IDF"] + ks("F0_", S8)), (o, T.NID[:], blk("H0", 1, 8), ["NID"] + ks("H0_", range(8))),
-        (o, T.IDF[:], blk("H0", 2, 8), ["IDF"] + ks("H0_", S8))], ["MS"])
+    pe(lin(T.MS[:, 0:384], [("IDB", blk("F0", 1, 8), ks("F0_", S8)), ("N1K", blk("H0", 1, 8), ks("H0_", range(8))),
+                            ("P1K", blk("H0", 2, 8), ks("H0_", S8))]), ["MS"])
+    act(blk("F1", 1, 8), T.MS[:, 0:384], F.Copy, ["MS"], ks("F1_", S8))
     cp(T.KI[:], T.KM[:].indirect(T.KO[:]), ["KM0", "KM1", "KMz", "KO"], ["KI"])
-    ts(blk("F1", 0), blk("H0", 9), 0.5, None, A.mult, None, ["H0_8"], ["F1_0"])
     ts(T.KB[:], T.KI[:], 2047, None, A.bitwise_and, None, ["KI"], ["KB"])
     cp(T.LB[:, 8:136], T.KB[:], ["KB"], ["LB"])
-
-    def marks():
-        ts(blk("F1", 1, 8), T.MS[:, 0:384], 1000.0, 2048.0, A.is_gt, A.mult, ["MS"], ks("F1_", S8))
-
-    def marks2():
-        pe([(T.MS[:, 0:384], T.IDF[:], blk("F1", 0, 8), ["IDF"] + ks("F1_", range(8)))] +
-           [(T.MS[:, 96 * d:96 * d + 96], T["IDF" if d % 2 else "NID"][:], blk("F1", 2 * d + 1, 2), ["IDF", "NID"] + ks("F1_", S8))
-            for d in range(4)], ["MS"])
-
-    def marks3():
-        cp(blk("ZZ1", 0, 8), T.MS[:, 0:384], ["MS"], ks("ZZ1_", range(8)))
 
     def newword():
         ts(T.KY[:], T.KI[:], 11, 15, A.arith_shift_right, A.bitwise_and, ["KI"], ["KY"])
         ts(T.LY[:, 8:136], T.KY[:], -1.0, 15.0, A.mult, A.add, ["KY"], ["LY"])
 
-    def newword2():
-        o = T.MS[:, 0:48]
-        pe([(o, T.LY[0:96, 8 - 8 * e:136 - 8 * e], T.IDF[0:96, e:96:2], ["LY", "IDF"]) for e in range(2)], ["MS"])
+    W = T.MS[:, 0:48]
+    walk(1, {(-1, "x"): [lambda: diffs(1, 0)], (0, "j"): [lambda: act(blk("ZZ1", 0, 8), T.MS[:, 0:384], F.Copy, ["MS"], ks("ZZ1_", range(8)))],
+             (0, "x"): [newword], (1, "x"): [lambda: pe(unfold(W, "LY"), ["MS"]), lambda: act(T.Y1W[:], W, F.Copy, ["MS"], ["Y1W"])],
+             (4, "o"): [lambda: pe(lin(W, [("IDB", T.Y0W[:, 0:48], ["Y0W"]), ("IDB", blk("F1", 0), ["F1_0"]), ("P1K", blk("H1", 1), ["H1_0"])]), ["MS"])],
+             (5, "c"): [lambda: ts(T.YI0[:, 0:48], W, 1024.0, 16.0, A.add, A.min, ["MS"], ["YI0"])]}, ())
 
-    def newword3():
-        cp(T.Y1W[:], T.MS[:, 0:48], ["MS"], ["Y1W"])
-
-    def first_word():
-        o = T.MS[:, 0:48]
-        pe([(o, T.IDB[:], T.Y0W[:, 0:48], ["IDB", "Y0W"]), (o, T.IDF[:], blk("F1", 0), ["IDF", "F1_0"]),
-            (o, T.IDF[:], blk("H1", 1), ["IDF", "H1_0"])], ["MS"])
-
-    def first_word2():
-        ts(T.YI0[:, 0:48], T.MS[:, 0:48], 16.0, None, A.min, None, ["MS"], ["YI0"])
-
-    walk(1, {(-1, 0): [marks, marks2], (0, 0): [marks3], (1, 0): [newword, newword2], 2: [newword3], 5: [first_word], 6: [first_word2]},
-         {}, ())
-
-    o = T.X[:, 0:48]
-    pe([(o, T.IDF[:], T.Y1W[:], ["IDF", "Y1W"]), (o, T.IDF[:], blk("H1", 8), ["IDF", "H1_7"]), (o, T.IDF[:], blk("H1", 9), ["IDF", "H1_8"])], ["X"])
-    ts(T.YI1[:, 0:48], o, 16.0, None, A.min, None, ["X"], ["YI1"])
+    pe(lin(X, [("IDB", T.Y1W[:], ["Y1W"]), ("P1K", blk("H1", 7), ["H1_6"]), ("IDB", blk("DL", 0), ["DL7"]), ("IDB", blk("DL", 1), ["DL8"])]), ["X"])
+    ts(T.YI1[:, 0:48], X, 1024.0, 16.0, A.add, A.min, ["X"], ["YI1"])
     for h in range(16):
         out, src = T.VN[:, 48 * h:48 * h + 48], T.VF[:, h:768:16]
         if h % 2:
@@ -623,8 +591,8 @@ def rank_program(g, core, T, topo):
 
     home(1)
     dma("y", T.yi[:, 768:1536], T.YI1[:, 0:48], "dO", total, ["YI1"], ["o4"])
-    home(2)
     dma("s", T.yv[:], T.VN[:], "dO", total, ks("VN", range(16)), ["o5"])
+    home(2)
     home(3)
     g.sync.wait_ge(T.sem.dO, total)
     for s, v in (("lo", lo[0]), ("qv", cnt["v"]), ("qs", cnt["s"]), ("qp", cnt["p"]), ("qg", cnt["g"])):

@@ -1,30 +1,55 @@
 from concourse.bass import DstId, RemoteDMATransfer
 from concourse.mybir import AluOpType as A, ActivationFunctionType as F
 
-SCRATCH = {"LTD": ("dram", [6, 128, 48], "bfloat16"), "RET": ("dram", [6, 128, 48], "bfloat16")}
+SCRATCH = {"LTD": ("dram", [6, 128, 48], "bfloat16"), "RET": ("dram", [6, 128, 48], "bfloat16"), "LTR": ("dram", [2, 128, 96], "bfloat16"),
+           "LTP": ("dram", [2, 128, 96], "bfloat16"), "LW": ("sbuf", [128, 6, 768], "bfloat16")}
 for _ty, _s in (
-        ("bfloat16", "C0 2064 C1 2064 C2 2064 C3 2064 OHN 768 CG0 768 CG1 768 VS 768 OUT 6912 SG0 768 SG1 768 VF 768 VN 768 "
-         "LTA 384 LF 384 Y0W 64 Y0R 768 YI0 64 YI1 64 ET 32 IDB 128 SBB 144 GE 128 IR 512 ONE 128 PAT 512 "
-         "F0 432 F1 432 ZZ0 432 ZZ1 432 H0 480 H1 480 DL 96 JC 48 T16 48 Y1W 48 "
-         "NIB 128 P1K 128 N1K 128 P2K 128 N2K 128 M384 128 P256 128 M48 128 I32 128 " + " ".join("OH%d 768" % k for k in range(9))),
-        ("int32", "JA 6144 JB 6144 STI 96 KI 128 KB 128 KY 128 PI 8 PJ 8"),
-        ("float16", "MJ0 768 MJ1 768 JZ 1536 IDF 128 SBF 144 LB 144 LY 144"),
+        ("bfloat16", "C0 2064 C1 2064 C2 2064 C3 2064 OHN 768 CG0 768 CG1 768 VS 768 OUT 6912 SG0 768 SG1 768 VF 768 VN 768 OH 6912 "
+         "LTA 384 LF 384 Y0W 64 Y0R 768 YI0 64 YI1 64 ET 32 IDB 128 SBB 144 GE 128 IR 512 ONE 128 PAT 512 PB 8 "
+         "F0 432 F1 432 FC0 432 FC1 432 ZZ0 432 ZZ1 432 H0 480 H1 480 DL 96 NE 48 CN 48 T16 48 Y1W 48 "
+         "NIB 128 P1K 128 N1K 128 P2K 128 N2K 128 M384 128 P256 128 M48 128 I32 128 N2 128 N3 128 P2 128 P3 128"),
+        ("int32", "JW 10240 STI 96 KM 1040 KB 128 KY 128 PI 8 PJ 8"),
+        ("float16", "JH 8192 MJ0 768 MJ1 768 JZ 1536 IDF 128 SBF 144 LB 144 LY 144 JC 48"),
         ("uint16", "STU 96 OFJ 48 OC0 48 OC1 48 LU 384 Y0U 48 SEL 48 KO 8"),
-        ("float32", "KM 1040 TC0 48 TC1 48 PC 8 PK 8 V8 8 V8A 8 V8B 8 XR 32 JR 48 IV 128"),
+        ("float32", "TC0 48 TC1 48 PC 8 PK 8 V8 8 V8A 8 V8B 8 XR 32 JR 48 IV 128"),
         ("psum", "X 512 AD 1024 KA 512 KBK 512 KEY 1024 MS 512")):
     _p = _s.split()
     for _n, _w in zip(_p[::2], _p[1::2]):
         SCRATCH[_n] = ("psum", [128, int(_w)], "float32") if _ty == "psum" else ("sbuf", [128, int(_w)], _ty)
 
-SEMAPHORES = "qv qs qp qg dJA dJB dC dSt dY dW dLo dLr dO lo rJ rC rL rF fC2 fJ3 fC3".split()
-SEMAPHORES += ["%s%d" % (a, d) for a in ("aJ", "aC", "aL", "aF") for d in (1, 2, 3)]
+SEMAPHORES = "qv qs qp qg dJa dJb dC dSt dY dW dLo dLr dO dB dB0 lc dL3 dLq aW2 aW3 lo rF1 rF3 aF1 aF2 aF30 aF31".split()
+SEMAPHORES += ["%s%d" % (a, d) for a in ("aC", "aL") for d in (1, 2, 3)] + ["aJ%d%d" % (d, i) for d in (1, 2, 3) for i in range(4)]
+SEMAPHORES += ["h%d" % k for k in range(1, 9)]
 
 WORLD = 256
-JAT = {0: ("JA", 0), 1: ("JA", 4096), 2: ("JB", 0), 3: ("JB", 4096)}
-SCALED = (("NIB", -1), ("N2K", -2048), ("P1K", 1024), ("N1K", -1024), ("M384", -384), ("I32", 32768), ("P2K", 2048), ("P256", 256), ("M48", -48))
+SCALED = {"NIB": -1, "N2K": -2048, "P1K": 1024, "N1K": -1024, "M384": -384, "I32": 32768,
+          "P2K": 2048, "P256": 256, "M48": -48}
+TO_SAME = ("IDB", "NIB", "N2", "N3")
+FROM_SAME = ("NIB", "IDB", "P2", "P3")
+_RA = [[("H", 1, "o")], [("H", 2, "o", 1)], [("C", 1, "a"), ("H", 3, "b", 2)], [("C", 2, "a"), ("C", 3, "b", 3)]]
+_RB = [[("H", 1, "o")], [("H", 2, "o")], [("C", 1, "a"), ("H", 3, "b", 2)], [("C", 2, "a"), ("C", 3, "b", 3)]]
+_R4 = [[("H", 1, "o")], [("H", 2, "a"), ("H", 3, "b", 1)], [("C", 1, "o")], [("C", 2, "a"), ("C", 3, "b", 3)]]
+CFG = {"give": ["H0", "H1", "C"], "relay": [_R4, _R4], "wide": (1, 2, 3), "bc": 5, "f": 1.25, "g": 1.56, "wake": 0.1, "bias": 2.0,
+       "margin": 0.3, "late": [], "halves": 0, "lc": 0, "dlast": range(9), "tail": 3, "cut": (0, 512, 1024, 1536, 2048), "hl": (), "own": 0, "early": 0, "le": 1, "lsplit": 0, "qat": 0.5, "loads": "3LQYSabO",
+       "eng": dict({m: "s" for m in "N2K NIB P1K N1K Y0U ID1 ID2".split()}, JZ0="g"),
+       "want": {-2: "IV|PI|V8|XR|ID0|Cz0 Cz1 Cz2 Cz3|IDB|PC|N2K NIB P1K N1K|SBB|ET GE SBF IDF|ID2 ID1|"
+                    "H0_0 T16 ONE CN PB M384 I32 PK LB LY H1_0|LU0|F0_1|FC0_1|OH1_0|OHN0 OHN1|STU|M0_0",
+                -1: "OH1_1|OH2_0 OH2_1|JR IR JZ0|J1_0|J2_0 J2_1 J2_2 J2_3|J3_0 J3_1 J3_2 J3_3|PAT KM0 KM1 KMz",
+                (0, "x"): "ID3", (1, "x"): "JZ1_0", (2, "j"): "LU1|OH3_0 OH3_1|J1_1", (2, "x"): "JZ1_1|ZZ0_3|F0_3 F0_5 F0_7",
+                2: "ZZ0_5 ZZ0_7|FC0_3|KEY0 KEY1|J1_2 J1_3|OH4_0 OH4_1",
+                (3, "c"): "OH5_0 OH5_1 OH5_2", 3: "OH5_3 OH5_4 OH5_5 OH5_6 OH5_7", (4, "c"): "OH5_8 OH5_9 OH5_10",
+                4: "OH5_11 OH5_12 OH5_13 OH5_14 OH5_15", 5: "JC Y0U", (8, "a"): "OH0_0", (8, "b"): "OH0_1",
+                (8, "v"): "KO"},
+       "want1": {(-1, "x"): "F1_1", 0: "FC1_1|ZZ1_3 ZZ1_5 ZZ1_7", (0, "x"): "KY|P2K|LY", (1, "j"): "P256 M48"},
+       "vsign": [], "ohq": {}, "siq": "vv", "gap2": 0,
+       "end": ["C70 C71 n5 w0 J8 X8 c60 a70 s60 c61 a71 s61 j5 O8 C80 n6 c70 c71 v70 v71 j6 a80 g8",
+               "C70 C71 n5 l1 J8 X8 c60 a70 s60 c61 a71 s61 j5 O8 C80 n6 b1 c70 c71 v70 s71 j6 a80 g8"],
+       "wq": {1: "gsvv", 2: "gggg", 3: "gggg"}, "nq": "vsss",
+       "at": {"LTS": 2.2, "LTA0": 2.9, "Y0R": 3.0, "STI": 3.3, "J0_0": 4.4, "J0_1": 5.4, "Y0W": 5.6, "C0_0": 7.4, "C0_1": 7.4,
+              "LTA1": 10.7, "LTA2": 12.0, "LTA3": 12.0, "T1": 13.0, "C1": 17.0, "T2": 16.0, "C2": 19.5, "T3": 19.0, "C3": 22.5}}
 
 
-def routes(topo, cores, r):
+def helpers(topo, cores, r):
     c, n = cores[r], len(cores)
     own = [e for e in topo.cores_of(c) if e != c and topo.may_write(e, cores[(r - 1) % n])]
     same = [e for e in own if topo.die(e) == topo.die(c)]
@@ -35,66 +60,192 @@ def routes(topo, cores, r):
 
 
 def piece(T, w, d, i, half=None):
-    nm, a = JAT[d] if w == "J" else ("C%d" % d, 0)
+    nm, a = {"J": ("JW", 2048 + 2048 * d if d else 0), "H": ("JH", 2048 * d), "C": ("C%d" % d, 16)}[w]
+    if w != "C":
+        return T[nm][:, a + CFG["cut"][i]:a + CFG["cut"][i + 1]]
     a += 512 * i + 256 * (half or 0)
     return T[nm][:, a:a + (512 if half is None else 256)]
+
+
+def plan(topo, T):
+    cores, n = T.cores, len(T.cores)
+    calls, total, marks = {}, {}, {}
+
+    def item(dst, eng, i, o, sem=None):
+        if sem is None:
+            marks[dst] = marks.get(dst, 0) + 1
+            sem = "h%d" % marks[dst]
+        total[dst, sem] = total.get((dst, sem), 0) + len(eng) * (len(o) if isinstance(o, list) else 1)
+        return (dst, eng, i, o, sem)
+
+    def call(core, turn, waits, items):
+        calls.setdefault(core, []).append((turn, waits, items))
+
+    H = [helpers(topo, cores, r) for r in range(n)]
+    for r in range(n):
+        c, relays = cores[r], H[r][0]
+        x = [cores[(r - d) % n] for d in range(n)]
+        gates = [H[(r - d) % n][1] for d in range(n)]
+        on, off = topo.engines(c, relays[0]), topo.engines(c, x[2])
+        E = {"a": off[0:4], "b": off[4:8], "o": off}
+
+        def send(i, w, d, eng, turn=None, half=None):
+            sem = "aC%d" % d if w == "C" else "aJ%d%d" % (d, i)
+            src, dst = piece(T, w, 0, i, half), piece(T, w, d, i, half)
+            if turn is None:
+                return item(x[d], E[eng], src, dst, sem)
+            it = item(gates[d][i], E[eng], src, dst)
+            call(gates[d][i], turn, [it[4]], [item(x[d], off, dst, dst, sem)])
+            return it
+
+        carriers = relays + gates[3][0:2]
+        order = [e for e in on if e not in off] + off
+        m = CFG["le"]
+        its = [item(e, order[m * i:m * i + m] if i < 4 else off[m * (i - 4):m * (i - 3)], T.LTD[i], T.LTD[0]) for i, e in enumerate(carriers)]
+        if CFG["lsplit"]:
+            call(c, 0, ["LTS"], its[0:4])
+            call(c, CFG["lsplit"], ["LT3"], its[4:6])
+        else:
+            call(c, 0, ["LTS", "LT3"], its)
+        for i, e in enumerate(carriers):
+            call(e, 0, [its[i][4]], [item(x[i // 2 + 1], off, T.LTD[0], T.LTA[:, 96 + 48 * i:144 + 48 * i], "aL%d" % (i // 2 + 1))])
+        if CFG["bc"] < 9:
+            it = item(gates[3][0], E["b"], T.LTP[1], T.LTP[1])
+            call(c, CFG["qat"], ["LTQ"], [item(x[2], E["a"], T.LTP[0], T.LTR[0], "aW2"), it])
+            call(gates[3][0], 0.5, [it[4]], [item(x[3], off, T.LTP[1], T.LTR[1], "aW3")])
+        got = {}
+        if CFG["halves"]:
+            def two(w, d, h):
+                nm, a = {"H": ("JH", 2048 * d), "C": ("C%d" % d, 16)}[w]
+                return T[nm][:, a + 1024 * h:a + 1024 * h + 1024]
+            its = [item(relays[h], on, two("H", 0, h), two("H", 0, h)) for h in range(2)]
+            its += [item(relays[2 + h], on[8 * h:8 * h + 8], two("C", 0, h), two("C", 0, h)) for h in range(2)]
+            call(c, 1, ["N0_0"], its[0:1])
+            call(c, 2, ["N0_1"], its[1:2])
+            call(c, 3, ["C0_0"], its[2:4])
+            for i, e in enumerate(relays):
+                w, h = "HC"[i // 2], i % 2
+                for turn, step in enumerate(CFG["halves"][i // 2]):
+                    out = []
+                    for d, eng, gate, at in step:
+                        sem = "aC%d" % d if w == "C" else "aJ%d%d" % (d, h)
+                        if gate is None:
+                            out.append(item(x[d], E[eng], two(w, 0, h), two(w, d, h), sem))
+                        else:
+                            y = gates[d][2 * gate + h]
+                            out.append(item(y, E[eng], two(w, 0, h), two(w, d, h)))
+                            call(y, at, [out[-1][4]], [item(x[d], off, two(w, d, h), two(w, d, h), sem)])
+                    call(e, 1 + turn, [] if turn else [its[i][4]], out)
+        for turn, w in enumerate([] if CFG["halves"] else CFG["give"]):
+            ii = range(4) if len(w) == 1 else [2 * int(w[1]), 2 * int(w[1]) + 1]
+            m = len(on) // len(ii)
+            for k, i in enumerate(ii):
+                got[w[0], i] = item(relays[i], on[m * k:m * k + m], piece(T, w[0], 0, i), piece(T, w[0], 0, i))
+            call(c, 1 + turn, sorted(set("%s0_%d" % (w[0].replace("H", "N"), i // 2) for i in ii)), [got[w[0], i] for i in ii])
+        for i, e in enumerate([] if CFG["halves"] else relays):
+            seen = set()
+            for turn, step in enumerate(CFG["relay"][i // 2]):
+                call(e, 1 + turn, [got[w, i][4] for w in sorted(set(s[0] for s in step) - seen)], [send(i, *s) for s in step])
+                seen |= set(s[0] for s in step)
+        total[relays[2], "rF1"] = 16
+        call(relays[2], 98, ["rF1"], [item(x[3], off[4 * l:4 * l + 4], T.RET[l], T.RET[l], "aF1") for l in range(2)])
+        for l in range(2):
+            total[relays[2 * l], "rF3"] = 8
+            call(relays[2 * l], 99, ["rF3"], [item(x[1], off, T.RET[4 + l], T.RET[4 + l], "aF3%d" % l)])
+    for c in calls:
+        calls[c].sort(key=lambda x: x[0])
+    return calls, total
 
 
 def transfers(topo, T, core, items):
     tr = []
     for c, e, i, o, s in items:
         rid, pid = topo.addr(c, core)
-        tr.append(RemoteDMATransfer(dst_ids=[DstId(rid=rid, pnc=pid)], dma_engine_mask=sum(1 << b for b in e), remote_sem=T.sem[s], src=i, dst=o))
+        srcs, dsts = i if isinstance(i, list) else [i], o if isinstance(o, list) else [o]
+        tr.append(RemoteDMATransfer(dst_ids=[DstId(rid=rid, pnc=pid) for _ in dsts], dma_engine_mask=sum(1 << b for b in e),
+                                    remote_sem=T.sem[s], srcs=srcs, dsts=dsts, alu_op=2 if len(srcs) > 1 else 0))
     return tr
 
 
 def hand_on(g, core, T, topo):
-    cores, n = T.cores, len(T.cores)
-    lo = [0]
-
-    def fused(items):
+    if not any(core in h for r in range(len(T.cores)) for h in helpers(topo, T.cores, r)):
+        return
+    calls, total = plan(topo, T)
+    lo = 0
+    for _, waits, items in calls.get(core, []):
+        for s in waits:
+            g.wait_ge(T.sem[s], total[core, s])
         g.remote_dma_fused(transfers(topo, T, core, items), local_sem=T.sem.lo)
-        lo[0] += sum(len(it[1]) for it in items)
+        lo += sum(len(it[1]) for it in items)
+    if lo:
+        g.wait_ge(T.sem.lo, lo)
 
-    def send(dst, out, in_, sem):
-        fused([(dst, topo.engines(core, dst), in_, out, sem)])
 
-    for r in range(n):
-        relays, gates = routes(topo, cores, r)
-        x = [cores[(r - d) % n] for d in range(n)]
-        into = [routes(topo, cores, (r - d) % n)[1] for d in range(n)]
-        carriers = relays + into[3][0:2]
-        if core in carriers:
-            i = carriers.index(core)
-            g.wait_ge(T.sem.rL, 2)
-            send(x[i // 2 + 1], T.LTA[:, 96 + 48 * i:144 + 48 * i], T.LTD[0], "aL%d" % (i // 2 + 1))
-    for r in range(n):
-        relays, gates = routes(topo, cores, r)
-        x = [cores[(r - d) % n] for d in range(n)]
-        into = [routes(topo, cores, (r - d) % n)[1] for d in range(n)]
-        if core in relays:
-            i = relays.index(core)
-            off = topo.engines(core, x[1])
-            a, b = off[0:4], off[4:8]
-            J, C = piece(T, "J", 0, i), piece(T, "C", 0, i)
-            g.wait_ge(T.sem.rJ, 8)
-            send(x[1], piece(T, "J", 1, i), J, "aJ1")
-            fused([(into[3][i], b, piece(T, "J", 0, i, 0), piece(T, "J", 3, i, 0), "fJ3")])
-            g.wait_ge(T.sem.rC, 4)
-            fused([(x[1], a, C, piece(T, "C", 1, i), "aC1"), (into[2][i], b, C, piece(T, "C", 2, i), "fC2")])
-            fused([(x[2], a, J, piece(T, "J", 2, i), "aJ2")])
-            fused([(x[3], a, piece(T, "J", 0, i, 1), piece(T, "J", 3, i, 1), "aJ3"), (into[3][i], b, C, piece(T, "C", 3, i), "fC3")])
-            if i in (0, 2):
-                d = 3 if i == 0 else 1
-                g.wait_ge(T.sem.rF, 16)
-                fused([(cores[(r + d) % n], off[4 * l:4 * l + 4], T.RET[2 * d - 2 + l], T.RET[2 * d - 2 + l], "aF%d" % d) for l in range(2)])
-        if core in gates:
-            i = gates.index(core)
-            for w, d, h in (("J", 3, 0), ("C", 2, None), ("C", 3, None)):
-                g.wait_ge(T.sem["f%s%d" % (w, d)], 4)
-                send(x[0], piece(T, w, d, i, h), piece(T, w, d, i, h), "a%s%d" % (w, d))
-    if lo[0]:
-        g.wait_ge(T.sem.lo, lo[0])
+def arrange(jobs, at):
+    wake = CFG["wake"]
+    last, seen, pred, succ = {}, {}, [], [[] for _ in jobs]
+    for i, (ch, reads, writes, tail) in enumerate(jobs):
+        p = set(last[r] for r in reads if r in last)
+        for w in writes:
+            p |= set(seen.get(w, [])) | ({last[w]} if w in last else set())
+        p.discard(i)
+        pred.append(p)
+        for j in p:
+            succ[j].append(i)
+        for r in reads:
+            seen.setdefault(r, []).append(i)
+        for w in writes:
+            last[w], seen[w] = i, []
+    way = [0.0] * len(jobs)
+    for i in range(len(jobs) - 1, -1, -1):
+        way[i] = jobs[i][0][0][1] + max([jobs[i][3]] + [wake + way[j] for j in succ[i]])
+    head = [max([at.get(r, 0.0) for r in j[1]] + [0.0]) for j in jobs]
+    tail = [j[3] for j in jobs]
+
+    def place(order, before, free):
+        busy, start, end, took, front = {}, {}, {}, {}, {}
+        for i in order:
+            best = None
+            for c, (q, dur, emit) in enumerate(jobs[i][0]):
+                t = max([free[i]] + [end[j] + (0.0 if q == took[j][0] and q in "py" else 2.0 if "y" in (q, took[j][0]) else wake) for j in before[i]])
+                if tail[i] >= 0:
+                    t = max(t, front.get(q, 0.0))
+                ready = t
+                for a, b in busy.get(q, []):
+                    if t + dur <= a and (tail[i] >= 0 or ready + dur + CFG["margin"] <= a):
+                        break
+                    t = max(t, b)
+                worth = t + dur + (CFG["bias"] * dur if q == "v" else 0.0)
+                if best is None or worth < best[0]:
+                    best = (worth, t, c)
+            q, dur, emit = took[i] = jobs[i][0][best[2]]
+            start[i], end[i] = best[1], best[1] + dur
+            if tail[i] >= 0:
+                front[q] = end[i]
+            busy.setdefault(q, []).append((start[i], end[i]))
+            busy[q].sort()
+        return start, end, took
+
+    every = range(len(jobs))
+    order, taken = [], set()
+
+    def take(i):
+        if i not in taken:
+            taken.add(i)
+            for j in sorted(pred[i]):
+                take(j)
+            order.append(i)
+
+    for i in every:
+        if tail[i] >= 0:
+            take(i)
+    for i in every:
+        take(i)
+    out = []
+    for i in order:
+        q = [CFG["eng"][w] for w in jobs[i][2] if w in CFG["eng"]]
+        out.append([c for c in jobs[i][0] if not q or len(jobs[i][0]) == 1 or c[0] == q[0]][0][2])
+    return out
 
 
 def rank_program(g, core, T, topo):
@@ -103,13 +254,13 @@ def rank_program(g, core, T, topo):
         hand_on(g, core, T, topo)
         return
     cores, n = T.cores, len(T.cores)
-    relays = routes(topo, cores, rank)[0]
-    carriers = relays + routes(topo, cores, (rank - 3) % n)[1][0:2]
+    relays = helpers(topo, cores, rank)[0]
+    calls, arrive = plan(topo, T)
     Q = {"v": g.vector, "s": g.scalar, "p": g.tensor, "g": g, "y": g.sync}
     SEM = {"v": "qv", "s": "qs", "p": "qp", "g": "qg"}
     cnt = {q: 0 for q in SEM}
     clock = {q: {} for q in Q}
-    lastw, readers = {}, {}
+    lastw, readers, jobs, lo = {}, {}, [], [0]
 
     def need(q, toks):
         best = {}
@@ -133,63 +284,106 @@ def rank_program(g, core, T, topo):
             out += readers.get(w, [])
         return out
 
-    def done(tok, reads, writes):
+    def done(q, sem, count, reads, writes):
+        c = dict(clock[q])
+        c[sem] = count
         for r in reads:
-            readers.setdefault(r, []).append(tok)
+            readers.setdefault(r, []).append((sem, count, c))
         for w in writes:
-            lastw[w] = tok
+            lastw[w] = (sem, count, c)
             readers[w] = []
 
-    def op(q, call, reads, writes):
+    def issue(q, call, reads, writes):
         need(q, deps(q, reads, writes))
         cnt[q] += 1
         call().then_inc(T.sem[SEM[q]], 1)
-        c = dict(clock[q])
-        c[SEM[q]] = cnt[q]
-        done((SEM[q], cnt[q], c), reads, writes)
-
-    def pe(items, writes, start=True, stop=True):
-        allr = []
-        for i, (o, l, r, rd) in enumerate(items):
-            need("p", deps("p", rd, writes if i == 0 else []))
-            allr += rd
-            ins = g.tensor.matmul(o, l, r, start and i == 0, stop and i == len(items) - 1)
-        cnt["p"] += 1
-        ins.then_inc(T.sem.qp, 1)
-        c = dict(clock["p"])
-        c["qp"] = cnt["p"]
-        done(("qp", cnt["p"], c), allr, writes)
-
-    def lin(o, terms):
-        return [(o, T[m][:], x, [m] + rd) for m, x, rd in terms]
+        done(q, SEM[q], cnt[q], reads, writes)
 
     def dma(q, out, in_, sem, total, reads, writes):
         need(q, [t for t in deps(q, reads, writes) if t and t[0] != sem])
         Q[q].dma_start(out, in_).then_inc(T.sem[sem], 16)
-        c = dict(clock[q])
-        c[sem] = total
-        done((sem, total, c), reads, writes)
+        done(q, sem, total, reads, writes)
 
-    def ts(out, in0, a, b, o0, o1, reads, writes):
+    CY = 0.00083 * CFG["f"]
+
+    def lasts(q, out, m):
+        k = 1
+        for x in out.shape[1:]:
+            k *= x
+        if q == "g":
+            return 0.17 * CFG["f"] + 2 * k * CY
+        if m == "g":
+            return (60 if q == "v" else 78) * CY + k * CFG["g"] * CY
+        return 30 * CY + max(64, k * (m if q == "v" else 1)) * CY
+
+    def put(choices, reads, writes, tail=0.0):
+        jobs.append(([(q, lasts(q, o, m), lambda q=q, c=c: issue(q, c, reads, writes)) for q, o, m, c in choices], reads, writes, lazy[0]))
+
+    lazy = [-1.0]
+
+    def want(keys):
+        for part in keys.split("|"):
+            jobs.append(([("w", 0.0, lambda: None)], part.split(), [], 0.0))
+
+    def TS(out, in0, a, b, o0, o1=None, m=1):
         if o1 is None:
-            op("v", lambda: g.vector.tensor_scalar(out, in0, a, None, o0), reads, writes)
-        else:
-            op("v", lambda: g.vector.tensor_scalar(out, in0, a, b, o0, o1), reads, writes)
+            return ("v", out, m, lambda: g.vector.tensor_scalar(out, in0, a, None, o0))
+        return ("v", out, m, lambda: g.vector.tensor_scalar(out, in0, a, b, o0, o1))
 
-    def tt(out, a, b, o, reads, writes):
-        op("v", lambda: g.vector.tensor_tensor(out, a, b, o), reads, writes)
+    def ACT(out, in_, func, bias=0.0, scale=1.0, m=1):
+        return ("s", out, m, lambda: g.scalar.activation(out, in_, func, bias=bias, scale=scale))
 
-    def cp(out, a, reads, writes):
-        op("v", lambda: g.vector.tensor_copy(out, a), reads, writes)
+    def IOTA(out, pattern, base, ch=0):
+        return ("g", out, 2, lambda: g.iota(out, pattern, base, ch, allow_small_or_imprecise_dtypes=True))
+
+    def ts(out, in0, a, b, o0, o1, reads, writes, m=1):
+        put([TS(out, in0, a, b, o0, o1, m)], reads, writes)
+
+    def tt(out, a, b, o, reads, writes, m=1):
+        put([("v", out, m, lambda: g.vector.tensor_tensor(out, a, b, o))], reads, writes)
 
     def fill(ap, val, writes):
-        op("v", lambda: g.vector.memset(ap, val), [], writes)
+        put([("v", ap, 0.5, lambda: g.vector.memset(ap, val))], [], writes)
 
-    def act(out, in_, func, reads, writes, bias=0.0, scale=1.0):
-        op("s", lambda: g.scalar.activation(out, in_, func, bias=bias, scale=scale), reads, writes)
+    def act(out, in_, func, reads, writes, bias=0.0, scale=1.0, m=1):
+        put([ACT(out, in_, func, bias, scale, m)], reads, writes)
+
+    def cp(out, a, reads, writes, qs="v", m=1):
+        ch = {"v": ("v", out, m, lambda: g.vector.tensor_copy(out, a)), "s": ACT(out, a, F.Copy, m=m),
+              "g": ("g", out, 2, lambda: g.affine_select(out, a, [[0, out.shape[1]]], A.is_ge, 0.0, 0, 0))}
+        put([ch[q] for q in qs], reads, writes)
 
     def iota(out, pattern, base, ch, writes):
-        op("g", lambda: g.iota(out, pattern, base, ch, allow_small_or_imprecise_dtypes=True), [], writes)
+        put([IOTA(out, pattern, base, ch)], [], writes)
+
+    def pe(items, writes, start=True, stop=True, maybe=None):
+        reads = [r for it in items for r in it[3]] + (["T16"] if maybe else [])
+
+        def emit():
+            its = items[0:1] + (maybe() if maybe else []) + items[1:]
+            for i, (o, l, r, rd) in enumerate(its):
+                need("p", deps("p", rd, writes if i == 0 else []))
+                ins = g.tensor.matmul(o, l, r, start and i == 0, stop and i == len(its) - 1)
+            cnt["p"] += 1
+            ins.then_inc(T.sem.qp, 1)
+            done("p", "qp", cnt["p"], reads, writes)
+        jobs.append(([("p", sum(max(min(64, l.shape[1]), r.shape[1]) for _, l, r, _ in items) * CY / 2, emit)], reads, writes, lazy[0]))
+
+    def lin(o, terms):
+        return [(o, T[m][:], x, [m] + rd) for m, x, rd in terms]
+
+    def fused(items, reads, tail, dur=0.4):
+        def emit():
+            need("g", deps("g", reads, []))
+            if "C0_0" in reads:
+                g.remote_dma_fused(transfers(topo, T, core, items), local_sem=T.sem.lc)
+                return
+            g.remote_dma_fused(transfers(topo, T, core, items), local_sem=T.sem.lo)
+            lo[0] += sum(len(it[1]) for it in items)
+        jobs.append(([("g", dur, emit)], reads, [], tail))
+
+    def later(out, in_, sem, total, reads, writes, tail=0.0):
+        jobs.append(([("y", 0.06, lambda: dma("y", out, in_, sem, total, reads, writes))], reads, writes + [sem], tail))
 
     def blk(name, k, m=1):
         return T[name][:, 48 * k:48 * (k + m)]
@@ -197,155 +391,183 @@ def rank_program(g, core, T, topo):
     def ks(name, r):
         return ["%s%d" % (name, k) for k in r]
 
-    dma("y", T.STI[:], T.st[:], "dSt", 16, [], ["STI"])
-    dma("s", T.Y0R[0:8, :], T.y0[:], "dY", 16, [], ["Y0R"])
+    def arrived(key, sem, count=None):
+        k = count or arrive[core, sem]
+        lastw[key] = (sem, k, {sem: k})
+
+    J0, C0 = ["J0_0", "J0_1"], ["C0_0", "C0_1"]
+    at = dict(CFG["at"])
     for d in range(1, n):
         s = (rank - d) % n
         for l in range(2):
             a = (s * 2 + l) * 768
-            dma("sy"[l], T.LTD[2 * d - 2 + l], T.lt[:, a:a + 768], "dLr", 96, [], ["LTS"])
-    for l in range(2):
-        a = (rank * 2 + l) * 768
-        dma("sy"[l], blk("LTA", l), T.lt[:, a:a + 768], "dLo", 32, [], ["LTA0"])
-    dma("s", T.JA[:, 0:1024], T.jm[:, 0:1024], "dJA", 16, [], ["J0a"])
-    dma("y", T.JA[:, 1024:2048], T.jm[:, 1024:2048], "dJB", 16, [], ["J0b"])
-    dma("s", T.C0[:, 0:2048], T.cf[:], "dC", 16, [], ["C0"])
+            if d < 3:
+                dma("sy"[l], T.LTD[2 * d - 2 + l], T.lt[:, a:a + 768], "dLr", 64, [], ["LTS"])
+    for w in CFG["loads"]:
+        if w == "3":
+            for l in range(2):
+                a = ((rank - 3) % n * 2 + l) * 768
+                dma("sy"[l], T.LTD[4 + l], T.lt[:, a:a + 768], "dL3", 32, [], ["LT3"])
+        if w == "O":
+            for p in range(16 if CFG["own"] else 0):
+                dma("sy"[p % 2], T.LW[p:128:16, 4:6], T.lt[:, rank * 1536:rank * 1536 + 1536], "dB0", 256, [], ["LW2_%d" % p])
+        if w == "Q" and CFG["bc"] < 9:
+            for j in range(2):
+                a = (rank - 2 - j) % n * 1536
+                dma("sy"[j], T.LTP[j], T.lt[:, a:a + 1536], "dLq", 32, [], ["LTQ"])
+        if w == "L":
+            for l in range(2):
+                a = (rank * 2 + l) * 768
+                dma("sy"[l], blk("LTA", l), T.lt[:, a:a + 768], "dLo", 32, [], ["LTA0"])
+        if w == "Y":
+            dma("s", T.Y0R[0:8, :], T.y0[:], "dY", 16, [], ["Y0R"])
+        if w == "S":
+            dma("y", T.STI[:], T.st[:], "dSt", 16, [], ["STI"])
+        if w == "a":
+            dma("s", T.JW[:, 0:CFG["cut"][2]], T.jm[:, 0:CFG["cut"][2]], "dJa", 16, [], ["J0_0"])
+        if w == "b":
+            dma("y", T.JW[:, CFG["cut"][2]:2048], T.jm[:, CFG["cut"][2]:2048], "dJb", 16, [], ["J0_1"])
     dma("y", T.Y0W[:, 0:48], T.y0[:], "dW", 16, [], ["Y0W"])
+    dma("y", T.C0[:, 16:2064], T.cf[:], "dC", 16, ["J0_0"], C0)
     for d in range(1, n):
-        for a, w, k in (("aJ", "J", (32, 16, 48)[d - 1]), ("aC", "C", (16, 32, 32)[d - 1]), ("aL", "LTA", 16)):
-            nm = "%s%d" % (a, d)
-            lastw["%s%d" % (w, d)] = (nm, k, {nm: k})
+        arrived("C%d" % d, "aC%d" % d)
+        arrived("LTA%d" % d, "aL%d" % d)
+        for i in range(4):
+            key = ("N%d_%d" if d in CFG["wide"] and CFG["wq"][d][i] != "-" else "J%d_%d") % (d, i)
+            arrived(key, "aJ%d%d" % (d, i // 2 if CFG["halves"] else i))
+            at[key] = at["T%d" % d] + 0.3 * i
+    for j in range(2 if CFG["bc"] < 9 else 0):
+        arrived("LTR%d" % j, "aW%d" % (j + 2))
+        if j == 0 and CFG["lc"]:
+            g.sync.wait_ge(T.sem.lc, 16)
+        for p in range(16):
+            dma("y", T.LW[p:128:16, 2 * j:2 * j + 2], T.LTR[j], "dB", 512, ["LTR%d" % j], ["LW%d_%d" % (j, p)])
 
     iota(T.PI[:, 0:1], [[0, 1]], 0, 1, ["PI"])
     iota(T.V8[:], [[-16, 8]], 0, 1, ["V8"])
     iota(T.IV[:], [[-1, 128]], 0, 1, ["IV"])
     iota(T.XR[:], [[0, 2], [1, 16]], 0, 0, ["XR"])
-    iota(T.JA[:, 2048:2560], [[1, 512]], 0, 0, ["IDA0"])
-
+    iota(T.JW[:, 2048:2560], [[1, 512]], 0, 0, ["ID0"])
+    for k in range(1, 4):
+        o, i = T.JW[:, 2048 + 512 * k:2560 + 512 * k], T.JW[:, 2048:2560]
+        put([TS(o, i, 512.0 * k, None, A.add), ACT(o, i, F.Identity, bias=512.0 * k), IOTA(o, [[1, 512]], 512 * k)], ["ID0"], ["ID%d" % k])
+    iota(T.JR[:], [[16, 48]], 0, 0, ["JR"])
+    iota(T.IR[0:1, :], [[0, 32], [-2048, 16]], 30720, 0, ["IR"])
+    iota(T.PAT[:], [[0, 512]], 0, 0, ["PAT"])
+    iota(T.PAT[:, 0:512:16], [[0, 32]], -16777215, 0, ["PAT"])
+    for b in range(2):
+        iota(T.KM[:, 512 * b:512 * b + 512], [[0, 512]], 0, 0, ["KM%d" % b])
+    iota(T.KM[:, 1024:1040], [[0, 16]], 30720, 0, ["KMz"])
     fill(T.SBB[:], 0.0, ["SBB"])
     for d in range(4):
-        fill(T["C%d" % d][:, 2048:2064], 0.0, ["Cz%d" % d])
-    fill(T.ONE[:], 1.0, ["ONE"])
+        fill(T["C%d" % d][:, 0:16], 0.0, ["Cz%d" % d])
     ts(T.PJ[:, 0:1], T.PI[:, 0:1], 15, None, A.bitwise_and, None, ["PI"], ["PJ"])
     ts(T.V8A[:], T.V8[:], -0.5, None, A.is_gt, None, ["V8"], ["V8A"])
     ts(T.V8B[:], T.V8[:], 15.5, None, A.is_lt, None, ["V8"], ["V8B"])
     cp(T.PC[:, 0:1], T.PJ[:, 0:1], ["PJ"], ["PC"])
     tt(T.SBB[:, 15:143:16], T.V8A[:], T.V8B[:], A.mult, ["V8A", "V8B"], ["SBB"])
     ts(T.IDB[:], T.IV[:], 0.0, None, A.is_equal, None, ["IV"], ["IDB"])
-    pe([(T.X[0:8, 0:128], T.SBB[:, 15:143:16], T.IDB[:], ["SBB", "IDB"])], ["X"])
-    cp(T.SBF[:], T.SBB[:], ["SBB"], ["SBF"])
     ts(T.ET[:], T.XR[:], T.PC[:, 0:1], None, A.is_equal, None, ["XR", "PC"], ["ET"])
-    cp(T.IDF[:], T.IDB[:], ["IDB"], ["IDF"])
-    act(T.GE[0:8, :], T.X[0:8, 0:128], F.Copy, ["X"], ["GE"])
-    for m, w in SCALED:
-        act(T[m][:], T.IDB[:], F.Copy, ["IDB"], [m], scale=float(w))
+    pe([(T.X[0:8, 0:128], T.SBB[:, 15:143:16], T.IDB[:], ["SBB", "IDB"])], ["X"])
+    cp(T.GE[0:8, :], T.X[0:8, 0:128], ["X"], ["GE"], "sv")
+    cp(T.SBF[:], T.SBB[:], ["SBB"], ["SBF"], "vs", 0.5)
+    cp(T.IDF[:], T.IDB[:], ["IDB"], ["IDF"], "vs", 0.5)
+    for m, w in SCALED.items():
+        put([TS(T[m][:], T.IDB[:], float(w), None, A.mult, m=0.5), ACT(T[m][:], T.IDB[:], F.Copy, scale=float(w))], ["IDB"], [m])
     for t in range(2):
         fill(T["H%d" % t][:, 0:96], -1.0, ks("H%d_" % t, (-1, 0)))
     fill(T.T16[:], -16.0, ["T16"])
+    fill(T.ONE[:], 1.0, ["ONE"])
+    cp(T.PB[:, 0:1], T.PJ[:, 0:1], ["PJ"], ["PB"])
     ts(T.PK[:, 0:1], T.PC[:, 0:1], 128.0, 15.0, A.mult, A.add, ["PC"], ["PK"])
     for m in ("LB", "LY"):
         ts(T[m][:, 0:16], T.IDB[:, 0:16], 0.0, None, A.mult, None, ["IDB"], [m])
+    ts(T.JC[:], T.JR[:], T.PC[:, 0:1], None, A.add, None, ["JR", "PC"], ["JC"])
+    fill(T.CN[:], -6.0, ["CN"])
+    ts(T.KO[:], T.JR[:, 0:8], T.PK[:, 0:1], 1024.0, A.add, A.min, ["JR", "PK"], ["KO"])
+    cp(T.Y0U[:], T.Y0W[:, 0:48], ["Y0W"], ["Y0U"], "vs")
+    cp(T.STU[:], T.STI[:], ["STI"], ["STU"], "vs")
+
+    on = topo.engines(core, relays[0])
+    off = topo.engines(core, cores[(rank + 2) % n])
+    up = [e for e in on if e not in off]
+    if CFG["wide"]:
+        for i in range(4):
+            cp(piece(T, "H", 0, i), piece(T, "J", 0, i), ["J0_%d" % (i // 2)], ["M0_%d" % i], CFG["nq"][i])
+    for d in CFG["wide"]:
+        for i in range(4):
+            if CFG["wq"][d][i] != "-":
+                cp(piece(T, "J", d, i), piece(T, "H", d, i), ["N%d_%d" % (d, i)], ["J%d_%d" % (d, i)], CFG["wq"][d][i])
 
     def sels(o, buf, rd, sb="SBF", contiguous=False):
         src = T[buf]
-        out = []
-        for h in range(16):
-            v = src[:, 48 * h:48 * h + 48] if contiguous else src[:, h:768:16]
-            out.append((o, T[sb][:, 15 - h:143 - h], v, rd + [sb]))
-        return out
+        return [(o, T[sb][:, 15 - h:143 - h], src[:, 48 * h:48 * h + 48] if contiguous else src[:, h:768:16], rd + [sb]) for h in range(16)]
 
     def tab(k):
         return (k - 1) // 2 if k > 0 else 0
 
-    def letters(a, b):
-        src, rd = T.LTA[:, 96 * a:96 * b], ks("LTA", range(a, b))
-        ts(blk("F0", 2 * a + 1, 2 * (b - a)), src, 15.5, 2048.0, A.is_gt, A.mult, rd, ks("F0_", range(2 * a + 1, 2 * b + 1)))
-        cp(T.LU[:, 96 * a:96 * b], src, rd, ks("LU", range(a, b)))
-
-    def diffs(t, a):
-        FN = "F%d" % t
-        rd = ks(FN + "_", range(2 * a, 9))
-        pe(lin(T.MS[:, 96 * a:384], [("IDB", blk(FN, 2 * a, 8 - 2 * a), rd)]) +
-           [lin(T.MS[:, 96 * d:96 * d + 96], [("IDB" if d % 2 else "NIB", blk(FN, 2 * d + 1, 2), rd)])[0] for d in range(a, 4)], ["MS"])
-
     def onehot(k):
-        off = T.Y0U[:] if k == 0 else blk("LU", k - 1)
-        act(T["OH%d" % k][:], T.ET[:].indirect(off), F.Copy, ["ET", "Y0U" if k == 0 else "LU%d" % ((k - 1) // 2)], ["OH%d" % k])
+        off, a = (T.Y0U, 0) if k == 0 else (T.LU, 48 * (k - 1))
+        for hf in range(2):
+            cp(T.OH[:, 768 * k + 384 * hf:768 * k + 384 * hf + 384], T.ET[:].indirect(off[:, a + 24 * hf:a + 24 * hf + 24]),
+               ["ET", "Y0U" if k == 0 else "LU%d" % tab(k)], ["OH%d_%d" % (k, hf)], CFG["ohq"].get((k, hf), "s"), "g")
 
-    lo = [0]
+    def onehots(a, b, at=0):
+        for h in range(16):
+            ts(T.OH[:, 768 * a + h:768 * b:16], T.LW[:, at:at + b - a, 48 * h:48 * h + 48], 15.0, T.PB[:, 0:1], A.min, A.is_equal,
+               ["PB", "LW2_15" if a < 5 else "LW1_15"], ["OH%d_%d" % (k, h) for k in range(a, b)], 0.5)
 
-    def fused(items, reads):
-        need("g", deps("g", reads, []))
-        g.remote_dma_fused(transfers(topo, T, core, items), local_sem=T.sem.lo)
-        lo[0] += sum(len(it[1]) for it in items)
-
-    on = topo.engines(core, relays[0])
-    off = topo.engines(core, cores[(rank + 2) % n])
-
-    order = [e for e in on if e not in off] + off
-    fused([(e, order[2 * i:2 * i + 2], T.LTD[i], T.LTD[0], "rL") for i, e in enumerate(carriers)], ["LTS"])
-    for a, key in ((0, "J0a"), (2, "J0b")):
-        fused([(relays[a + i], on[8 * i:8 * i + 8], piece(T, "J", 0, a + i), piece(T, "J", 0, a + i), "rJ") for i in range(2)], [key])
-    fused([(relays[i], on[4 * i:4 * i + 4], piece(T, "C", 0, i), piece(T, "C", 0, i), "rC") for i in range(4)], ["C0"])
-
-    iota(T.JR[:], [[16, 48]], 0, 0, ["JR"])
-    iota(T.IR[0:1, :], [[0, 32], [-2048, 16]], 30720, 0, ["IR"])
-    iota(T.JB[:, 2048:4096], [[1, 2048]], 0, 0, ["IDB2"])
-    iota(T.PAT[:], [[0, 512]], 0, 0, ["PAT"])
-    iota(T.PAT[:, 0:512:16], [[0, 32]], -16777215, 0, ["PAT"])
-    iota(T.KM[:, 0:1024], [[0, 1024]], 0, 0, ["KM0", "KM1"])
-    iota(T.KM[:, 1024:1040], [[0, 16]], 30720, 0, ["KMz"])
-
-    cp(T.STU[:], T.STI[:], ["STI"], ["STU"])
+    for d in range(4):
+        src = T.LTA[:, 96 * d:96 * d + 96]
+        ts(blk("F0", 2 * d + 1, 2), src, 15.5, 2048.0, A.is_gt, A.mult, ["LTA%d" % d], ks("F0_", (2 * d + 1, 2 * d + 2)), 0.5)
+        if 2 * d + 1 < CFG["bc"] and (d or not CFG["own"]):
+            cp(T.LU[:, 96 * d:96 * d + 96], src, ["LTA%d" % d], ["LU%d" % d], "vs", 0.5)
+    for k in range(3 if CFG["own"] else 1, CFG["bc"]):
+        onehot(k)
+    if CFG["own"]:
+        onehots(1, 3, 4)
+    if CFG["bc"] < 9:
+        onehots(CFG["bc"], 9, CFG["bc"] - 5)
+    onehot(0)
     for hf in range(2):
         pe([(T.AD[:, 512 * hf:512 * hf + 384], T.GE[0:8, :], T.Y0R[0:8, 384 * hf:384 * hf + 384], ["GE", "Y0R"])], ["AD%d" % hf])
-    for hf in range(2):
         ts(T.OHN[:, 384 * hf:384 * hf + 384], T.AD[:, 512 * hf:512 * hf + 384], T.PC[:, 0:1], None, A.is_equal, None,
            ["AD%d" % hf, "PC"], ["OHN%d" % hf])
-    letters(0, 1)
-    onehot(1)
-    onehot(2)
-    tt(blk("ZZ0", 1), blk("F0", 1), blk("F0", 2), A.subtract, ["F0_1", "F0_2"], ["ZZ0_1"])
-
-    def same(k):
-        ts(T.JA[:, 2048 + 512 * k:2560 + 512 * k], T.JA[:, 2048:2560], 512.0 * k, None, A.add, None, ["IDA0"], ["IDA%d" % k])
-
-    same(1)
-    same(2)
-
-    def late_constants():
-        act(T.JC[:], T.JR[:], F.Copy, ["JR"], ["JC"])
-        ts(T.KO[:], T.JR[:, 0:8], T.PK[:, 0:1], 1024.0, A.add, A.min, ["JR", "PK"], ["KO"])
-        cp(T.Y0U[:], T.Y0W[:, 0:48], ["Y0W"], ["Y0U"])
-        ts(T.JZ[:, 0:1536:2], T.OHN[:], 0.0, None, A.mult, None, ["OHN0", "OHN1"], ["JZ0"])
-
-    def start_images():
-        cp(T.JZ[:, 1:1536:2], T.JA[:, 0:2048].indirect(blk("STU", 1)), ["STU", "J0a", "J0b"], ["JZ1"])
-
-    def start_keys():
-        for b in range(2):
-            items = [(T.KEY[0:96, 512 * b:512 * b + 512], T.ONE[0:1, 0:96], T.IR[0:1, :], ["ONE", "IR"])]
-            for hp in range(4 * b, 4 * b + 4):
-                for e in range(2):
-                    a = 96 * (hp + 8 * e) + 1 - e
-                    items.append((T.KEY[0:96, 128 * hp:128 * hp + 128], T.JZ[:, a:a + 96], T.IDF[:], ["JZ0", "JZ1", "IDF"]))
-            pe(items, ["KEY%d" % b], stop=False)
+    for a, b in ((1, 3), (3, 8)):
+        ts(blk("FC0", a, b - a), blk("F0", a, b - a), -16.0, None, A.add, None, ks("F0_", range(a, b)), ks("FC0_", range(a, b)), 0.5)
+    for d in range(1, 4):
+        ts(blk("ZZ0", 2 * d + 1, 2), T.LTA[:, 96 * d:96 * d + 96], 15.5, 2048.0 * d, A.is_lt, A.mult, ["LTA%d" % d],
+           ks("ZZ0_", (2 * d + 1, 2 * d + 2)), 0.5)
+    put([TS(T.JZ[:, 0:1536:2], T.OHN[:], 0.0, None, A.mult, m=0.5),
+         ("g", T.OHN[:], 2, lambda: g.affine_select(T.JZ[:, 0:1536:2], T.OHN[:], [[0, 768]], A.is_gt, 0.0, 0, 0))], ["OHN0", "OHN1"], ["JZ0"])
+    for hf in range(2):
+        cp(T.JZ[:, 1 + 768 * hf:768 + 768 * hf:2], T.JW[:, 0:2048].indirect(T.STU[:, 48 + 24 * hf:72 + 24 * hf]), ["STU"] + J0,
+           ["JZ1_%d" % hf], CFG["siq"][hf], "g")
+    for b in range(2):
+        items = [(T.KEY[0:96, 512 * b:512 * b + 512], T.ONE[0:1, 0:96], T.IR[0:1, :], ["ONE", "IR"])]
+        for hp in range(4 * b, 4 * b + 4):
+            for e in range(2):
+                a = 96 * (hp + 8 * e) + 1 - e
+                items.append((T.KEY[0:96, 128 * hp:128 * hp + 128], T.JZ[:, a:a + 96], T.IDF[:], ["JZ0", "JZ1_0", "JZ1_1", "IDF"]))
+        pe(items, ["KEY%d" % b], stop=False)
 
     KP = ["KA", "KBK"]
-    X = T.X[:, 0:48]
+    X, W = T.X[:, 0:48], T.MS[:, 0:48]
+    total = 16 * 11
 
     def jwin(d):
-        nm, a = JAT[d]
-        a = a // 2
-        rd = ["J0a", "J0b"] if d == 0 else ["J%d" % d]
-        return T[nm][:, a:a + 4096], rd + (ks("IDA", range(4)) if d < 2 else ["IDB2"])
+        rd = ks("ID", range(4))
+        if d == 0:
+            return T.JW[:, 0:4096], rd + J0
+        return T.JW[:, 2048:4096 + 2048 * d], rd + ["J%d_%d" % (e, i) for e in range(1, d + 1) for i in range(4)]
 
     def unfold(o, m):
         return [(o, T[m][0:96, 8 - 8 * e:136 - 8 * e], T.IDF[0:96, e:96:2], [m, "IDF"]) for e in range(2)]
 
-    def walk(t, gaps, vsign):
+    def walk(t, extra):
         first = 1 - t
         FN, ZN, HN = "F%d" % t, "ZZ%d" % t, "H%d" % t
+        how = {}
 
         def fk(k):
             return "%s_%d" % (FN, k)
@@ -353,247 +575,317 @@ def rank_program(g, core, T, topo):
         def hk(k):
             return "%s_%d" % (HN, k)
 
-        def vblk(k, hf):
-            if k < first:
-                return T.VS[:, 384 * hf:384 * hf + 384], "VS_%d" % hf
-            return T.OUT[:, 768 * k + 384 * hf:768 * k + 384 * hf + 384], "OUT%d_%d" % (k, hf)
+        def vblk(k, h0, h1=None):
+            a, b = 384 * h0, 384 * (h1 or h0 + 1)
+            nm, o = ("VS", 0) if k < first else ("OUT", 768 * k)
+            return T[nm][:, o + a:o + b], ["%s%d_%d" % (nm, k, hf) for hf in range(h0, h1 or h0 + 1)]
 
-        def step_j(k):
+        def images(k):
             m = "MJ%d" % (k % 2)
-            if k < first:
-                tt(T[m][:], T.JA[:, 0:2048].indirect(blk("STU", 0)), T.OHN[:], A.mult, ["STU", "OHN0", "OHN1", "J0a", "J0b"], [m])
-            else:
+            if k >= first:
                 win, rd = jwin(tab(k))
-                tt(T[m][:], win.indirect(T.OFJ[:]), T["OH%d" % k][:], A.mult, rd + ["OFJ", "OH%d" % k], [m])
+                tt(T[m][:], win.indirect(T.OFJ[:]), T.OH[:, 768 * k:768 * k + 768], A.mult, rd + ["OFJ"] + ks("OH%d_" % k, range(16)), [m], "g")
+            elif t == 0:
+                tt(T[m][:], T.JW[:, 0:2048].indirect(blk("STU", 0)), T.OHN[:], A.mult, ["STU", "OHN0", "OHN1"] + J0, [m], "g")
 
-        def step_x(k):
+        def pick(k):
             m = "MJ%d" % (k % 2)
-            items = unfold(X, "LB") if k < first and t else sels(X, m, [m], contiguous=k < first)
-            if k < 8:
-                items += lin(X, [("NIB" if tab(k + 1) % 2 else "IDB", blk(FN, k + 1), [fk(k + 1)])])
-            pe(items, ["X"])
+            if k < first and t:
+                pe(lin(X, [("N1K", blk("H0", 0), ["H0_-1"]), ("P1K", blk("H0", 9), ["H0_8"])]) + unfold(X, "LB"), ["X"])
+                return
+            pe((lin(X, [("NIB", blk(FN, 8), [fk(8)])]) if k == 8 else []) + sels(X, m, [m], contiguous=k < first), ["X"])
 
-        def step_off(k):
+        def roots(k):
             a, o = "TC%d" % (k % 2), "OC%d" % (k % 2)
-            if k < first:
-                tt(T[a][:], X, blk(FN, first), A.subtract, ["X", fk(first)], [a])
-            elif k == 8:
-                tt(T[a][:], X, blk(FN, 8), A.add, ["X", fk(8)], [a])
+            if k == 8:
+                ts(T[o][:], X, 16.0, 0.0, A.add, A.max, ["X"], [o])
+                return
+            if k < first and t:
+                cp(T.OFJ[:], X, ["X"], ["OFJ"])
             else:
-                tt(T[a][:], X, blk(ZN, k), A.add, ["X", "%s_%d" % (ZN, k)], [a])
-            if k < 8:
-                ts(T.OFJ[:], X, 2048.0 * (tab(k + 1) % 2), None, A.add, None, ["X"], ["OFJ"])
-            ts(T[o][:], T[a][:], 2048.0, None, A.min, None, [a], [o])
+                nxt = ZN if k > 1 else FN
+                tt(T.OFJ[:], X, blk(nxt, k + 1), A.add, ["X", "%s_%d" % (nxt, k + 1)], ["OFJ"])
+            if k < first and not t:
+                ts(T[o][:], X, 16.0, None, A.add, None, ["X"], [o])
+            else:
+                tt(T[o][:], X, blk("FC%d" % t, max(k, first)), A.subtract, ["X", "FC%d_%d" % (t, max(k, first))], [o])
 
-        def step_c(k, hf):
-            d, o, c = tab(k), "OC%d" % (k % 2), "VS" if k < first else "CG%d" % (k % 2)
-            act(T[c][:, 384 * hf:384 * hf + 384], T["C%d" % d][:, 0:2056].indirect(T[o][:, 24 * hf:24 * hf + 24]), F.Copy,
-                ["C%d" % d, "Cz%d" % d, o], ["%s_%d" % (c, hf)])
+        def coef(k, h0, h1):
+            d, o = tab(k), "OC%d" % (k % 2)
+            out, w = vblk(k, h0, h1) if k < first else (T["CG%d" % (k % 2)][:, 384 * h0:384 * h1], ["CG%d_%d" % (k % 2, hf) for hf in range(h0, h1)])
+            act(out, T["C%d" % d][:].indirect(T[o][:, 24 * h0:24 * h1]), F.Copy, (["C%d" % d] if d else C0) + ["Cz%d" % d, o], w, m="g")
 
         def add(k, hf):
-            if k < first:
-                return
             v, vk = vblk(k - 1, hf)
             c = "CG%d" % (k % 2)
-            pe(lin(T.AD[:, 512 * hf:512 * hf + 384], [("IDB", v, [vk]), ("IDB", T[c][:, 384 * hf:384 * hf + 384], ["%s_%d" % (c, hf)])]),
+            pe(lin(T.AD[:, 512 * hf:512 * hf + 384], [("IDB", T[c][:, 384 * hf:384 * hf + 384], ["%s_%d" % (c, hf)]), ("IDB", v, vk)]),
                ["AD%d" % hf])
 
         def cut(k, hf):
-            if k < first:
-                return
             v, vk = vblk(k, hf)
-            ts(v, T.AD[:, 512 * hf:512 * hf + 384], 255.0, -255.0, A.min, A.max, ["AD%d" % hf], [vk])
+            ts(v, T.AD[:, 512 * hf:512 * hf + 384], 255.0, -255.0, A.min, A.max, ["AD%d" % hf], vk)
 
-        how = {}
-
-        def sign(k, hf, q, src=None):
-            if k < first:
-                return
-            v, vk = src or vblk(k, hf)
+        def sign(k, h0, h1, raw=False, only="sv"):
+            v, vk = (T.AD[:, 0:384], ["AD0"]) if raw else vblk(k, h0, h1)
             s = "SG%d" % (k % 2)
-            o, w = T[s][:, 384 * hf:384 * hf + 384], ["%s_%d" % (s, hf)]
-            how[k, hf] = q
-            if q == "v":
-                ts(o, v, 0.0, 2.0, A.is_ge, A.mult, [vk], w if src is None or vk[0] != "A" else w + [vk])
+            o, w = T[s][:, 384 * h0:384 * h1], ["%s_%d" % (s, hf) for hf in range(h0, h1)]
+
+            def by(ch):
+                def call():
+                    for hf in range(h0, h1):
+                        how[k, hf] = ch[0]
+                    return ch[3]()
+                return ch[0:3] + (call,)
+            if raw:
+                put([by(ACT(o, v, F.Sign, bias=0.5))], vk, w + vk)
             else:
-                act(o, v, F.Sign, [vk], w if src is None or vk[0] != "A" else w + [vk], bias=0.5)
+                put([ch for ch in (by(ACT(o, v, F.Sign, bias=0.5)), by(TS(o, v, 0.0, 2.0, A.is_ge, A.mult, 0.5))) if ch[0] in only], vk, w)
 
         def count(k, dead=None):
-            if k < first:
-                return
             p, s = KP[k % 2], "SG%d" % (k % 2)
             o = T[p][:, 0:48]
-            items = sels(o, s, [s + "_0", s + "_1"], "SBB")
-            if how[k, 0] != how[k, 1]:
-                a = 24 * (how[k, 1] == "v")
-                items += lin(T[p][:, a:a + 24], [("IDB", T.T16[:, 0:24], ["T16"])])
-            items += lin(o, [("IDB", blk(FN, k), [fk(k)])] + (dead or [("N2K", blk(HN, k), [hk(k - 1)])]))
-            pe(items, [p])
+            dead = lin(o, dead or [("N2K", blk(HN, k), [hk(k - 1)])])
+            n1 = len(dead) if k not in CFG["dlast"] else len(dead) - 1
+            pe(lin(o, [("IDB", blk(FN, k), [fk(k)])]) + dead[:n1] + sels(o, s, [s + "_0", s + "_1"], "SBB") + dead[n1:], [p],
+               maybe=lambda: [lin(T[p][:, 24 * hf:24 * hf + 24], [("IDB", T.T16[:, 0:24], ["T16"])])[0] for hf in range(2)
+                              if how[k, hf] == "v" != how[k, 1 - hf]])
+
+        def both(k):
+            return 16.0 if how[k, 0] == how[k, 1] == "v" else 0.0
 
         def judge(k):
-            if k < first:
-                return
-            p = KP[k % 2]
-            thr = 2063.0 if how[k, 0] == how[k, 1] == "v" else 2047.0
-            act(blk(HN, k + 1), T[p][:, 0:48], F.Sign, [p], [hk(k)], bias=thr, scale=-1.0)
+            p, o = T[KP[k % 2]][:, 0:48], blk(HN, k + 1)
+            put([("s", o, 1, lambda: g.scalar.activation(o, p, F.Sign, bias=2047.0 + both(k), scale=-1.0))], [KP[k % 2]], [hk(k)])
+
+        def last(k):
+            p, o = T[KP[k % 2]][:, 0:48], blk("DL", k - 7)
+            put([("v", o, 1, lambda: g.vector.tensor_scalar(o, p, both(k) - 2049.0, 16.0, A.is_lt, A.mult))], [KP[k % 2]], ["DL%d" % k])
 
         def left(d):
-            k = 2 * d + 1
+            k, o = 2 * d + 1, T.KEY[:, 512 * (d % 2):512 * (d % 2) + 96]
             terms = [("IDB", T.LTA[:, 96 * d:96 * d + 96], ["LTA%d" % d]), ("IDB", blk(FN, k, 2), [fk(k), fk(k + 1)])]
             if d < 3:
                 terms += [("N1K", blk(HN, k, 2), [hk(k - 1), hk(k)]), ("P1K", blk(HN, k + 1, 2), [hk(k), hk(k + 1)])]
-            pe(lin(T.KEY[:, 512 * (d % 2):512 * (d % 2) + 96], terms), ["KEY%d" % (d % 2)])
+            pe(lin(o, terms), ["KEY%d" % (d % 2)])
 
         def left2(d):
-            ts(T.LF[:, 96 * d:96 * d + 96], T.KEY[:, 512 * (d % 2):512 * (d % 2) + 96], 16.0, None, A.min, None,
-               ["KEY%d" % (d % 2)], ["LF%d" % d])
+            ts(T.LF[:, 96 * d:96 * d + 96], T.KEY[:, 512 * (d % 2):512 * (d % 2) + 96], 16.0, None, A.min, None, ["KEY%d" % (d % 2)], ["LF%d" % d])
 
-        def last(k):
-            ts(blk("DL", k - 7), T[KP[k % 2]][:, 0:48], -2049.0, 16.0, A.is_lt, A.mult, [KP[k % 2]], ["DL%d" % k])
-            tt(blk("LF", k - 1), blk("LF", k - 1), blk("DL", k - 7), A.max, ["LF3", "DL%d" % k], ["LF3"])
+        def folded(l):
+            return (relays[2 * l], up, [blk("LF", 6 + l), blk("DL", l)], T.RET[4 + l], "rF3")
 
-        def goes(d):
-            if d == 2:
-                c, e, sem = cores[(rank + 2) % n], off, "aF2"
-            else:
-                c, e, sem = relays[0 if d == 3 else 2], on, "rF"
-            m = len(e) // 2
-            fused([(c, e[m * l:m * l + m], blk("LF", 2 * d + l), T.RET[2 * d - 2 + l], sem) for l in range(2)], ["LF%d" % d])
-
-        def run(key):
-            for f in gaps.get(key, []):
+        for k in range(first - 1, 8):
+            images(k)
+            for f in extra.get((k, "j"), []):
                 f()
+            hl = t in CFG["hl"]
+            if hl and k - 1 >= first:
+                add(k - 1, 0)
+            pick(k)
+            for f in extra.get((k, "x"), []):
+                f()
+            if hl:
+                if k - 2 >= first:
+                    cut(k - 2, 1)
+                if k - 1 >= first:
+                    add(k - 1, 1)
+                    cut(k - 1, 0)
+            for hf in range(0 if hl else 2):
+                if k - 2 >= first and not ((t, k) == (0, 3) and CFG["early"]):
+                    cut(k - 2, hf)
+                if k - 1 >= first:
+                    add(k - 1, hf)
+            after = []
+            if k - 2 >= first:
+                for hf in range(2):
+                    if t or (k - 2, hf) not in CFG["vsign"]:
+                        sign(k - 2, hf, hf + 1, only="s")
+                    elif hf < CFG["gap2"]:
+                        sign(k - 2, hf, hf + 1, only="v")
+                    else:
+                        after.append(hf)
+            if t and k == 1:
+                left2(3)
+            for f in extra.get((k, "c"), []):
+                f()
+            roots(k)
+            for hf in after:
+                sign(k - 2, hf, hf + 1, only="v")
+            for f in extra.get((k, "o"), []):
+                f()
+            if k - 3 >= first:
+                judge(k - 3)
+            if k < 7 and hl and k >= first:
+                coef(k, 0, 1)
+                coef(k, 1, 2)
+            elif k < 7:
+                coef(k, 0, 2)
+            if (t, k) == (0, 2) and CFG["early"]:
+                cut(1, 0)
+                cut(1, 1)
+            if first <= k - 2 < 5:
+                count(k - 2)
+            if t and k == 0:
+                left(3)
+            for f in extra.get(k, []):
+                f()
+        raw, rk = vblk(8, 1)
 
-        for k in range(first - 1, 9):
-            if k >= first or t == 0:
-                step_j(k)
-            run((k, "j"))
-            add(k - 1, 0)
-            step_x(k)
-            run((k, "x"))
-            cut(k - 2, 1)
-            add(k - 1, 1)
-            cut(k - 1, 0)
-            judge(k - 3)
-            for hf in range(2):
-                sign(k - 2, hf, "v" if (k - 2, hf) in vsign else "s")
-            if t and k in (2, 6, 8):
-                left2({2: 3, 6: 0, 8: 1}[k])
-            run((k, "c"))
-            step_off(k)
-            if t and k == 8:
-                goes(1)
-            run((k, "o"))
-            step_c(k, 0)
-            if k < 8:
-                step_c(k, 1)
-            count(k - 2)
-            if t and k in (1, 5, 7):
-                left({1: 3, 5: 0, 7: 1}[k])
-        cut(7, 1)
-        add(8, 0)
-        sign(7, 0, "s")
-        judge(6)
-        sign(7, 1, "v")
-        raw = T.CG0[:, 384:768]
-        tt(raw, T.C3[:, 0:2056].indirect(T.OC0[:, 24:48]), vblk(7, 1)[0], A.add, ["C3", "Cz3", "OC0", "OUT7_1"], ["CG0_1"])
-        S = T.MS[:, 0:48]
-        gone = [("IDB", T.JC[:], ["JC"])] + [("M384", blk(HN, k + 1), [hk(k)]) for k in range(first, 7)]
+        def back1():
+            if t:
+                left2(1)
+                fused([(relays[2], on[8 * l:8 * l + 8], blk("LF", 2 + l), T.RET[l], "rF1") for l in range(2)], ["LF1"], 0.0)
+
+        gone = [("IDF", T.JC[:], ["JC"])] + [("M384", blk(HN, k + 1), [hk(k)]) for k in range(first, 7)]
+        do = {"w": lambda k: t or pe(lin(W, [("M384", T.CN[:], ["CN"])] + gone[:-2]), ["MS"], stop=False), "J": images, "X": pick, "O": roots, "j": judge, "n": count, "b": lambda k: back1(), "l": lambda k: t and left(k), "L": left2, "i": lambda k: extra["i"][k](),
+              "g": lambda k: tt(raw, T.C3[:].indirect(T.OC0[:, 24:48]), vblk(7, 1)[0], A.add, ["C3", "Cz3", "OC0", "OUT7_1"], rk, "g")}
+        for w in CFG["end"][t].split():
+            k, hf = int(w[1]), int(w[2:3] or 0)
+            if w[0] in do:
+                do[w[0]](k)
+            elif w[0] in "sv":
+                sign(k, hf, hf + 1, only=w[0])
+            elif w[0] == "C":
+                coef(k, hf, hf + 1)
+            else:
+                {"a": add, "c": cut}[w[0]](k, hf)
         if t == 0:
+            pe(lin(W, gone[-2:]), ["MS"], start=False)
             count(7)
-            pe(lin(S, gone), ["MS"], stop=False)
             cut(8, 0)
-            sign(8, 1, "s", (raw, "CG0_1"))
+            for f in extra.get((8, "a"), []):
+                f()
+            p = T[KP[1]][:, 0:48]
+            put([("v", p, 1, lambda: g.vector.tensor_scalar(T.TC1[:], p, 2047.0 + both(7), 768.0, A.is_gt, A.mult))], [KP[1]], ["TC1", KP[1]])
+            tt(T.SEL[:], W, T.TC1[:], A.add, ["MS", "TC1"], ["SEL"])
             judge(7)
-            ts(vblk(8, 1)[0], raw, 255.0, -255.0, A.min, A.max, ["CG0_1"], ["OUT8_1"])
-            pe(lin(S, [("M384", blk(HN, 8), [hk(7)])]), ["MS"], start=False)
-            sign(8, 0, "s")
-            count(8)
         else:
             dead = [("P2K", blk(HN, 7), [hk(6)])]
+            back2 = [(cores[(rank + 2) % n], off[4 * l:4 * l + 4], blk("LF", 4 + l), T.RET[2 + l], "aF2") for l in range(2)]
+            if CFG["tail"] == 2:
+                left(2)
             count(7, dead)
-            sign(8, 0, "s", (T.AD[:, 0:384], "AD0"))
-            sign(8, 1, "v", (raw, "CG0_1"))
-            ts(vblk(8, 1)[0], raw, 255.0, -255.0, A.min, A.max, ["CG0_1"], ["OUT8_1"])
+            if CFG["tail"] == 0:
+                left(2)
+            sign(8, 0, 1, True)
+            if CFG["tail"] == 2:
+                left2(2)
+                fused(back2, ["LF2"], 0.0)
+            sign(8, 1, 2, only="v")
             last(7)
             count(8, dead + [("P256", blk("DL", 0), ["DL7"])])
+            if CFG["tail"] == 0:
+                left2(2)
+                fused(back2 + [folded(0)], ["LF2", "LF3", "DL7"], 0.0)
+            if CFG["tail"] in (1, 3):
+                left(2)
+            if CFG["tail"] == 3:
+                fused([folded(0)[0:1] + (off,) + folded(0)[2:]], ["LF3", "DL7"], 0.0)
             cut(8, 0)
-            pe(lin(S, gone + [("M384", blk(HN, 7), [hk(6)]), ("M48", blk("DL", 0), ["DL7"])]), ["MS"])
-            left(2)
+            pe(lin(W, gone + [("M384", blk(HN, 7), [hk(6)]), ("M48", blk("DL", 0), ["DL7"])]), ["MS"])
             last(8)
-            goes(3)
-        ts(T.SEL[:], S, T.PC[:, 0:1], 384.0 * (8 - first), A.add, A.add, ["MS", "PC"], ["SEL"])
-        if t:
-            left2(2)
-            goes(2)
+            if CFG["tail"] in (1, 2):
+                fused([folded(0)[0:1] + (off,) + folded(0)[2:], folded(1)], ["LF3", "DL7", "DL8"], 0.0)
+            else:
+                fused([folded(1)], ["LF3", "DL8"], 0.0)
+            if CFG["tail"] in (1, 3):
+                left2(2)
+                fused(back2, ["LF2"], 0.0)
+            ts(T.SEL[:], W, 384.0 * 8, None, A.add, None, ["MS"], ["SEL"])
         outs = ["OUT%d_%d" % (k, hf) for k in range(first, 9) for hf in range(2)]
         win = T.OUT[:, 768 * first:6912]
-        act(T.VF[:, 384:768], win.indirect(T.SEL[:, 24:48]), F.Copy, ["SEL"] + outs, ["VF1"])
-        cp(T.VF[:, 0:384], win.indirect(T.SEL[:, 0:24]), ["SEL"] + outs, ["VF0"])
-        if t == 0:
-            judge(8)
+        act(T.VF[:, 0:384], win.indirect(T.SEL[:, 0:24]), F.Copy, ["SEL"] + outs, ["VF0"], m="g")
+        ts(T.VF[:, 384:768], win.indirect(T.SEL[:, 24:48]), 255.0, -255.0, A.min, A.max, ["SEL"] + outs, ["VF1"], "g")
+        if t:
+            left(0)
+            left2(0)
+            inserted()
+            inserted2()
+        return sign, count, judge
 
-    def oh(*kk):
-        return [lambda k=k: onehot(k) for k in kk]
+    lazy[0] = 0.0
+    soon = {k: [lambda keys=keys: want(keys)] for k, keys in CFG["want"].items()}
+    for f in soon.pop(-2):
+        f()
+    for turn, keys, items in calls[core]:
+        fused(items, [k for key in keys for k in (ks("M0_", (2 * int(key[3]), 2 * int(key[3]) + 1)) if key[0] == "N" else [key])],
+              0.0, 0.4 if turn else 2.0)
+        for f in soon.pop("L", []) if turn >= (0.5 if CFG["bc"] < 9 else 0) else []:
+            f()
+    for f in soon.pop(-1):
+        f()
+    sign, count, judge = walk(0, soon)
 
-    walk(0, {(0, "x"): [lambda: same(3)], (1, "x"): [late_constants], (2, "j"): [lambda: letters(1, 4)],
-             (2, "x"): [lambda: diffs(0, 1), start_images], (2, "c"): [lambda: cp(blk("ZZ0", 2, 6), T.MS[:, 96:384], ["MS"], ks("ZZ0_", range(2, 8)))],
-             (2, "o"): oh(3, 4), (3, "o"): oh(5) + [start_keys], (4, "o"): oh(6), (5, "o"): oh(7), (6, "o"): oh(8)},
-         [(k, hf) for k in range(1, 5) for hf in range(2)])
-
-    act(blk("F1", 0), blk("H0", 9), F.Identity, ["H0_8"], ["F1_0"], bias=1024.0, scale=1024.0)
-    onehot(0)
+    sign(8, 0, 2, only="s")
+    for f in soon.get((8, "v"), []):
+        f()
     for b in range(2):
         pe([(T.KEY[0:96, 128 * hp:128 * hp + 128], T.VF[:, hp:768:8], T.I32[:], ["VF0", "VF1", "I32"]) for hp in range(4 * b, 4 * b + 4)],
            ["KEY%d" % b], start=False)
-    for b in range(2):
-        op("v", lambda b=b: g.vector.tensor_tensor_scan(T.KM[0:96, 512 * b:512 * b + 512], T.PAT[0:96, :], T.KEY[0:96, 512 * b:512 * b + 512],
-                                                       0.0, A.add, A.max), ["PAT", "KEY%d" % b], ["KM%d" % b])
+        o = T.KM[0:96, 512 * b:512 * b + 512]
+        put([("v", o, 1, lambda b=b, o=o: g.vector.tensor_tensor_scan(o, T.PAT[0:96, :], T.KEY[0:96, 512 * b:512 * b + 512], 0.0, A.add, A.max))],
+            ["PAT", "KEY%d" % b], ["KM%d" % b])
+    count(8)
+    for f in soon.get((8, "b"), []):
+        f()
+    judge(8)
+    keys, kk = T.KM[:].indirect(T.KO[:]), ["KM0", "KM1", "KMz", "KO"]
+    ts(T.KB[:], keys, 2047, None, A.bitwise_and, None, kk, ["KB"], "g")
+    cp(T.LB[:, 8:136], T.KB[:], ["KB"], ["LB"], "vs")
+    act(blk("F1", 0), blk("H0", 9), F.Identity, ["H0_8"], ["F1_0"], 1024.0, 1024.0)
+    act(blk("FC1", 0), blk("H0", 9), F.Identity, ["H0_8"], ["FC1_0"], 1008.0, 1024.0)
     S8 = range(1, 9)
+    lazy[0] = -1.0
     pe(lin(T.MS[:, 0:384], [("IDB", blk("F0", 1, 8), ks("F0_", S8)), ("N1K", blk("H0", 1, 8), ks("H0_", range(8))),
                             ("P1K", blk("H0", 2, 8), ks("H0_", S8))]), ["MS"])
-    act(blk("F1", 1, 8), T.MS[:, 0:384], F.Copy, ["MS"], ks("F1_", S8))
-    cp(T.KI[:], T.KM[:].indirect(T.KO[:]), ["KM0", "KM1", "KMz", "KO"], ["KI"])
-    ts(T.KB[:], T.KI[:], 2047, None, A.bitwise_and, None, ["KI"], ["KB"])
-    cp(T.LB[:, 8:136], T.KB[:], ["KB"], ["LB"])
+    cp(blk("F1", 1, 8), T.MS[:, 0:384], ["MS"], ks("F1_", S8), "sv")
+    lazy[0] = -1.0
+    ts(T.KY[:], keys, 11, 15, A.arith_shift_right, A.bitwise_and, kk, ["KY"], "g")
+    put([TS(T.LY[:, 8:136], T.KY[:], -1.0, 15.0, A.mult, A.add), ACT(T.LY[:, 8:136], T.KY[:], F.Identity, 15.0, -1.0)], ["KY"], ["LY"])
+    act(blk("FC1", 1, 7), blk("F1", 1, 7), F.Identity, ks("F1_", range(1, 8)), ks("FC1_", range(1, 8)), -16.0)
+    for d in range(1, 4):
+        k2 = (2 * d + 1, 2 * d + 2)
+        act(blk("ZZ1", 2 * d + 1, 2), blk("F1", 2 * d + 1, 2), F.Identity, ks("F1_", k2), ks("ZZ1_", k2), 2048.0 * d, -1.0 * d)
 
-    def newword():
-        ts(T.KY[:], T.KI[:], 11, 15, A.arith_shift_right, A.bitwise_and, ["KI"], ["KY"])
-        ts(T.LY[:, 8:136], T.KY[:], -1.0, 15.0, A.mult, A.add, ["KY"], ["LY"])
+    def letter():
+        pe(unfold(W, "LY"), ["MS"])
+        cp(T.Y1W[:], W, ["MS"], ["Y1W"], "vs")
 
-    W = T.MS[:, 0:48]
-    walk(1, {(-1, "x"): [lambda: diffs(1, 0)], (0, "j"): [lambda: act(blk("ZZ1", 0, 8), T.MS[:, 0:384], F.Copy, ["MS"], ks("ZZ1_", range(8)))],
-             (0, "x"): [newword], (1, "x"): [lambda: pe(unfold(W, "LY"), ["MS"]), lambda: act(T.Y1W[:], W, F.Copy, ["MS"], ["Y1W"])],
-             (4, "o"): [lambda: pe(lin(W, [("IDB", T.Y0W[:, 0:48], ["Y0W"]), ("IDB", blk("F1", 0), ["F1_0"]), ("P1K", blk("H1", 1), ["H1_0"])]), ["MS"])],
-             (5, "c"): [lambda: ts(T.YI0[:, 0:48], W, 1024.0, 16.0, A.add, A.min, ["MS"], ["YI0"])]}, ())
+    def inserted():
+        pe(lin(W, [("IDB", T.Y0W[:, 0:48], ["Y0W"]), ("IDB", blk("F1", 0), ["F1_0"]), ("P1K", blk("H1", 1), ["H1_0"])]), ["MS"])
+
+    def inserted2():
+        ts(T.YI0[:, 0:48], W, 1024.0, 16.0, A.add, A.min, ["MS"], ["YI0"])
+
+    lazy[0] = 0.0
+    soon = {k: [lambda keys=keys: want(keys)] for k, keys in CFG["want1"].items()}
+    soon.update({(1, "x"): [letter], "i": [inserted, inserted2]})
+    walk(1, soon)
 
     pe(lin(X, [("IDB", T.Y1W[:], ["Y1W"]), ("P1K", blk("H1", 7), ["H1_6"]), ("IDB", blk("DL", 0), ["DL7"]), ("IDB", blk("DL", 1), ["DL8"])]), ["X"])
     ts(T.YI1[:, 0:48], X, 1024.0, 16.0, A.add, A.min, ["X"], ["YI1"])
     for h in range(16):
-        out, src = T.VN[:, 48 * h:48 * h + 48], T.VF[:, h:768:16]
-        if h % 2:
-            act(out, src, F.Copy, ["VF0", "VF1"], ["VN%d" % h])
-        else:
-            cp(out, src, ["VF0", "VF1"], ["VN%d" % h])
-    total = 16 * 11
-    dma("y", T.yi[:, 0:768], T.YI0[:, 0:48], "dO", total, ["YI0"], ["o1"])
+        cp(T.VN[:, 48 * h:48 * h + 48], T.VF[:, h:768:16], ["VF0", "VF1"], ["VN%d" % h], "vs"[h % 2], 0.5)
+    for emit in arrange(jobs, at):
+        emit()
+
+    def home(d, l, q, sem, count):
+        a = ((rank - d) % n * 2 + l) * 768
+        arrived("LI", sem, count)
+        dma(q, T.yl[:, a:a + 768], T.RET[2 * d - 2 + l], "dO", total, ["LI"], ["o3%d%d" % (d, l)])
+
     for l in range(2):
         a = (rank * 2 + l) * 768
         dma("y", T.yl[:, a:a + 768], blk("LF", l), "dO", total, ["LF0"], ["o2%d" % l])
-
-    def home(d):
-        s = (rank - d) % n
-        nm = "aF%d" % d
-        lastw["LI%d" % d] = (nm, 8, {nm: 8})
-        for l in range(2):
-            a = (s * 2 + l) * 768
-            dma("ys"[l] if d == 3 else "y", T.yl[:, a:a + 768], T.RET[2 * d - 2 + l], "dO", total, ["LI%d" % d], ["o3%d%d" % (d, l)])
-
-    home(1)
+    dma("y", T.yi[:, 0:768], T.YI0[:, 0:48], "dO", total, ["YI0"], ["o1"])
     dma("y", T.yi[:, 768:1536], T.YI1[:, 0:48], "dO", total, ["YI1"], ["o4"])
+    for l in range(2):
+        home(1, l, "y", "aF1", 8)
     dma("s", T.yv[:], T.VN[:], "dO", total, ks("VN", range(16)), ["o5"])
-    home(2)
-    home(3)
+    for l in range(2):
+        home(2, l, "y", "aF2", 8)
+    home(3, 0, "y", "aF30", 8)
+    home(3, 1, "s", "aF31", 8)
     g.sync.wait_ge(T.sem.dO, total)
-    for s, v in (("lo", lo[0]), ("qv", cnt["v"]), ("qs", cnt["s"]), ("qp", cnt["p"]), ("qg", cnt["g"])):
+    for s, v in (("lo", lo[0]), ("lc", 16), ("qv", cnt["v"]), ("qs", cnt["s"]), ("qp", cnt["p"]), ("qg", cnt["g"])):
         g.wait_ge(T.sem[s], v)

from concourse.bass import DstId, RemoteDMATransfer
from concourse.mybir import AluOpType as A, ActivationFunctionType as F

SCRATCH = {"LTD": ("dram", [6, 128, 48], "bfloat16"), "RET": ("dram", [6, 128, 48], "bfloat16"), "LTR": ("dram", [2, 128, 96], "bfloat16"),
           "LTP": ("dram", [2, 128, 96], "bfloat16"), "LW": ("sbuf", [128, 6, 768], "bfloat16")}
for _ty, _s in (
        ("bfloat16", "C0 2064 C1 2064 C2 2064 C3 2064 OHN 768 CG0 768 CG1 768 VS 768 OUT 6912 SG0 768 SG1 768 VF 768 VN 768 OH 6912 "
         "LTA 384 LF 384 Y0W 64 Y0R 768 YI0 64 YI1 64 ET 32 IDB 128 SBB 144 GE 128 IR 512 ONE 128 PAT 512 PB 8 "
         "F0 432 F1 432 FC0 432 FC1 432 ZZ0 432 ZZ1 432 H0 480 H1 480 DL 96 NE 48 CN 48 T16 48 Y1W 48 "
         "NIB 128 P1K 128 N1K 128 P2K 128 N2K 128 M384 128 P256 128 M48 128 I32 128 N2 128 N3 128 P2 128 P3 128"),
        ("int32", "JW 10240 STI 96 KM 1040 KB 128 KY 128 PI 8 PJ 8"),
        ("float16", "JH 8192 MJ0 768 MJ1 768 JZ 1536 IDF 128 SBF 144 LB 144 LY 144 JC 48"),
        ("uint16", "STU 96 OFJ 48 OC0 48 OC1 48 LU 384 Y0U 48 SEL 48 KO 8"),
        ("float32", "TC0 48 TC1 48 PC 8 PK 8 V8 8 V8A 8 V8B 8 XR 32 JR 48 IV 128"),
        ("psum", "X 512 AD 1024 KA 512 KBK 512 KEY 1024 MS 512")):
    _p = _s.split()
    for _n, _w in zip(_p[::2], _p[1::2]):
        SCRATCH[_n] = ("psum", [128, int(_w)], "float32") if _ty == "psum" else ("sbuf", [128, int(_w)], _ty)

SEMAPHORES = "qv qs qp qg dJa dJb dC dSt dY dW dLo dLr dO dB dB0 lc dL3 dLq aW2 aW3 lo rF1 rF3 aF1 aF2 aF30 aF31".split()
SEMAPHORES += ["%s%d" % (a, d) for a in ("aC", "aL") for d in (1, 2, 3)] + ["aJ%d%d" % (d, i) for d in (1, 2, 3) for i in range(4)]
SEMAPHORES += ["h%d" % k for k in range(1, 9)]

WORLD = 256
SCALED = {"NIB": -1, "N2K": -2048, "P1K": 1024, "N1K": -1024, "M384": -384, "I32": 32768,
          "P2K": 2048, "P256": 256, "M48": -48}
TO_SAME = ("IDB", "NIB", "N2", "N3")
FROM_SAME = ("NIB", "IDB", "P2", "P3")
_RA = [[("H", 1, "o")], [("H", 2, "o", 1)], [("C", 1, "a"), ("H", 3, "b", 2)], [("C", 2, "a"), ("C", 3, "b", 3)]]
_RB = [[("H", 1, "o")], [("H", 2, "o")], [("C", 1, "a"), ("H", 3, "b", 2)], [("C", 2, "a"), ("C", 3, "b", 3)]]
_R4 = [[("H", 1, "o")], [("H", 2, "a"), ("H", 3, "b", 1)], [("C", 1, "o")], [("C", 2, "a"), ("C", 3, "b", 3)]]
CFG = {"give": ["H0", "H1", "C"], "relay": [_R4, _R4], "wide": (1, 2, 3), "bc": 5, "f": 1.25, "g": 1.56, "wake": 0.1, "bias": 2.0,
       "margin": 0.3, "late": [], "halves": 0, "lc": 0, "dlast": range(9), "tail": 3, "cut": (0, 512, 1024, 1536, 2048), "hl": (), "own": 0, "early": 0, "le": 1, "lsplit": 0, "qat": 0.5, "loads": "3LQYSabO",
       "eng": dict({m: "s" for m in "N2K NIB P1K N1K Y0U ID1 ID2".split()}, JZ0="g"),
       "want": {-2: "IV|PI|V8|XR|ID0|Cz0 Cz1 Cz2 Cz3|IDB|PC|N2K NIB P1K N1K|SBB|ET GE SBF IDF|ID2 ID1|"
                    "H0_0 T16 ONE CN PB M384 I32 PK LB LY H1_0|LU0|F0_1|FC0_1|OH1_0|OHN0 OHN1|STU|M0_0",
                -1: "OH1_1|OH2_0 OH2_1|JR IR JZ0|J1_0|J2_0 J2_1 J2_2 J2_3|J3_0 J3_1 J3_2 J3_3|PAT KM0 KM1 KMz",
                (0, "x"): "ID3", (1, "x"): "JZ1_0", (2, "j"): "LU1|OH3_0 OH3_1|J1_1", (2, "x"): "JZ1_1|ZZ0_3|F0_3 F0_5 F0_7",
                2: "ZZ0_5 ZZ0_7|FC0_3|KEY0 KEY1|J1_2 J1_3|OH4_0 OH4_1",
                (3, "c"): "OH5_0 OH5_1 OH5_2", 3: "OH5_3 OH5_4 OH5_5 OH5_6 OH5_7", (4, "c"): "OH5_8 OH5_9 OH5_10",
                4: "OH5_11 OH5_12 OH5_13 OH5_14 OH5_15", 5: "JC Y0U", (8, "a"): "OH0_0", (8, "b"): "OH0_1",
                (8, "v"): "KO"},
       "want1": {(-1, "x"): "F1_1", 0: "FC1_1|ZZ1_3 ZZ1_5 ZZ1_7", (0, "x"): "KY|P2K|LY", (1, "j"): "P256 M48"},
       "vsign": [], "ohq": {}, "siq": "vv", "gap2": 0,
       "end": ["C70 C71 n5 w0 J8 X8 c60 a70 s60 c61 a71 s61 j5 O8 C80 n6 c70 c71 v70 v71 j6 a80 g8",
               "C70 C71 n5 l1 J8 X8 c60 a70 s60 c61 a71 s61 j5 O8 C80 n6 b1 c70 c71 v70 s71 j6 a80 g8"],
       "wq": {1: "gsvv", 2: "gggg", 3: "gggg"}, "nq": "vsss",
       "at": {"LTS": 2.2, "LTA0": 2.9, "Y0R": 3.0, "STI": 3.3, "J0_0": 4.4, "J0_1": 5.4, "Y0W": 5.6, "C0_0": 7.4, "C0_1": 7.4,
              "LTA1": 10.7, "LTA2": 12.0, "LTA3": 12.0, "T1": 13.0, "C1": 17.0, "T2": 16.0, "C2": 19.5, "T3": 19.0, "C3": 22.5}}


def helpers(topo, cores, r):
    c, n = cores[r], len(cores)
    own = [e for e in topo.cores_of(c) if e != c and topo.may_write(e, cores[(r - 1) % n])]
    same = [e for e in own if topo.die(e) == topo.die(c)]
    oth = [e for e in own if topo.die(e) != topo.die(c)]
    relays = [same[0], oth[0], same[1], oth[1]]
    far = [e for e in range(WORLD) if topo.mates(e, c) and topo.may_write(e, c)]
    return relays, [[y for y in far if topo.die(y) == topo.die(e)][i // 2] for i, e in enumerate(relays)]


def piece(T, w, d, i, half=None):
    nm, a = {"J": ("JW", 2048 + 2048 * d if d else 0), "H": ("JH", 2048 * d), "C": ("C%d" % d, 16)}[w]
    if w != "C":
        return T[nm][:, a + CFG["cut"][i]:a + CFG["cut"][i + 1]]
    a += 512 * i + 256 * (half or 0)
    return T[nm][:, a:a + (512 if half is None else 256)]


def plan(topo, T):
    cores, n = T.cores, len(T.cores)
    calls, total, marks = {}, {}, {}

    def item(dst, eng, i, o, sem=None):
        if sem is None:
            marks[dst] = marks.get(dst, 0) + 1
            sem = "h%d" % marks[dst]
        total[dst, sem] = total.get((dst, sem), 0) + len(eng) * (len(o) if isinstance(o, list) else 1)
        return (dst, eng, i, o, sem)

    def call(core, turn, waits, items):
        calls.setdefault(core, []).append((turn, waits, items))

    H = [helpers(topo, cores, r) for r in range(n)]
    for r in range(n):
        c, relays = cores[r], H[r][0]
        x = [cores[(r - d) % n] for d in range(n)]
        gates = [H[(r - d) % n][1] for d in range(n)]
        on, off = topo.engines(c, relays[0]), topo.engines(c, x[2])
        E = {"a": off[0:4], "b": off[4:8], "o": off}

        def send(i, w, d, eng, turn=None, half=None):
            sem = "aC%d" % d if w == "C" else "aJ%d%d" % (d, i)
            src, dst = piece(T, w, 0, i, half), piece(T, w, d, i, half)
            if turn is None:
                return item(x[d], E[eng], src, dst, sem)
            it = item(gates[d][i], E[eng], src, dst)
            call(gates[d][i], turn, [it[4]], [item(x[d], off, dst, dst, sem)])
            return it

        carriers = relays + gates[3][0:2]
        order = [e for e in on if e not in off] + off
        m = CFG["le"]
        its = [item(e, order[m * i:m * i + m] if i < 4 else off[m * (i - 4):m * (i - 3)], T.LTD[i], T.LTD[0]) for i, e in enumerate(carriers)]
        if CFG["lsplit"]:
            call(c, 0, ["LTS"], its[0:4])
            call(c, CFG["lsplit"], ["LT3"], its[4:6])
        else:
            call(c, 0, ["LTS", "LT3"], its)
        for i, e in enumerate(carriers):
            call(e, 0, [its[i][4]], [item(x[i // 2 + 1], off, T.LTD[0], T.LTA[:, 96 + 48 * i:144 + 48 * i], "aL%d" % (i // 2 + 1))])
        if CFG["bc"] < 9:
            it = item(gates[3][0], E["b"], T.LTP[1], T.LTP[1])
            call(c, CFG["qat"], ["LTQ"], [item(x[2], E["a"], T.LTP[0], T.LTR[0], "aW2"), it])
            call(gates[3][0], 0.5, [it[4]], [item(x[3], off, T.LTP[1], T.LTR[1], "aW3")])
        got = {}
        if CFG["halves"]:
            def two(w, d, h):
                nm, a = {"H": ("JH", 2048 * d), "C": ("C%d" % d, 16)}[w]
                return T[nm][:, a + 1024 * h:a + 1024 * h + 1024]
            its = [item(relays[h], on, two("H", 0, h), two("H", 0, h)) for h in range(2)]
            its += [item(relays[2 + h], on[8 * h:8 * h + 8], two("C", 0, h), two("C", 0, h)) for h in range(2)]
            call(c, 1, ["N0_0"], its[0:1])
            call(c, 2, ["N0_1"], its[1:2])
            call(c, 3, ["C0_0"], its[2:4])
            for i, e in enumerate(relays):
                w, h = "HC"[i // 2], i % 2
                for turn, step in enumerate(CFG["halves"][i // 2]):
                    out = []
                    for d, eng, gate, at in step:
                        sem = "aC%d" % d if w == "C" else "aJ%d%d" % (d, h)
                        if gate is None:
                            out.append(item(x[d], E[eng], two(w, 0, h), two(w, d, h), sem))
                        else:
                            y = gates[d][2 * gate + h]
                            out.append(item(y, E[eng], two(w, 0, h), two(w, d, h)))
                            call(y, at, [out[-1][4]], [item(x[d], off, two(w, d, h), two(w, d, h), sem)])
                    call(e, 1 + turn, [] if turn else [its[i][4]], out)
        for turn, w in enumerate([] if CFG["halves"] else CFG["give"]):
            ii = range(4) if len(w) == 1 else [2 * int(w[1]), 2 * int(w[1]) + 1]
            m = len(on) // len(ii)
            for k, i in enumerate(ii):
                got[w[0], i] = item(relays[i], on[m * k:m * k + m], piece(T, w[0], 0, i), piece(T, w[0], 0, i))
            call(c, 1 + turn, sorted(set("%s0_%d" % (w[0].replace("H", "N"), i // 2) for i in ii)), [got[w[0], i] for i in ii])
        for i, e in enumerate([] if CFG["halves"] else relays):
            seen = set()
            for turn, step in enumerate(CFG["relay"][i // 2]):
                call(e, 1 + turn, [got[w, i][4] for w in sorted(set(s[0] for s in step) - seen)], [send(i, *s) for s in step])
                seen |= set(s[0] for s in step)
        total[relays[2], "rF1"] = 16
        call(relays[2], 98, ["rF1"], [item(x[3], off[4 * l:4 * l + 4], T.RET[l], T.RET[l], "aF1") for l in range(2)])
        for l in range(2):
            total[relays[2 * l], "rF3"] = 8
            call(relays[2 * l], 99, ["rF3"], [item(x[1], off, T.RET[4 + l], T.RET[4 + l], "aF3%d" % l)])
    for c in calls:
        calls[c].sort(key=lambda x: x[0])
    return calls, total


def transfers(topo, T, core, items):
    tr = []
    for c, e, i, o, s in items:
        rid, pid = topo.addr(c, core)
        srcs, dsts = i if isinstance(i, list) else [i], o if isinstance(o, list) else [o]
        tr.append(RemoteDMATransfer(dst_ids=[DstId(rid=rid, pnc=pid) for _ in dsts], dma_engine_mask=sum(1 << b for b in e),
                                    remote_sem=T.sem[s], srcs=srcs, dsts=dsts, alu_op=2 if len(srcs) > 1 else 0))
    return tr


def hand_on(g, core, T, topo):
    if not any(core in h for r in range(len(T.cores)) for h in helpers(topo, T.cores, r)):
        return
    calls, total = plan(topo, T)
    lo = 0
    for _, waits, items in calls.get(core, []):
        for s in waits:
            g.wait_ge(T.sem[s], total[core, s])
        g.remote_dma_fused(transfers(topo, T, core, items), local_sem=T.sem.lo)
        lo += sum(len(it[1]) for it in items)
    if lo:
        g.wait_ge(T.sem.lo, lo)


def arrange(jobs, at):
    wake = CFG["wake"]
    last, seen, pred, succ = {}, {}, [], [[] for _ in jobs]
    for i, (ch, reads, writes, tail) in enumerate(jobs):
        p = set(last[r] for r in reads if r in last)
        for w in writes:
            p |= set(seen.get(w, [])) | ({last[w]} if w in last else set())
        p.discard(i)
        pred.append(p)
        for j in p:
            succ[j].append(i)
        for r in reads:
            seen.setdefault(r, []).append(i)
        for w in writes:
            last[w], seen[w] = i, []
    way = [0.0] * len(jobs)
    for i in range(len(jobs) - 1, -1, -1):
        way[i] = jobs[i][0][0][1] + max([jobs[i][3]] + [wake + way[j] for j in succ[i]])
    head = [max([at.get(r, 0.0) for r in j[1]] + [0.0]) for j in jobs]
    tail = [j[3] for j in jobs]

    def place(order, before, free):
        busy, start, end, took, front = {}, {}, {}, {}, {}
        for i in order:
            best = None
            for c, (q, dur, emit) in enumerate(jobs[i][0]):
                t = max([free[i]] + [end[j] + (0.0 if q == took[j][0] and q in "py" else 2.0 if "y" in (q, took[j][0]) else wake) for j in before[i]])
                if tail[i] >= 0:
                    t = max(t, front.get(q, 0.0))
                ready = t
                for a, b in busy.get(q, []):
                    if t + dur <= a and (tail[i] >= 0 or ready + dur + CFG["margin"] <= a):
                        break
                    t = max(t, b)
                worth = t + dur + (CFG["bias"] * dur if q == "v" else 0.0)
                if best is None or worth < best[0]:
                    best = (worth, t, c)
            q, dur, emit = took[i] = jobs[i][0][best[2]]
            start[i], end[i] = best[1], best[1] + dur
            if tail[i] >= 0:
                front[q] = end[i]
            busy.setdefault(q, []).append((start[i], end[i]))
            busy[q].sort()
        return start, end, took

    every = range(len(jobs))
    order, taken = [], set()

    def take(i):
        if i not in taken:
            taken.add(i)
            for j in sorted(pred[i]):
                take(j)
            order.append(i)

    for i in every:
        if tail[i] >= 0:
            take(i)
    for i in every:
        take(i)
    out = []
    for i in order:
        q = [CFG["eng"][w] for w in jobs[i][2] if w in CFG["eng"]]
        out.append([c for c in jobs[i][0] if not q or len(jobs[i][0]) == 1 or c[0] == q[0]][0][2])
    return out


def rank_program(g, core, T, topo):
    rank = T.rank_of(core)
    if rank is None:
        hand_on(g, core, T, topo)
        return
    cores, n = T.cores, len(T.cores)
    relays = helpers(topo, cores, rank)[0]
    calls, arrive = plan(topo, T)
    Q = {"v": g.vector, "s": g.scalar, "p": g.tensor, "g": g, "y": g.sync}
    SEM = {"v": "qv", "s": "qs", "p": "qp", "g": "qg"}
    cnt = {q: 0 for q in SEM}
    clock = {q: {} for q in Q}
    lastw, readers, jobs, lo = {}, {}, [], [0]

    def need(q, toks):
        best = {}
        for t in toks:
            if t and clock[q].get(t[0], 0) < t[1] and (t[0] not in best or best[t[0]][1] < t[1]):
                best[t[0]] = t
        for t in sorted(best.values(), key=lambda t: -len(t[2])):
            if clock[q].get(t[0], 0) >= t[1]:
                continue
            Q[q].wait_ge(T.sem[t[0]], t[1])
            for s, v in t[2].items():
                if clock[q].get(s, 0) < v:
                    clock[q][s] = v

    def deps(q, reads, writes):
        out = [lastw.get(r) for r in reads]
        for w in writes:
            t = lastw.get(w)
            if t and not (q == "p" and t[0] == "qp"):
                out.append(t)
            out += readers.get(w, [])
        return out

    def done(q, sem, count, reads, writes):
        c = dict(clock[q])
        c[sem] = count
        for r in reads:
            readers.setdefault(r, []).append((sem, count, c))
        for w in writes:
            lastw[w] = (sem, count, c)
            readers[w] = []

    def issue(q, call, reads, writes):
        need(q, deps(q, reads, writes))
        cnt[q] += 1
        call().then_inc(T.sem[SEM[q]], 1)
        done(q, SEM[q], cnt[q], reads, writes)

    def dma(q, out, in_, sem, total, reads, writes):
        need(q, [t for t in deps(q, reads, writes) if t and t[0] != sem])
        Q[q].dma_start(out, in_).then_inc(T.sem[sem], 16)
        done(q, sem, total, reads, writes)

    CY = 0.00083 * CFG["f"]

    def lasts(q, out, m):
        k = 1
        for x in out.shape[1:]:
            k *= x
        if q == "g":
            return 0.17 * CFG["f"] + 2 * k * CY
        if m == "g":
            return (60 if q == "v" else 78) * CY + k * CFG["g"] * CY
        return 30 * CY + max(64, k * (m if q == "v" else 1)) * CY

    def put(choices, reads, writes, tail=0.0):
        jobs.append(([(q, lasts(q, o, m), lambda q=q, c=c: issue(q, c, reads, writes)) for q, o, m, c in choices], reads, writes, lazy[0]))

    lazy = [-1.0]

    def want(keys):
        for part in keys.split("|"):
            jobs.append(([("w", 0.0, lambda: None)], part.split(), [], 0.0))

    def TS(out, in0, a, b, o0, o1=None, m=1):
        if o1 is None:
            return ("v", out, m, lambda: g.vector.tensor_scalar(out, in0, a, None, o0))
        return ("v", out, m, lambda: g.vector.tensor_scalar(out, in0, a, b, o0, o1))

    def ACT(out, in_, func, bias=0.0, scale=1.0, m=1):
        return ("s", out, m, lambda: g.scalar.activation(out, in_, func, bias=bias, scale=scale))

    def IOTA(out, pattern, base, ch=0):
        return ("g", out, 2, lambda: g.iota(out, pattern, base, ch, allow_small_or_imprecise_dtypes=True))

    def ts(out, in0, a, b, o0, o1, reads, writes, m=1):
        put([TS(out, in0, a, b, o0, o1, m)], reads, writes)

    def tt(out, a, b, o, reads, writes, m=1):
        put([("v", out, m, lambda: g.vector.tensor_tensor(out, a, b, o))], reads, writes)

    def fill(ap, val, writes):
        put([("v", ap, 0.5, lambda: g.vector.memset(ap, val))], [], writes)

    def act(out, in_, func, reads, writes, bias=0.0, scale=1.0, m=1):
        put([ACT(out, in_, func, bias, scale, m)], reads, writes)

    def cp(out, a, reads, writes, qs="v", m=1):
        ch = {"v": ("v", out, m, lambda: g.vector.tensor_copy(out, a)), "s": ACT(out, a, F.Copy, m=m),
              "g": ("g", out, 2, lambda: g.affine_select(out, a, [[0, out.shape[1]]], A.is_ge, 0.0, 0, 0))}
        put([ch[q] for q in qs], reads, writes)

    def iota(out, pattern, base, ch, writes):
        put([IOTA(out, pattern, base, ch)], [], writes)

    def pe(items, writes, start=True, stop=True, maybe=None):
        reads = [r for it in items for r in it[3]] + (["T16"] if maybe else [])

        def emit():
            its = items[0:1] + (maybe() if maybe else []) + items[1:]
            for i, (o, l, r, rd) in enumerate(its):
                need("p", deps("p", rd, writes if i == 0 else []))
                ins = g.tensor.matmul(o, l, r, start and i == 0, stop and i == len(its) - 1)
            cnt["p"] += 1
            ins.then_inc(T.sem.qp, 1)
            done("p", "qp", cnt["p"], reads, writes)
        jobs.append(([("p", sum(max(min(64, l.shape[1]), r.shape[1]) for _, l, r, _ in items) * CY / 2, emit)], reads, writes, lazy[0]))

    def lin(o, terms):
        return [(o, T[m][:], x, [m] + rd) for m, x, rd in terms]

    def fused(items, reads, tail, dur=0.4):
        def emit():
            need("g", deps("g", reads, []))
            if "C0_0" in reads:
                g.remote_dma_fused(transfers(topo, T, core, items), local_sem=T.sem.lc)
                return
            g.remote_dma_fused(transfers(topo, T, core, items), local_sem=T.sem.lo)
            lo[0] += sum(len(it[1]) for it in items)
        jobs.append(([("g", dur, emit)], reads, [], tail))

    def later(out, in_, sem, total, reads, writes, tail=0.0):
        jobs.append(([("y", 0.06, lambda: dma("y", out, in_, sem, total, reads, writes))], reads, writes + [sem], tail))

    def blk(name, k, m=1):
        return T[name][:, 48 * k:48 * (k + m)]

    def ks(name, r):
        return ["%s%d" % (name, k) for k in r]

    def arrived(key, sem, count=None):
        k = count or arrive[core, sem]
        lastw[key] = (sem, k, {sem: k})

    J0, C0 = ["J0_0", "J0_1"], ["C0_0", "C0_1"]
    at = dict(CFG["at"])
    for d in range(1, n):
        s = (rank - d) % n
        for l in range(2):
            a = (s * 2 + l) * 768
            if d < 3:
                dma("sy"[l], T.LTD[2 * d - 2 + l], T.lt[:, a:a + 768], "dLr", 64, [], ["LTS"])
    for w in CFG["loads"]:
        if w == "3":
            for l in range(2):
                a = ((rank - 3) % n * 2 + l) * 768
                dma("sy"[l], T.LTD[4 + l], T.lt[:, a:a + 768], "dL3", 32, [], ["LT3"])
        if w == "O":
            for p in range(16 if CFG["own"] else 0):
                dma("sy"[p % 2], T.LW[p:128:16, 4:6], T.lt[:, rank * 1536:rank * 1536 + 1536], "dB0", 256, [], ["LW2_%d" % p])
        if w == "Q" and CFG["bc"] < 9:
            for j in range(2):
                a = (rank - 2 - j) % n * 1536
                dma("sy"[j], T.LTP[j], T.lt[:, a:a + 1536], "dLq", 32, [], ["LTQ"])
        if w == "L":
            for l in range(2):
                a = (rank * 2 + l) * 768
                dma("sy"[l], blk("LTA", l), T.lt[:, a:a + 768], "dLo", 32, [], ["LTA0"])
        if w == "Y":
            dma("s", T.Y0R[0:8, :], T.y0[:], "dY", 16, [], ["Y0R"])
        if w == "S":
            dma("y", T.STI[:], T.st[:], "dSt", 16, [], ["STI"])
        if w == "a":
            dma("s", T.JW[:, 0:CFG["cut"][2]], T.jm[:, 0:CFG["cut"][2]], "dJa", 16, [], ["J0_0"])
        if w == "b":
            dma("y", T.JW[:, CFG["cut"][2]:2048], T.jm[:, CFG["cut"][2]:2048], "dJb", 16, [], ["J0_1"])
    dma("y", T.Y0W[:, 0:48], T.y0[:], "dW", 16, [], ["Y0W"])
    dma("y", T.C0[:, 16:2064], T.cf[:], "dC", 16, ["J0_0"], C0)
    for d in range(1, n):
        arrived("C%d" % d, "aC%d" % d)
        arrived("LTA%d" % d, "aL%d" % d)
        for i in range(4):
            key = ("N%d_%d" if d in CFG["wide"] and CFG["wq"][d][i] != "-" else "J%d_%d") % (d, i)
            arrived(key, "aJ%d%d" % (d, i // 2 if CFG["halves"] else i))
            at[key] = at["T%d" % d] + 0.3 * i
    for j in range(2 if CFG["bc"] < 9 else 0):
        arrived("LTR%d" % j, "aW%d" % (j + 2))
        if j == 0 and CFG["lc"]:
            g.sync.wait_ge(T.sem.lc, 16)
        for p in range(16):
            dma("y", T.LW[p:128:16, 2 * j:2 * j + 2], T.LTR[j], "dB", 512, ["LTR%d" % j], ["LW%d_%d" % (j, p)])

    iota(T.PI[:, 0:1], [[0, 1]], 0, 1, ["PI"])
    iota(T.V8[:], [[-16, 8]], 0, 1, ["V8"])
    iota(T.IV[:], [[-1, 128]], 0, 1, ["IV"])
    iota(T.XR[:], [[0, 2], [1, 16]], 0, 0, ["XR"])
    iota(T.JW[:, 2048:2560], [[1, 512]], 0, 0, ["ID0"])
    for k in range(1, 4):
        o, i = T.JW[:, 2048 + 512 * k:2560 + 512 * k], T.JW[:, 2048:2560]
        put([TS(o, i, 512.0 * k, None, A.add), ACT(o, i, F.Identity, bias=512.0 * k), IOTA(o, [[1, 512]], 512 * k)], ["ID0"], ["ID%d" % k])
    iota(T.JR[:], [[16, 48]], 0, 0, ["JR"])
    iota(T.IR[0:1, :], [[0, 32], [-2048, 16]], 30720, 0, ["IR"])
    iota(T.PAT[:], [[0, 512]], 0, 0, ["PAT"])
    iota(T.PAT[:, 0:512:16], [[0, 32]], -16777215, 0, ["PAT"])
    for b in range(2):
        iota(T.KM[:, 512 * b:512 * b + 512], [[0, 512]], 0, 0, ["KM%d" % b])
    iota(T.KM[:, 1024:1040], [[0, 16]], 30720, 0, ["KMz"])
    fill(T.SBB[:], 0.0, ["SBB"])
    for d in range(4):
        fill(T["C%d" % d][:, 0:16], 0.0, ["Cz%d" % d])
    ts(T.PJ[:, 0:1], T.PI[:, 0:1], 15, None, A.bitwise_and, None, ["PI"], ["PJ"])
    ts(T.V8A[:], T.V8[:], -0.5, None, A.is_gt, None, ["V8"], ["V8A"])
    ts(T.V8B[:], T.V8[:], 15.5, None, A.is_lt, None, ["V8"], ["V8B"])
    cp(T.PC[:, 0:1], T.PJ[:, 0:1], ["PJ"], ["PC"])
    tt(T.SBB[:, 15:143:16], T.V8A[:], T.V8B[:], A.mult, ["V8A", "V8B"], ["SBB"])
    ts(T.IDB[:], T.IV[:], 0.0, None, A.is_equal, None, ["IV"], ["IDB"])
    ts(T.ET[:], T.XR[:], T.PC[:, 0:1], None, A.is_equal, None, ["XR", "PC"], ["ET"])
    pe([(T.X[0:8, 0:128], T.SBB[:, 15:143:16], T.IDB[:], ["SBB", "IDB"])], ["X"])
    cp(T.GE[0:8, :], T.X[0:8, 0:128], ["X"], ["GE"], "sv")
    cp(T.SBF[:], T.SBB[:], ["SBB"], ["SBF"], "vs", 0.5)
    cp(T.IDF[:], T.IDB[:], ["IDB"], ["IDF"], "vs", 0.5)
    for m, w in SCALED.items():
        put([TS(T[m][:], T.IDB[:], float(w), None, A.mult, m=0.5), ACT(T[m][:], T.IDB[:], F.Copy, scale=float(w))], ["IDB"], [m])
    for t in range(2):
        fill(T["H%d" % t][:, 0:96], -1.0, ks("H%d_" % t, (-1, 0)))
    fill(T.T16[:], -16.0, ["T16"])
    fill(T.ONE[:], 1.0, ["ONE"])
    cp(T.PB[:, 0:1], T.PJ[:, 0:1], ["PJ"], ["PB"])
    ts(T.PK[:, 0:1], T.PC[:, 0:1], 128.0, 15.0, A.mult, A.add, ["PC"], ["PK"])
    for m in ("LB", "LY"):
        ts(T[m][:, 0:16], T.IDB[:, 0:16], 0.0, None, A.mult, None, ["IDB"], [m])
    ts(T.JC[:], T.JR[:], T.PC[:, 0:1], None, A.add, None, ["JR", "PC"], ["JC"])
    fill(T.CN[:], -6.0, ["CN"])
    ts(T.KO[:], T.JR[:, 0:8], T.PK[:, 0:1], 1024.0, A.add, A.min, ["JR", "PK"], ["KO"])
    cp(T.Y0U[:], T.Y0W[:, 0:48], ["Y0W"], ["Y0U"], "vs")
    cp(T.STU[:], T.STI[:], ["STI"], ["STU"], "vs")

    on = topo.engines(core, relays[0])
    off = topo.engines(core, cores[(rank + 2) % n])
    up = [e for e in on if e not in off]
    if CFG["wide"]:
        for i in range(4):
            cp(piece(T, "H", 0, i), piece(T, "J", 0, i), ["J0_%d" % (i // 2)], ["M0_%d" % i], CFG["nq"][i])
    for d in CFG["wide"]:
        for i in range(4):
            if CFG["wq"][d][i] != "-":
                cp(piece(T, "J", d, i), piece(T, "H", d, i), ["N%d_%d" % (d, i)], ["J%d_%d" % (d, i)], CFG["wq"][d][i])

    def sels(o, buf, rd, sb="SBF", contiguous=False):
        src = T[buf]
        return [(o, T[sb][:, 15 - h:143 - h], src[:, 48 * h:48 * h + 48] if contiguous else src[:, h:768:16], rd + [sb]) for h in range(16)]

    def tab(k):
        return (k - 1) // 2 if k > 0 else 0

    def onehot(k):
        off, a = (T.Y0U, 0) if k == 0 else (T.LU, 48 * (k - 1))
        for hf in range(2):
            cp(T.OH[:, 768 * k + 384 * hf:768 * k + 384 * hf + 384], T.ET[:].indirect(off[:, a + 24 * hf:a + 24 * hf + 24]),
               ["ET", "Y0U" if k == 0 else "LU%d" % tab(k)], ["OH%d_%d" % (k, hf)], CFG["ohq"].get((k, hf), "s"), "g")

    def onehots(a, b, at=0):
        for h in range(16):
            ts(T.OH[:, 768 * a + h:768 * b:16], T.LW[:, at:at + b - a, 48 * h:48 * h + 48], 15.0, T.PB[:, 0:1], A.min, A.is_equal,
               ["PB", "LW2_15" if a < 5 else "LW1_15"], ["OH%d_%d" % (k, h) for k in range(a, b)], 0.5)

    for d in range(4):
        src = T.LTA[:, 96 * d:96 * d + 96]
        ts(blk("F0", 2 * d + 1, 2), src, 15.5, 2048.0, A.is_gt, A.mult, ["LTA%d" % d], ks("F0_", (2 * d + 1, 2 * d + 2)), 0.5)
        if 2 * d + 1 < CFG["bc"] and (d or not CFG["own"]):
            cp(T.LU[:, 96 * d:96 * d + 96], src, ["LTA%d" % d], ["LU%d" % d], "vs", 0.5)
    for k in range(3 if CFG["own"] else 1, CFG["bc"]):
        onehot(k)
    if CFG["own"]:
        onehots(1, 3, 4)
    if CFG["bc"] < 9:
        onehots(CFG["bc"], 9, CFG["bc"] - 5)
    onehot(0)
    for hf in range(2):
        pe([(T.AD[:, 512 * hf:512 * hf + 384], T.GE[0:8, :], T.Y0R[0:8, 384 * hf:384 * hf + 384], ["GE", "Y0R"])], ["AD%d" % hf])
        ts(T.OHN[:, 384 * hf:384 * hf + 384], T.AD[:, 512 * hf:512 * hf + 384], T.PC[:, 0:1], None, A.is_equal, None,
           ["AD%d" % hf, "PC"], ["OHN%d" % hf])
    for a, b in ((1, 3), (3, 8)):
        ts(blk("FC0", a, b - a), blk("F0", a, b - a), -16.0, None, A.add, None, ks("F0_", range(a, b)), ks("FC0_", range(a, b)), 0.5)
    for d in range(1, 4):
        ts(blk("ZZ0", 2 * d + 1, 2), T.LTA[:, 96 * d:96 * d + 96], 15.5, 2048.0 * d, A.is_lt, A.mult, ["LTA%d" % d],
           ks("ZZ0_", (2 * d + 1, 2 * d + 2)), 0.5)
    put([TS(T.JZ[:, 0:1536:2], T.OHN[:], 0.0, None, A.mult, m=0.5),
         ("g", T.OHN[:], 2, lambda: g.affine_select(T.JZ[:, 0:1536:2], T.OHN[:], [[0, 768]], A.is_gt, 0.0, 0, 0))], ["OHN0", "OHN1"], ["JZ0"])
    for hf in range(2):
        cp(T.JZ[:, 1 + 768 * hf:768 + 768 * hf:2], T.JW[:, 0:2048].indirect(T.STU[:, 48 + 24 * hf:72 + 24 * hf]), ["STU"] + J0,
           ["JZ1_%d" % hf], CFG["siq"][hf], "g")
    for b in range(2):
        items = [(T.KEY[0:96, 512 * b:512 * b + 512], T.ONE[0:1, 0:96], T.IR[0:1, :], ["ONE", "IR"])]
        for hp in range(4 * b, 4 * b + 4):
            for e in range(2):
                a = 96 * (hp + 8 * e) + 1 - e
                items.append((T.KEY[0:96, 128 * hp:128 * hp + 128], T.JZ[:, a:a + 96], T.IDF[:], ["JZ0", "JZ1_0", "JZ1_1", "IDF"]))
        pe(items, ["KEY%d" % b], stop=False)

    KP = ["KA", "KBK"]
    X, W = T.X[:, 0:48], T.MS[:, 0:48]
    total = 16 * 11

    def jwin(d):
        rd = ks("ID", range(4))
        if d == 0:
            return T.JW[:, 0:4096], rd + J0
        return T.JW[:, 2048:4096 + 2048 * d], rd + ["J%d_%d" % (e, i) for e in range(1, d + 1) for i in range(4)]

    def unfold(o, m):
        return [(o, T[m][0:96, 8 - 8 * e:136 - 8 * e], T.IDF[0:96, e:96:2], [m, "IDF"]) for e in range(2)]

    def walk(t, extra):
        first = 1 - t
        FN, ZN, HN = "F%d" % t, "ZZ%d" % t, "H%d" % t
        how = {}

        def fk(k):
            return "%s_%d" % (FN, k)

        def hk(k):
            return "%s_%d" % (HN, k)

        def vblk(k, h0, h1=None):
            a, b = 384 * h0, 384 * (h1 or h0 + 1)
            nm, o = ("VS", 0) if k < first else ("OUT", 768 * k)
            return T[nm][:, o + a:o + b], ["%s%d_%d" % (nm, k, hf) for hf in range(h0, h1 or h0 + 1)]

        def images(k):
            m = "MJ%d" % (k % 2)
            if k >= first:
                win, rd = jwin(tab(k))
                tt(T[m][:], win.indirect(T.OFJ[:]), T.OH[:, 768 * k:768 * k + 768], A.mult, rd + ["OFJ"] + ks("OH%d_" % k, range(16)), [m], "g")
            elif t == 0:
                tt(T[m][:], T.JW[:, 0:2048].indirect(blk("STU", 0)), T.OHN[:], A.mult, ["STU", "OHN0", "OHN1"] + J0, [m], "g")

        def pick(k):
            m = "MJ%d" % (k % 2)
            if k < first and t:
                pe(lin(X, [("N1K", blk("H0", 0), ["H0_-1"]), ("P1K", blk("H0", 9), ["H0_8"])]) + unfold(X, "LB"), ["X"])
                return
            pe((lin(X, [("NIB", blk(FN, 8), [fk(8)])]) if k == 8 else []) + sels(X, m, [m], contiguous=k < first), ["X"])

        def roots(k):
            a, o = "TC%d" % (k % 2), "OC%d" % (k % 2)
            if k == 8:
                ts(T[o][:], X, 16.0, 0.0, A.add, A.max, ["X"], [o])
                return
            if k < first and t:
                cp(T.OFJ[:], X, ["X"], ["OFJ"])
            else:
                nxt = ZN if k > 1 else FN
                tt(T.OFJ[:], X, blk(nxt, k + 1), A.add, ["X", "%s_%d" % (nxt, k + 1)], ["OFJ"])
            if k < first and not t:
                ts(T[o][:], X, 16.0, None, A.add, None, ["X"], [o])
            else:
                tt(T[o][:], X, blk("FC%d" % t, max(k, first)), A.subtract, ["X", "FC%d_%d" % (t, max(k, first))], [o])

        def coef(k, h0, h1):
            d, o = tab(k), "OC%d" % (k % 2)
            out, w = vblk(k, h0, h1) if k < first else (T["CG%d" % (k % 2)][:, 384 * h0:384 * h1], ["CG%d_%d" % (k % 2, hf) for hf in range(h0, h1)])
            act(out, T["C%d" % d][:].indirect(T[o][:, 24 * h0:24 * h1]), F.Copy, (["C%d" % d] if d else C0) + ["Cz%d" % d, o], w, m="g")

        def add(k, hf):
            v, vk = vblk(k - 1, hf)
            c = "CG%d" % (k % 2)
            pe(lin(T.AD[:, 512 * hf:512 * hf + 384], [("IDB", T[c][:, 384 * hf:384 * hf + 384], ["%s_%d" % (c, hf)]), ("IDB", v, vk)]),
               ["AD%d" % hf])

        def cut(k, hf):
            v, vk = vblk(k, hf)
            ts(v, T.AD[:, 512 * hf:512 * hf + 384], 255.0, -255.0, A.min, A.max, ["AD%d" % hf], vk)

        def sign(k, h0, h1, raw=False, only="sv"):
            v, vk = (T.AD[:, 0:384], ["AD0"]) if raw else vblk(k, h0, h1)
            s = "SG%d" % (k % 2)
            o, w = T[s][:, 384 * h0:384 * h1], ["%s_%d" % (s, hf) for hf in range(h0, h1)]

            def by(ch):
                def call():
                    for hf in range(h0, h1):
                        how[k, hf] = ch[0]
                    return ch[3]()
                return ch[0:3] + (call,)
            if raw:
                put([by(ACT(o, v, F.Sign, bias=0.5))], vk, w + vk)
            else:
                put([ch for ch in (by(ACT(o, v, F.Sign, bias=0.5)), by(TS(o, v, 0.0, 2.0, A.is_ge, A.mult, 0.5))) if ch[0] in only], vk, w)

        def count(k, dead=None):
            p, s = KP[k % 2], "SG%d" % (k % 2)
            o = T[p][:, 0:48]
            dead = lin(o, dead or [("N2K", blk(HN, k), [hk(k - 1)])])
            n1 = len(dead) if k not in CFG["dlast"] else len(dead) - 1
            pe(lin(o, [("IDB", blk(FN, k), [fk(k)])]) + dead[:n1] + sels(o, s, [s + "_0", s + "_1"], "SBB") + dead[n1:], [p],
               maybe=lambda: [lin(T[p][:, 24 * hf:24 * hf + 24], [("IDB", T.T16[:, 0:24], ["T16"])])[0] for hf in range(2)
                              if how[k, hf] == "v" != how[k, 1 - hf]])

        def both(k):
            return 16.0 if how[k, 0] == how[k, 1] == "v" else 0.0

        def judge(k):
            p, o = T[KP[k % 2]][:, 0:48], blk(HN, k + 1)
            put([("s", o, 1, lambda: g.scalar.activation(o, p, F.Sign, bias=2047.0 + both(k), scale=-1.0))], [KP[k % 2]], [hk(k)])

        def last(k):
            p, o = T[KP[k % 2]][:, 0:48], blk("DL", k - 7)
            put([("v", o, 1, lambda: g.vector.tensor_scalar(o, p, both(k) - 2049.0, 16.0, A.is_lt, A.mult))], [KP[k % 2]], ["DL%d" % k])

        def left(d):
            k, o = 2 * d + 1, T.KEY[:, 512 * (d % 2):512 * (d % 2) + 96]
            terms = [("IDB", T.LTA[:, 96 * d:96 * d + 96], ["LTA%d" % d]), ("IDB", blk(FN, k, 2), [fk(k), fk(k + 1)])]
            if d < 3:
                terms += [("N1K", blk(HN, k, 2), [hk(k - 1), hk(k)]), ("P1K", blk(HN, k + 1, 2), [hk(k), hk(k + 1)])]
            pe(lin(o, terms), ["KEY%d" % (d % 2)])

        def left2(d):
            ts(T.LF[:, 96 * d:96 * d + 96], T.KEY[:, 512 * (d % 2):512 * (d % 2) + 96], 16.0, None, A.min, None, ["KEY%d" % (d % 2)], ["LF%d" % d])

        def folded(l):
            return (relays[2 * l], up, [blk("LF", 6 + l), blk("DL", l)], T.RET[4 + l], "rF3")

        for k in range(first - 1, 8):
            images(k)
            for f in extra.get((k, "j"), []):
                f()
            hl = t in CFG["hl"]
            if hl and k - 1 >= first:
                add(k - 1, 0)
            pick(k)
            for f in extra.get((k, "x"), []):
                f()
            if hl:
                if k - 2 >= first:
                    cut(k - 2, 1)
                if k - 1 >= first:
                    add(k - 1, 1)
                    cut(k - 1, 0)
            for hf in range(0 if hl else 2):
                if k - 2 >= first and not ((t, k) == (0, 3) and CFG["early"]):
                    cut(k - 2, hf)
                if k - 1 >= first:
                    add(k - 1, hf)
            after = []
            if k - 2 >= first:
                for hf in range(2):
                    if t or (k - 2, hf) not in CFG["vsign"]:
                        sign(k - 2, hf, hf + 1, only="s")
                    elif hf < CFG["gap2"]:
                        sign(k - 2, hf, hf + 1, only="v")
                    else:
                        after.append(hf)
            if t and k == 1:
                left2(3)
            for f in extra.get((k, "c"), []):
                f()
            roots(k)
            for hf in after:
                sign(k - 2, hf, hf + 1, only="v")
            for f in extra.get((k, "o"), []):
                f()
            if k - 3 >= first:
                judge(k - 3)
            if k < 7 and hl and k >= first:
                coef(k, 0, 1)
                coef(k, 1, 2)
            elif k < 7:
                coef(k, 0, 2)
            if (t, k) == (0, 2) and CFG["early"]:
                cut(1, 0)
                cut(1, 1)
            if first <= k - 2 < 5:
                count(k - 2)
            if t and k == 0:
                left(3)
            for f in extra.get(k, []):
                f()
        raw, rk = vblk(8, 1)

        def back1():
            if t:
                left2(1)
                fused([(relays[2], on[8 * l:8 * l + 8], blk("LF", 2 + l), T.RET[l], "rF1") for l in range(2)], ["LF1"], 0.0)

        gone = [("IDF", T.JC[:], ["JC"])] + [("M384", blk(HN, k + 1), [hk(k)]) for k in range(first, 7)]
        do = {"w": lambda k: t or pe(lin(W, [("M384", T.CN[:], ["CN"])] + gone[:-2]), ["MS"], stop=False), "J": images, "X": pick, "O": roots, "j": judge, "n": count, "b": lambda k: back1(), "l": lambda k: t and left(k), "L": left2, "i": lambda k: extra["i"][k](),
              "g": lambda k: tt(raw, T.C3[:].indirect(T.OC0[:, 24:48]), vblk(7, 1)[0], A.add, ["C3", "Cz3", "OC0", "OUT7_1"], rk, "g")}
        for w in CFG["end"][t].split():
            k, hf = int(w[1]), int(w[2:3] or 0)
            if w[0] in do:
                do[w[0]](k)
            elif w[0] in "sv":
                sign(k, hf, hf + 1, only=w[0])
            elif w[0] == "C":
                coef(k, hf, hf + 1)
            else:
                {"a": add, "c": cut}[w[0]](k, hf)
        if t == 0:
            pe(lin(W, gone[-2:]), ["MS"], start=False)
            count(7)
            cut(8, 0)
            for f in extra.get((8, "a"), []):
                f()
            p = T[KP[1]][:, 0:48]
            put([("v", p, 1, lambda: g.vector.tensor_scalar(T.TC1[:], p, 2047.0 + both(7), 768.0, A.is_gt, A.mult))], [KP[1]], ["TC1", KP[1]])
            tt(T.SEL[:], W, T.TC1[:], A.add, ["MS", "TC1"], ["SEL"])
            judge(7)
        else:
            dead = [("P2K", blk(HN, 7), [hk(6)])]
            back2 = [(cores[(rank + 2) % n], off[4 * l:4 * l + 4], blk("LF", 4 + l), T.RET[2 + l], "aF2") for l in range(2)]
            if CFG["tail"] == 2:
                left(2)
            count(7, dead)
            if CFG["tail"] == 0:
                left(2)
            sign(8, 0, 1, True)
            if CFG["tail"] == 2:
                left2(2)
                fused(back2, ["LF2"], 0.0)
            sign(8, 1, 2, only="v")
            last(7)
            count(8, dead + [("P256", blk("DL", 0), ["DL7"])])
            if CFG["tail"] == 0:
                left2(2)
                fused(back2 + [folded(0)], ["LF2", "LF3", "DL7"], 0.0)
            if CFG["tail"] in (1, 3):
                left(2)
            if CFG["tail"] == 3:
                fused([folded(0)[0:1] + (off,) + folded(0)[2:]], ["LF3", "DL7"], 0.0)
            cut(8, 0)
            pe(lin(W, gone + [("M384", blk(HN, 7), [hk(6)]), ("M48", blk("DL", 0), ["DL7"])]), ["MS"])
            last(8)
            if CFG["tail"] in (1, 2):
                fused([folded(0)[0:1] + (off,) + folded(0)[2:], folded(1)], ["LF3", "DL7", "DL8"], 0.0)
            else:
                fused([folded(1)], ["LF3", "DL8"], 0.0)
            if CFG["tail"] in (1, 3):
                left2(2)
                fused(back2, ["LF2"], 0.0)
            ts(T.SEL[:], W, 384.0 * 8, None, A.add, None, ["MS"], ["SEL"])
        outs = ["OUT%d_%d" % (k, hf) for k in range(first, 9) for hf in range(2)]
        win = T.OUT[:, 768 * first:6912]
        act(T.VF[:, 0:384], win.indirect(T.SEL[:, 0:24]), F.Copy, ["SEL"] + outs, ["VF0"], m="g")
        ts(T.VF[:, 384:768], win.indirect(T.SEL[:, 24:48]), 255.0, -255.0, A.min, A.max, ["SEL"] + outs, ["VF1"], "g")
        if t:
            left(0)
            left2(0)
            inserted()
            inserted2()
        return sign, count, judge

    lazy[0] = 0.0
    soon = {k: [lambda keys=keys: want(keys)] for k, keys in CFG["want"].items()}
    for f in soon.pop(-2):
        f()
    for turn, keys, items in calls[core]:
        fused(items, [k for key in keys for k in (ks("M0_", (2 * int(key[3]), 2 * int(key[3]) + 1)) if key[0] == "N" else [key])],
              0.0, 0.4 if turn else 2.0)
        for f in soon.pop("L", []) if turn >= (0.5 if CFG["bc"] < 9 else 0) else []:
            f()
    for f in soon.pop(-1):
        f()
    sign, count, judge = walk(0, soon)

    sign(8, 0, 2, only="s")
    for f in soon.get((8, "v"), []):
        f()
    for b in range(2):
        pe([(T.KEY[0:96, 128 * hp:128 * hp + 128], T.VF[:, hp:768:8], T.I32[:], ["VF0", "VF1", "I32"]) for hp in range(4 * b, 4 * b + 4)],
           ["KEY%d" % b], start=False)
        o = T.KM[0:96, 512 * b:512 * b + 512]
        put([("v", o, 1, lambda b=b, o=o: g.vector.tensor_tensor_scan(o, T.PAT[0:96, :], T.KEY[0:96, 512 * b:512 * b + 512], 0.0, A.add, A.max))],
            ["PAT", "KEY%d" % b], ["KM%d" % b])
    count(8)
    for f in soon.get((8, "b"), []):
        f()
    judge(8)
    keys, kk = T.KM[:].indirect(T.KO[:]), ["KM0", "KM1", "KMz", "KO"]
    ts(T.KB[:], keys, 2047, None, A.bitwise_and, None, kk, ["KB"], "g")
    cp(T.LB[:, 8:136], T.KB[:], ["KB"], ["LB"], "vs")
    act(blk("F1", 0), blk("H0", 9), F.Identity, ["H0_8"], ["F1_0"], 1024.0, 1024.0)
    act(blk("FC1", 0), blk("H0", 9), F.Identity, ["H0_8"], ["FC1_0"], 1008.0, 1024.0)
    S8 = range(1, 9)
    lazy[0] = -1.0
    pe(lin(T.MS[:, 0:384], [("IDB", blk("F0", 1, 8), ks("F0_", S8)), ("N1K", blk("H0", 1, 8), ks("H0_", range(8))),
                            ("P1K", blk("H0", 2, 8), ks("H0_", S8))]), ["MS"])
    cp(blk("F1", 1, 8), T.MS[:, 0:384], ["MS"], ks("F1_", S8), "sv")
    lazy[0] = -1.0
    ts(T.KY[:], keys, 11, 15, A.arith_shift_right, A.bitwise_and, kk, ["KY"], "g")
    put([TS(T.LY[:, 8:136], T.KY[:], -1.0, 15.0, A.mult, A.add), ACT(T.LY[:, 8:136], T.KY[:], F.Identity, 15.0, -1.0)], ["KY"], ["LY"])
    act(blk("FC1", 1, 7), blk("F1", 1, 7), F.Identity, ks("F1_", range(1, 8)), ks("FC1_", range(1, 8)), -16.0)
    for d in range(1, 4):
        k2 = (2 * d + 1, 2 * d + 2)
        act(blk("ZZ1", 2 * d + 1, 2), blk("F1", 2 * d + 1, 2), F.Identity, ks("F1_", k2), ks("ZZ1_", k2), 2048.0 * d, -1.0 * d)

    def letter():
        pe(unfold(W, "LY"), ["MS"])
        cp(T.Y1W[:], W, ["MS"], ["Y1W"], "vs")

    def inserted():
        pe(lin(W, [("IDB", T.Y0W[:, 0:48], ["Y0W"]), ("IDB", blk("F1", 0), ["F1_0"]), ("P1K", blk("H1", 1), ["H1_0"])]), ["MS"])

    def inserted2():
        ts(T.YI0[:, 0:48], W, 1024.0, 16.0, A.add, A.min, ["MS"], ["YI0"])

    lazy[0] = 0.0
    soon = {k: [lambda keys=keys: want(keys)] for k, keys in CFG["want1"].items()}
    soon.update({(1, "x"): [letter], "i": [inserted, inserted2]})
    walk(1, soon)

    pe(lin(X, [("IDB", T.Y1W[:], ["Y1W"]), ("P1K", blk("H1", 7), ["H1_6"]), ("IDB", blk("DL", 0), ["DL7"]), ("IDB", blk("DL", 1), ["DL8"])]), ["X"])
    ts(T.YI1[:, 0:48], X, 1024.0, 16.0, A.add, A.min, ["X"], ["YI1"])
    for h in range(16):
        cp(T.VN[:, 48 * h:48 * h + 48], T.VF[:, h:768:16], ["VF0", "VF1"], ["VN%d" % h], "vs"[h % 2], 0.5)
    for emit in arrange(jobs, at):
        emit()

    def home(d, l, q, sem, count):
        a = ((rank - d) % n * 2 + l) * 768
        arrived("LI", sem, count)
        dma(q, T.yl[:, a:a + 768], T.RET[2 * d - 2 + l], "dO", total, ["LI"], ["o3%d%d" % (d, l)])

    for l in range(2):
        a = (rank * 2 + l) * 768
        dma("y", T.yl[:, a:a + 768], blk("LF", l), "dO", total, ["LF0"], ["o2%d" % l])
    dma("y", T.yi[:, 0:768], T.YI0[:, 0:48], "dO", total, ["YI0"], ["o1"])
    dma("y", T.yi[:, 768:1536], T.YI1[:, 0:48], "dO", total, ["YI1"], ["o4"])
    for l in range(2):
        home(1, l, "y", "aF1", 8)
    dma("s", T.yv[:], T.VN[:], "dO", total, ks("VN", range(16)), ["o5"])
    for l in range(2):
        home(2, l, "y", "aF2", 8)
    home(3, 0, "y", "aF30", 8)
    home(3, 1, "s", "aF31", 8)
    g.sync.wait_ge(T.sem.dO, total)
    for s, v in (("lo", lo[0]), ("lc", 16), ("qv", cnt["v"]), ("qs", cnt["s"]), ("qp", cnt["p"]), ("qg", cnt["g"])):
        g.wait_ge(T.sem[s], v)
